import numpy as np
import ml_dtypes


def mxq(x, axis, fmt="e4m3"):
    dtype, down = {"e4m3": (ml_dtypes.float8_e4m3fn, 7), "e5m2": (ml_dtypes.float8_e5m2, 14)}[fmt]
    v = np.moveaxis(np.asarray(x, np.float32).astype(ml_dtypes.bfloat16).astype(np.float64), axis, -1)
    blocks = v.reshape(v.shape[:-1] + (-1, 32))
    amax = np.abs(blocks).max(-1, keepdims=True)
    byte = np.maximum(np.where(amax > 0, np.frexp(amax)[1] - 1 + 127, 0) - down, 1)
    scale = np.exp2(byte - 127.0)
    codes = (blocks / scale).astype(np.float32).astype(dtype).astype(np.float64)
    return np.moveaxis((codes * scale).reshape(v.shape), -1, axis)


WIDE = False


def mx_kscale(k):
    if not WIDE:
        return np.ones(k)
    levels = np.array([10, -10, 5, -5, 0])
    if k % 512:
        return np.exp2(np.random.permutation(np.resize(levels, k // 32))).repeat(32)
    a = np.empty((k // 512, 16))
    for p in range(k // 512):
        a[p, :8] = np.random.permutation(np.resize(levels, 8))
        for g in range(8):
            far = levels[np.abs(levels - a[p, g]) >= 10]
            a[p, g + 8] = far[np.random.randint(len(far))]
    return np.exp2(a.ravel()).repeat(32)


def f64(x):
    return np.asarray(x).astype(np.float64)


def striped(idx):
    return np.tile(idx.reshape(-1, 16).T, (8, 1)).astype(np.uint16)


def unstriped(offs):
    return offs[:16].T.reshape(-1).astype(np.int64)


E2M1 = np.array([0.0, 0.5, 1.0, 1.5, 2.0, 3.0, 4.0, 6.0, -0.0, -0.5, -1.0, -1.5, -2.0, -3.0, -4.0, -6.0])


def pack_weight(w, fmt):
    k, n = w.shape
    w = f64(np.asarray(w, np.float32).astype(ml_dtypes.bfloat16)).reshape(k // 32, 32, n)
    amax = np.abs(w).max(1)
    if fmt == "e4m3":
        byte = np.frexp(amax)[1] - 1 + 127 - 7
    else:
        mant, ex = np.frexp(amax / 6.0)
        byte = np.where(mant > 0.5, ex, ex - 1) + 127
    byte = np.clip(np.where(amax > 0, byte, 1), 1, 254)
    scaled = (w * np.exp2(127.0 - byte)[:, None, :]).reshape(k, n).astype(np.float32)
    by_word = np.ascontiguousarray(scaled.reshape(k // 512, 128, 4, n).transpose(0, 1, 3, 2))
    if fmt == "e4m3":
        words = by_word.astype(ml_dtypes.float8_e4m3fn).view(np.uint8)
    else:
        c = by_word.astype(ml_dtypes.float4_e2m1fn).view(np.uint8) & 0xF
        words = (c[..., 0::2] | (c[..., 1::2] << 4)).reshape(k // 512, 128, 2 * n)
    return np.ascontiguousarray(words), np.ascontiguousarray(byte.astype(np.uint8).reshape(k // 512, 16, n))


def unpack_weight(words, scales, fmt):
    g, _, n = scales.shape
    words = np.ascontiguousarray(words).reshape(g, 128, n, -1)
    if fmt == "e4m3":
        vals = words.view(ml_dtypes.float8_e4m3fn).astype(np.float64)
    else:
        nib = np.empty((g, 128, n, 4), np.uint8)
        nib[..., 0::2] = words & 0xF
        nib[..., 1::2] = words >> 4
        vals = E2M1[nib]
    vals = vals * np.repeat(np.exp2(scales.astype(np.float64) - 127.0), 8, axis=1)[..., None]
    return vals.transpose(0, 1, 3, 2).reshape(g * 512, n)


def gelu(v):
    return 0.5 * v * (1.0 + np.tanh(np.sqrt(2.0 / np.pi) * (v + 0.044715 * v**3)))


def bf(x):
    return np.asarray(x, np.float32).astype(ml_dtypes.bfloat16)


def planes(Y):
    n, m = Y.shape
    b = f64(bf(Y)).reshape(n // 32, 32, m)
    amax = np.abs(b).max(1)
    byte = np.clip(np.where(amax > 0, np.frexp(amax)[1] - 1 + 127 - 7, 1), 1, 254)
    codes = (b * np.exp2(127.0 - byte)[:, None, :]).reshape(n, m).astype(np.float32).astype(ml_dtypes.float8_e4m3fn).view(np.uint8)
    words = codes.reshape(n // 512, 128, 4, m).transpose(0, 1, 3, 2)
    return np.ascontiguousarray(words), np.ascontiguousarray(byte.astype(np.uint8).reshape(n // 512, 16, m))


K, T, S, H, T2, P, N = 1024, 2048, 1024, 1024, 2048, 1024, 512

def setup_inputs():
    n = np.random.standard_normal
    s = mx_kscale(K)[:, None]
    u = mx_kscale(H)[:, None]
    col = np.exp(0.8 * n(N))
    tab_words, tab_scales = pack_weight(n((K, T)) * s, "e4m3")
    w2_words, w2_scales = pack_weight(n((H, N)) / np.sqrt(H) * col / u, "e2m1")
    return {
        "tab_words": tab_words, "tab_scales": tab_scales,
        "offs": striped(np.random.permutation(T)[:S]),
        "w1": (0.5 * n((K, H)) / np.sqrt(K) / s).astype(np.float32),
        "wgs": np.exp(0.3 * n((128, S))).astype(np.float32),
        "offs2": striped(np.random.permutation(T2)[:S]),
        "offs3": striped(np.random.permutation(T2)[:P]),
        "offs4": striped(np.random.permutation(T2)[:P]),
        "rest": n((H, P)).astype(np.float32),
        "gz": (np.exp(0.3 * n(H)) * u[:, 0]).astype(np.float32),
        "w2_words": w2_words, "w2_scales": w2_scales,
        "w3": (n((H, N)) / np.sqrt(H) * col / u).astype(np.float32),
    }

def reference(tab_words, tab_scales, offs, w1, wgs, offs2, offs3, offs4, rest, gz, w2_words, w2_scales, w3):
    v = unpack_weight(tab_words, tab_scales, "e4m3")[:, unstriped(offs)]
    h = np.exp(mxq(f64(w1), 0, "e4m3").T @ v)
    page = np.zeros((H, T2))
    page[:, unstriped(offs2)] = np.tile(f64(wgs), (H // 128, 1)) * h
    parent = page[:, unstriped(offs3)]
    daughter = page[:, unstriped(offs4)]
    z = f64(gz)[:, None] * (parent + f64(rest)) / (1.0 + np.square(daughter))
    zq = mxq(z, 0, "e4m3")
    a = unpack_weight(w2_words, w2_scales, "e2m1").T @ zq
    b = mxq(f64(w3), 0, "e4m3").T @ zq
    y = a - b / (1.0 + np.exp(-b))
    words, scales = planes(y)
    return y, words, scales

@@ -1,0 +1,349 @@
+from contextlib import ExitStack
+
+import concourse.mybir as mybir
+
+K, T, S, H, T2, PAIRS, N = 1024, 2048, 1024, 1024, 2048, 1024, 512
+FLOPS = 2 * K * H * S + 2 * 2 * H * N * PAIRS
+
+F32 = mybir.dt.float32
+BF16 = mybir.dt.bfloat16
+I32 = mybir.dt.int32
+U32 = mybir.dt.uint32
+U16 = mybir.dt.uint16
+U8 = mybir.dt.uint8
+FP8X4 = mybir.dt.float8_e4m3fn_x4
+FP4X4 = mybir.dt.float4_e2m1fn_x4
+ACT = mybir.ActivationFunctionType
+ALU = mybir.AluOpType
+
+P = 128
+PACK = 4
+KP = P * PACK
+BANK = 512
+LN_FLOOR = 2.0 ** -60
+CHUNKS = ((0, 256), (256, 256), (512, 256), (768, 128), (896, 128))
+
+
+def tile_list_airway_tree_step_kernel(
+    tc, tab_words, tab_scales, offs, w1, wgs, offs2, offs3, offs4, rest, gz,
+    w2_words, w2_scales, w3, out_0, out_1, out_2,
+):
+    nc = tc.nc
+    with ExitStack() as ctx:
+        keep = ctx.enter_context(tc.tile_pool(name="keep", bufs=1))
+        psum = ctx.enter_context(tc.psum_pool(name="psum", bufs=8))
+
+        lists = {}
+        for name in ("offs", "offs2", "offs3", "offs4"):
+            lists[name] = keep.tile([P, S // 16], U16, name=name)
+
+        with tc.tile_pool(name="early", bufs=1) as early:
+            tab_s = early.tile([P, T], U8, name="tab_s")
+            w2_s_raw = early.tile([P, 2 * N], U8, name="w2_s_raw")
+            nc.vector.memset(tab_s[:].bitcast(I32), 0)
+            nc.vector.memset(w2_s_raw[:].bitcast(I32), 0)
+            pages = [keep.tile([P, T2], F32, name="page%d" % i) for i in range(2)]
+            for page in pages:
+                nc.vector.memset(page[:], 0.0)
+
+            def load_weight(w, a, b):
+                raw = early.tile([P, PACK, KP], F32, name="w_raw", tag="w_raw", bufs=3)
+                nc.sync.dma_start(
+                    out=raw[:],
+                    in_=w[KP * a : KP * (a + 1), KP * b : KP * (b + 1)].rearrange("(p j) c -> p j c", j=PACK),
+                )
+                return raw
+
+            def staging():
+                return keep.tile([P, PACK * KP], BF16, name="stage", tag="stage", bufs=3, align_bytes=64)
+
+            def quantize_weight(raw, name):
+                stage = staging()
+                nc.scalar.copy(
+                    out=stage[:].rearrange("p (t m j) -> p m t j", t=PACK, j=PACK),
+                    in_=raw[:].rearrange("p j (m t) -> p m t j", t=PACK),
+                )
+                codes = keep.tile([P, KP], U32, name=name + "_c", align_bytes=64)
+                scales = keep.tile([P, KP], U8, name=name + "_s", align_bytes=64)
+                nc.vector.quantize_mx(out=codes[:].bitcast(FP8X4), scales=scales[:], in_=stage[:])
+                return codes, scales
+
+            nc.sync.dma_start(lists["offs"][:], offs)
+            tab_s_dram = tab_scales.bitcast(I32)
+            for q in range(4):
+                nc.sync.dma_start(
+                    out=tab_s[32 * q : 32 * q + 8, :].bitcast(I32),
+                    in_=tab_s_dram[:, 4 * q : 4 * q + 4, :],
+                )
+            w1_raw = {(0, 0): load_weight(w1, 0, 0)}
+            w2_w_raw = early.tile([P, 2, 2 * N], U8, name="w2_w_raw")
+            nc.sync.dma_start(out=w2_w_raw[:].bitcast(I32), in_=w2_words.bitcast(I32).rearrange("a p c -> p a c"))
+            w2_s_dram = w2_scales.bitcast(I32)
+            for q in range(4):
+                nc.sync.dma_start(
+                    out=w2_s_raw[32 * q : 32 * q + 4, :].bitcast(I32).rearrange("r (a c) -> r a c", a=2),
+                    in_=w2_s_dram[:, 4 * q : 4 * q + 4, :].rearrange("a r c -> r a c"),
+                )
+
+            def load_table(a):
+                tw = keep.tile([P, T], U32, name="tab_w%d" % a, tag="slot%d" % a)
+                nc.sync.dma_start(out=tw[:].bitcast(I32), in_=tab_words[a].rearrange("p t i -> p (t i)").bitcast(I32))
+                return tw
+
+            tab_w = [load_table(0)]
+            w1_raw[1, 0] = load_weight(w1, 1, 0)
+            tab_w.append(load_table(1))
+            nc.sync.dma_start(lists["offs2"][:], offs2)
+            wgs_rows = wgs.rearrange("(i t) j -> i t j", t=PACK)
+            wgs_first = keep.tile([P, S], F32, name="wgs_first")
+            wgs_later = keep.tile([P, (PACK - 1) * S], F32, name="wgs_later")
+            for q in range(4):
+                nc.sync.dma_start(out=wgs_first[32 * q : 32 * (q + 1), :], in_=wgs_rows[:, 0, :])
+            nc.sync.dma_start(lists["offs4"][:], offs4)
+            nc.sync.dma_start(lists["offs3"][:], offs3)
+            for q in range(4):
+                nc.sync.dma_start(
+                    out=wgs_later[32 * q : 32 * (q + 1), :],
+                    in_=wgs_rows[:, 1:PACK, :].rearrange("i t j -> i (t j)"),
+                )
+            wgs_t = [wgs_first[:]] + [wgs_later[:, S * t : S * (t + 1)] for t in range(PACK - 1)]
+            gz_sb = keep.tile([P, 2, PACK], F32, name="gz_sb")
+            nc.sync.dma_start(out=gz_sb[:], in_=gz.rearrange("(b p t) -> p b t", b=2, t=PACK))
+
+            rest_rows = rest.rearrange("(b p t) m -> b t p m", b=2, t=PACK)
+
+            def load_rest(s):
+                tile = keep.tile([P, PAIRS], F32, name="rest_sb", tag="rest_sb", bufs=5)
+                nc.sync.dma_start(out=tile[:], in_=rest_rows[s // PACK, s % PACK])
+                return tile
+
+            rest_sb = {0: load_rest(0)}
+
+            v_s = keep.tile([P, S], U8, name="v_s", align_bytes=64)
+            nc.vector.tensor_copy(out=v_s[:], in_=tab_s[:].indirect(lists["offs"][:]))
+            w2_w = keep.tile([P, 2 * 2 * N], U8, name="w2_w", align_bytes=64)
+            w2_s = keep.tile([P, 2 * N], U8, name="w2_s", align_bytes=64)
+            nc.vector.tensor_copy(
+                out=w2_w[:].rearrange("p (a t m e) -> p a t m e", a=2, t=PACK, e=2),
+                in_=w2_w_raw[:].rearrange("p a (m t e) -> p a t m e", t=PACK, e=2),
+            )
+            nc.vector.tensor_copy(
+                out=w2_s[:].rearrange("p (a t m) -> p a t m", a=2, t=PACK),
+                in_=w2_s_raw[:].rearrange("p (a m t) -> p a t m", a=2, t=PACK),
+            )
+            v_w = [keep.tile([P, S], U32, name="v_w%d" % a, align_bytes=64) for a in range(2)]
+            w1_q = {}
+            nc.vector.tensor_copy(out=v_w[0][:], in_=tab_w[0][:].indirect(lists["offs"][:]))
+            for a in range(2):
+                w1_q[a, 0] = quantize_weight(w1_raw[a, 0], "w1_%d0" % a)
+            for half in range(2):
+                nc.vector.tensor_copy(
+                    out=v_w[1][:, BANK * half : BANK * (half + 1)],
+                    in_=tab_w[1][:].indirect(lists["offs"][:, 32 * half : 32 * (half + 1)]),
+                )
+            for a in range(2):
+                page = keep.tile([P, T2], F32, name="page%d" % (2 + a), tag="slot%d" % a)
+                nc.gpsimd.memset(page[:], 0.0)
+                pages.append(page)
+
+            h_sb = {}
+
+            def features(s):
+                b, t = divmod(s, PACK)
+                h = keep.tile([P, S], F32, name="h", tag="h", bufs=8)
+                for half in range(2):
+                    cols = slice(BANK * half, BANK * (half + 1))
+                    acc = psum.tile([P, BANK], F32, name="acc", tag="ring")
+                    for a in range(2):
+                        codes, scales = w1_q[a, b]
+                        nc.tensor.matmul_mx(
+                            out=acc[:],
+                            lhsT=codes[:, P * t : P * (t + 1)].bitcast(FP8X4),
+                            lhsT_scale=scales[:, P * t : P * (t + 1)],
+                            rhs=v_w[a][:, cols].bitcast(FP8X4),
+                            rhs_scale=v_s[4 * a : P, cols],
+                            start=(a == 0),
+                            stop=(a == 1),
+                        )
+                    nc.scalar.activation(out=h[:, cols], in_=acc[:], func=ACT.Exp)
+                h_sb[s] = h
+
+            def scatter(s):
+                nc.vector.tensor_tensor(
+                    out=pages[s % PACK][:].indirect(lists["offs2"][:]), in0=h_sb[s][:], in1=wgs_t[s % PACK], op=ALU.mult
+                )
+
+            damp = {}
+
+            def damping(s):
+                b, t = divmod(s, PACK)
+                d = damp[b][:, t, :]
+                nc.vector.tensor_copy(out=d, in_=pages[t][:].indirect(lists["offs4"][:]))
+                nc.scalar.activation(out=d, in_=d, func=ACT.Ln, bias=LN_FLOOR)
+                nc.scalar.activation(out=d, in_=d, func=ACT.Sigmoid, scale=-2.0)
+                nc.scalar.activation(out=d, in_=d, func=ACT.Copy, scale=gz_sb[:, b, t : t + 1])
+
+            def parents(out, s, m0, w):
+                nc.vector.tensor_tensor(
+                    out=out,
+                    in0=pages[s % PACK][:].indirect(lists["offs3"][:, m0 // 16 : (m0 + w) // 16]),
+                    in1=rest_sb[s][:, m0 : m0 + w],
+                    op=ALU.add,
+                )
+
+            z_c = [keep.tile([P, PAIRS], U32, name="z_c%d" % b, align_bytes=64) for b in range(2)]
+            z_s = [keep.tile([P, PAIRS], U8, name="z_s%d" % b, align_bytes=64) for b in range(2)]
+
+            def make_z(b, summed, m0, w, stage):
+                nc.vector.tensor_tensor(
+                    out=stage[:, 0 : PACK * w].rearrange("p (c i t) -> p c t i", i=2, t=PACK),
+                    in0=summed.rearrange("p t (c i) -> p c t i", i=2),
+                    in1=damp[b][:, :, m0 : m0 + w].rearrange("p t (c i) -> p c t i", i=2),
+                    op=ALU.mult,
+                )
+                return stage
+
+            def quantize_z(b, stage, m0, w):
+                nc.vector.quantize_mx(
+                    out=z_c[b][:, m0 : m0 + w].bitcast(FP8X4), scales=z_s[b][:, m0 : m0 + w], in_=stage[:, 0 : PACK * w]
+                )
+
+            for s in range(PACK):
+                features(s)
+            for a in range(2):
+                w1_raw[a, 1] = load_weight(w1, a, 1)
+            for s in range(1, PACK):
+                rest_sb[s] = load_rest(s)
+            for a in range(2):
+                w1_q[a, 1] = quantize_weight(w1_raw[a, 1], "w1_%d1" % a)
+            w3_raw = [load_weight(w3, a, 0) for a in range(2)]
+            rest_sb[PACK] = load_rest(PACK)
+            for s in range(PACK, 2 * PACK):
+                features(s)
+            w3_q = [quantize_weight(w3_raw[a], "w3_%d" % a) for a in range(2)]
+        late = ctx.enter_context(tc.tile_pool(name="late", bufs=1))
+
+        damp[0] = keep.tile([P, PACK, PAIRS], F32, name="damp0")
+        damp[1] = keep.tile([P, PACK, PAIRS], F32, name="damp1")
+        summed0 = keep.tile([P, PACK, PAIRS], F32, name="summed0")
+        for half in range(2):
+            cols = slice(BANK * half, BANK * (half + 1))
+            nc.vector.tensor_tensor(
+                out=pages[0][:].indirect(lists["offs2"][:, 32 * half : 32 * (half + 1)]),
+                in0=h_sb[0][:, cols],
+                in1=wgs_first[:, cols],
+                op=ALU.mult,
+            )
+        for s in range(PACK):
+            scatter(s + 1)
+            damping(s)
+            parents(summed0[:, s, :], s, 0, PAIRS)
+            if s > 0:
+                rest_sb[PACK + s] = load_rest(PACK + s)
+        scatter(PACK + 1)
+        damping(PACK)
+        scatter(PACK + 2)
+        damping(PACK + 1)
+        damping(PACK + 2)
+        scatter(PACK + 3)
+        damping(PACK + 3)
+        stages = [make_z(0, summed0[:, :, BANK * i : BANK * (i + 1)], BANK * i, BANK, staging()) for i in range(2)]
+        for i in range(2):
+            quantize_z(0, stages[i], BANK * i, BANK)
+
+        def second_pass(acc_a, acc_b, b, t, m0, w, start, stop):
+            cols = slice(m0, m0 + w)
+            nc.tensor.matmul_mx(
+                out=acc_b,
+                lhsT=w3_q[b][0][:, P * t : P * (t + 1)].bitcast(FP8X4),
+                lhsT_scale=w3_q[b][1][:, P * t : P * (t + 1)],
+                rhs=z_c[b][:, cols].bitcast(FP8X4),
+                rhs_scale=z_s[b][:, cols],
+                start=start,
+                stop=stop,
+            )
+            c0 = N * b + P * t
+            nc.tensor.matmul_mx(
+                out=acc_a,
+                lhsT=w2_w[:, 2 * c0 : 2 * (c0 + P)].bitcast(FP4X4),
+                lhsT_scale=w2_s[:, c0 : c0 + P],
+                rhs=z_c[b][:, cols].bitcast(FP8X4),
+                rhs_scale=z_s[b][:, cols],
+                start=start,
+                stop=stop,
+            )
+
+        y_c = late.tile([P, PAIRS], U32, name="y_c", align_bytes=64)
+        y_s = late.tile([P, PAIRS], U8, name="y_s", align_bytes=64)
+        out_rows = out_0.rearrange("(p t) m -> p t m", t=PACK)
+        out_words = out_1[0].rearrange("p m t -> p (m t)").bitcast(I32)
+        out_scales = out_2[0].bitcast(I32)
+
+        def subtract(y, acc_a, acc_b):
+            gate = late.tile([P, BANK], F32, name="gate", tag="gate", bufs=3)
+            nc.scalar.activation(out=gate[:], in_=acc_b, func=ACT.Silu)
+            nc.vector.tensor_tensor(out=y, in0=acc_a, in1=gate[:], op=ALU.subtract)
+
+        def hand_out(y, m0, w, on_vector):
+            nc.sync.dma_start(out=out_rows[:, :, m0 : m0 + w], in_=y[:])
+            stage = late.tile([P, PACK * w], BF16, name="y_stage", tag="y_stage", bufs=3, align_bytes=64)
+            dst = stage[:, 0 : PACK * w].rearrange("p (c i t) -> p c t i", i=2, t=PACK)
+            src = y[:].rearrange("p t (c i) -> p c t i", i=2)
+            if on_vector:
+                nc.vector.tensor_copy(out=dst, in_=src)
+            else:
+                nc.scalar.copy(out=dst, in_=src)
+            nc.vector.quantize_mx(
+                out=y_c[:, m0 : m0 + w].bitcast(FP8X4), scales=y_s[:, m0 : m0 + w], in_=stage[:, 0 : PACK * w]
+            )
+            nc.sync.dma_start(out=out_words[:, m0 : m0 + w], in_=y_c[:, m0 : m0 + w].bitcast(I32))
+
+        opened = {}
+
+        def open_tile(m0):
+            acc_a = psum.tile([P, BANK], F32, name="acc", tag="ring")
+            acc_b = psum.tile([P, BANK], F32, name="acc", tag="ring")
+            for t in range(PACK):
+                cols = slice(P * t, P * (t + 1))
+                second_pass(acc_a[:, cols], acc_b[:, cols], 0, t, m0, P, t == 0, False)
+            opened[m0] = (acc_a, acc_b)
+
+        def close_tile(m0):
+            acc_a, acc_b = opened[m0]
+            for t in range(PACK):
+                cols = slice(P * t, P * (t + 1))
+                second_pass(acc_a[:, cols], acc_b[:, cols], 1, t, m0, P, False, t == PACK - 1)
+
+        def finish_tile(m0):
+            acc_a, acc_b = opened[m0]
+            y = late.tile([P, PACK, P], F32, name="y", tag="y", bufs=4)
+            subtract(y[:].rearrange("p t m -> p (t m)"), acc_a[:], acc_b[:])
+            hand_out(y, m0, P, m0 >= PAIRS - 2 * P)
+            if m0 + BANK < PAIRS:
+                open_tile(m0 + BANK)
+
+        def chunk_front(m0, w):
+            part = late.tile([P, PACK, w], F32, name="summed1", tag="summed1", bufs=2)
+            for t in range(PACK):
+                parents(part[:, t, :], PACK + t, m0, w)
+            return part
+
+        for m0 in range(0, BANK, P):
+            open_tile(m0)
+        parts = [chunk_front(*CHUNKS[0]), chunk_front(*CHUNKS[1])]
+        for i, (m0, w) in enumerate(CHUNKS):
+            stage = late.tile([P, PACK * w], BF16, name="z_stage", tag="z_stage", bufs=2, align_bytes=64)
+            make_z(1, parts[i][:], m0, w, stage)
+            if i + 2 < len(CHUNKS):
+                parts.append(chunk_front(*CHUNKS[i + 2]))
+            quantize_z(1, stage, m0, w)
+            if i > 0:
+                before, width = CHUNKS[i - 1]
+                for m1 in range(before, before + width, P):
+                    finish_tile(m1)
+            for m1 in range(m0, m0 + w, P):
+                close_tile(m1)
+        finish_tile(CHUNKS[-1][0])
+        for q in range(4):
+            queue = nc.sync if q % 2 == 0 else nc.scalar
+            queue.dma_start(out=out_scales[4 * q : 4 * q + 4, :], in_=y_s[32 * q : 32 * q + 4, :].bitcast(I32))

@@ -40,11 +40,11 @@ def tile_list_airway_tree_step_kernel(
         with tc.tile_pool(name="early", bufs=1) as early:
             tab_s = early.tile([P, T], U8, name="tab_s")
             w2_s_raw = early.tile([P, 2 * N], U8, name="w2_s_raw")
-            nc.vector.memset(tab_s[:].bitcast(I32), 0)
-            nc.vector.memset(w2_s_raw[:].bitcast(I32), 0)
+            nc.gpsimd.memset(tab_s[:].bitcast(I32), 0)
+            nc.gpsimd.memset(w2_s_raw[:].bitcast(I32), 0)
             pages = [keep.tile([P, T2], F32, name="page%d" % i) for i in range(2)]
             for page in pages:
-                nc.vector.memset(page[:], 0.0)
+                nc.gpsimd.memset(page[:], 0.0)
 
             def load_weight(w, a, b):
                 raw = early.tile([P, PACK, KP], F32, name="w_raw", tag="w_raw", bufs=3)
@@ -68,31 +68,28 @@ def tile_list_airway_tree_step_kernel(
                 nc.vector.quantize_mx(out=codes[:].bitcast(FP8X4), scales=scales[:], in_=stage[:])
                 return codes, scales
 
+            def load_table(a):
+                tw = keep.tile([P, T], U32, name="tab_w%d" % a, tag="slot%d" % a)
+                nc.sync.dma_start(out=tw[:].bitcast(I32), in_=tab_words[a].rearrange("p t i -> p (t i)").bitcast(I32))
+                return tw
+
             nc.sync.dma_start(lists["offs"][:], offs)
+            w2_w_raw = early.tile([P, 2, 2 * N], U8, name="w2_w_raw")
+            nc.sync.dma_start(out=w2_w_raw[:].bitcast(I32), in_=w2_words.bitcast(I32).rearrange("a p c -> p a c"))
             tab_s_dram = tab_scales.bitcast(I32)
             for q in range(4):
                 nc.sync.dma_start(
                     out=tab_s[32 * q : 32 * q + 8, :].bitcast(I32),
                     in_=tab_s_dram[:, 4 * q : 4 * q + 4, :],
                 )
-            w1_raw = {(0, 0): load_weight(w1, 0, 0)}
-            w2_w_raw = early.tile([P, 2, 2 * N], U8, name="w2_w_raw")
-            nc.sync.dma_start(out=w2_w_raw[:].bitcast(I32), in_=w2_words.bitcast(I32).rearrange("a p c -> p a c"))
+            w1_raw = {(a, 0): load_weight(w1, a, 0) for a in range(2)}
+            tab_w = [load_table(a) for a in range(2)]
             w2_s_dram = w2_scales.bitcast(I32)
             for q in range(4):
                 nc.sync.dma_start(
                     out=w2_s_raw[32 * q : 32 * q + 4, :].bitcast(I32).rearrange("r (a c) -> r a c", a=2),
                     in_=w2_s_dram[:, 4 * q : 4 * q + 4, :].rearrange("a r c -> r a c"),
                 )
-
-            def load_table(a):
-                tw = keep.tile([P, T], U32, name="tab_w%d" % a, tag="slot%d" % a)
-                nc.sync.dma_start(out=tw[:].bitcast(I32), in_=tab_words[a].rearrange("p t i -> p (t i)").bitcast(I32))
-                return tw
-
-            tab_w = [load_table(0)]
-            w1_raw[1, 0] = load_weight(w1, 1, 0)
-            tab_w.append(load_table(1))
             nc.sync.dma_start(lists["offs2"][:], offs2)
             wgs_rows = wgs.rearrange("(i t) j -> i t j", t=PACK)
             wgs_first = keep.tile([P, S], F32, name="wgs_first")
@@ -119,28 +116,26 @@ def tile_list_airway_tree_step_kernel(
 
             rest_sb = {0: load_rest(0)}
 
-            v_s = keep.tile([P, S], U8, name="v_s", align_bytes=64)
-            nc.vector.tensor_copy(out=v_s[:], in_=tab_s[:].indirect(lists["offs"][:]))
             w2_w = keep.tile([P, 2 * 2 * N], U8, name="w2_w", align_bytes=64)
             w2_s = keep.tile([P, 2 * N], U8, name="w2_s", align_bytes=64)
             nc.vector.tensor_copy(
                 out=w2_w[:].rearrange("p (a t m e) -> p a t m e", a=2, t=PACK, e=2),
                 in_=w2_w_raw[:].rearrange("p a (m t e) -> p a t m e", t=PACK, e=2),
             )
-            nc.vector.tensor_copy(
-                out=w2_s[:].rearrange("p (a t m) -> p a t m", a=2, t=PACK),
-                in_=w2_s_raw[:].rearrange("p (a m t) -> p a t m", a=2, t=PACK),
-            )
+            v_s = keep.tile([P, S], U8, name="v_s", align_bytes=64)
+            nc.vector.tensor_copy(out=v_s[:], in_=tab_s[:].indirect(lists["offs"][:]))
+            w1_q = {(a, 0): quantize_weight(w1_raw[a, 0], "w1_%d0" % a) for a in range(2)}
             v_w = [keep.tile([P, S], U32, name="v_w%d" % a, align_bytes=64) for a in range(2)]
-            w1_q = {}
             nc.vector.tensor_copy(out=v_w[0][:], in_=tab_w[0][:].indirect(lists["offs"][:]))
-            for a in range(2):
-                w1_q[a, 0] = quantize_weight(w1_raw[a, 0], "w1_%d0" % a)
             for half in range(2):
                 nc.vector.tensor_copy(
                     out=v_w[1][:, BANK * half : BANK * (half + 1)],
                     in_=tab_w[1][:].indirect(lists["offs"][:, 32 * half : 32 * (half + 1)]),
                 )
+            nc.vector.tensor_copy(
+                out=w2_s[:].rearrange("p (a t m) -> p a t m", a=2, t=PACK),
+                in_=w2_s_raw[:].rearrange("p (a m t) -> p a t m", a=2, t=PACK),
+            )
             for a in range(2):
                 page = keep.tile([P, T2], F32, name="page%d" % (2 + a), tag="slot%d" % a)
                 nc.gpsimd.memset(page[:], 0.0)
@@ -181,7 +176,10 @@ def tile_list_airway_tree_step_kernel(
                 nc.vector.tensor_copy(out=d, in_=pages[t][:].indirect(lists["offs4"][:]))
                 nc.scalar.activation(out=d, in_=d, func=ACT.Ln, bias=LN_FLOOR)
                 nc.scalar.activation(out=d, in_=d, func=ACT.Sigmoid, scale=-2.0)
-                nc.scalar.activation(out=d, in_=d, func=ACT.Copy, scale=gz_sb[:, b, t : t + 1])
+
+            def gain(rows, s):
+                b, t = divmod(s, PACK)
+                nc.scalar.activation(out=rows, in_=rows, func=ACT.Copy, scale=gz_sb[:, b, t : t + 1])
 
             def parents(out, s, m0, w):
                 nc.vector.tensor_tensor(
@@ -238,21 +236,33 @@ def tile_list_airway_tree_step_kernel(
             scatter(s + 1)
             damping(s)
             parents(summed0[:, s, :], s, 0, PAIRS)
+            nc.gpsimd.tensor_tensor(out=summed0[:, s, :], in0=summed0[:, s, :], in1=damp[0][:, s, :], op=ALU.mult)
+            gain(summed0[:, s, :], s)
             if s > 0:
                 rest_sb[PACK + s] = load_rest(PACK + s)
-        scatter(PACK + 1)
-        damping(PACK)
-        scatter(PACK + 2)
-        damping(PACK + 1)
-        damping(PACK + 2)
-        scatter(PACK + 3)
-        damping(PACK + 3)
-        stages = [make_z(0, summed0[:, :, BANK * i : BANK * (i + 1)], BANK * i, BANK, staging()) for i in range(2)]
-        for i in range(2):
-            quantize_z(0, stages[i], BANK * i, BANK)
 
-        def second_pass(acc_a, acc_b, b, t, m0, w, start, stop):
-            cols = slice(m0, m0 + w)
+
+        def damping_with_gain(t):
+            damping(PACK + t)
+            gain(damp[1][:, t, :], PACK + t)
+
+        scatter(PACK + 1)
+        damping_with_gain(0)
+        scatter(PACK + 2)
+        damping_with_gain(1)
+        for i in range(2):
+            stage = staging()
+            nc.scalar.copy(
+                out=stage[:].rearrange("p (c i t) -> p c t i", i=2, t=PACK),
+                in_=summed0[:, :, BANK * i : BANK * (i + 1)].rearrange("p t (c i) -> p c t i", i=2),
+            )
+            quantize_z(0, stage, BANK * i, BANK)
+        damping_with_gain(2)
+        scatter(PACK + 3)
+        damping_with_gain(3)
+
+        def pass_w3(acc_b, b, t, m0, start, stop):
+            cols = slice(m0, m0 + P)
             nc.tensor.matmul_mx(
                 out=acc_b,
                 lhsT=w3_q[b][0][:, P * t : P * (t + 1)].bitcast(FP8X4),
@@ -262,6 +272,9 @@ def tile_list_airway_tree_step_kernel(
                 start=start,
                 stop=stop,
             )
+
+        def pass_w2(acc_a, b, t, m0, start, stop):
+            cols = slice(m0, m0 + P)
             c0 = N * b + P * t
             nc.tensor.matmul_mx(
                 out=acc_a,
@@ -305,14 +318,16 @@ def tile_list_airway_tree_step_kernel(
             acc_b = psum.tile([P, BANK], F32, name="acc", tag="ring")
             for t in range(PACK):
                 cols = slice(P * t, P * (t + 1))
-                second_pass(acc_a[:, cols], acc_b[:, cols], 0, t, m0, P, t == 0, False)
+                pass_w3(acc_b[:, cols], 0, t, m0, t == 0, False)
+                pass_w2(acc_a[:, cols], 0, t, m0, t == 0, False)
             opened[m0] = (acc_a, acc_b)
 
         def close_tile(m0):
             acc_a, acc_b = opened[m0]
             for t in range(PACK):
-                cols = slice(P * t, P * (t + 1))
-                second_pass(acc_a[:, cols], acc_b[:, cols], 1, t, m0, P, False, t == PACK - 1)
+                pass_w3(acc_b[:, P * t : P * (t + 1)], 1, t, m0, False, t == PACK - 1)
+            for t in range(PACK):
+                pass_w2(acc_a[:, P * t : P * (t + 1)], 1, t, m0, False, t == PACK - 1)
 
         def finish_tile(m0):
             acc_a, acc_b = opened[m0]
@@ -323,19 +338,19 @@ def tile_list_airway_tree_step_kernel(
                 open_tile(m0 + BANK)
 
         def chunk_front(m0, w):
-            part = late.tile([P, PACK, w], F32, name="summed1", tag="summed1", bufs=2)
+            part = late.tile([P, PACK, w], F32, name="summed1", tag="summed1", bufs=3)
             for t in range(PACK):
                 parents(part[:, t, :], PACK + t, m0, w)
             return part
 
         for m0 in range(0, BANK, P):
             open_tile(m0)
-        parts = [chunk_front(*CHUNKS[0]), chunk_front(*CHUNKS[1])]
+        parts = [chunk_front(*CHUNKS[i]) for i in range(3)]
         for i, (m0, w) in enumerate(CHUNKS):
             stage = late.tile([P, PACK * w], BF16, name="z_stage", tag="z_stage", bufs=2, align_bytes=64)
             make_z(1, parts[i][:], m0, w, stage)
-            if i + 2 < len(CHUNKS):
-                parts.append(chunk_front(*CHUNKS[i + 2]))
+            if i + 3 < len(CHUNKS):
+                parts.append(chunk_front(*CHUNKS[i + 3]))
             quantize_z(1, stage, m0, w)
             if i > 0:
                 before, width = CHUNKS[i - 1]

@@ -42,12 +42,12 @@ def tile_list_airway_tree_step_kernel(
             w2_s_raw = early.tile([P, 2 * N], U8, name="w2_s_raw")
             nc.gpsimd.memset(tab_s[:].bitcast(I32), 0)
             nc.gpsimd.memset(w2_s_raw[:].bitcast(I32), 0)
-            pages = [keep.tile([P, T2], F32, name="page%d" % i) for i in range(2)]
+            pages = [keep.tile([P, T2], F32, name="page%d" % i) for i in range(PACK)]
             for page in pages:
-                nc.gpsimd.memset(page[:], 0.0)
+                nc.vector.memset(page[:], 0.0)
 
             def load_weight(w, a, b):
-                raw = early.tile([P, PACK, KP], F32, name="w_raw", tag="w_raw", bufs=3)
+                raw = early.tile([P, PACK, KP], F32, name="w_raw", tag="w_raw", bufs=4)
                 nc.sync.dma_start(
                     out=raw[:],
                     in_=w[KP * a : KP * (a + 1), KP * b : KP * (b + 1)].rearrange("(p j) c -> p j c", j=PACK),
@@ -69,7 +69,7 @@ def tile_list_airway_tree_step_kernel(
                 return codes, scales
 
             def load_table(a):
-                tw = keep.tile([P, T], U32, name="tab_w%d" % a, tag="slot%d" % a)
+                tw = early.tile([P, T], U32, name="tab_w", tag="w_raw", bufs=4)
                 nc.sync.dma_start(out=tw[:].bitcast(I32), in_=tab_words[a].rearrange("p t i -> p (t i)").bitcast(I32))
                 return tw
 
@@ -136,16 +136,13 @@ def tile_list_airway_tree_step_kernel(
                 out=w2_s[:].rearrange("p (a t m) -> p a t m", a=2, t=PACK),
                 in_=w2_s_raw[:].rearrange("p (a m t) -> p a t m", a=2, t=PACK),
             )
-            for a in range(2):
-                page = keep.tile([P, T2], F32, name="page%d" % (2 + a), tag="slot%d" % a)
-                nc.gpsimd.memset(page[:], 0.0)
-                pages.append(page)
 
+            h_all = keep.tile([P, 2 * PACK, S], F32, name="h_all")
             h_sb = {}
 
             def features(s):
                 b, t = divmod(s, PACK)
-                h = keep.tile([P, S], F32, name="h", tag="h", bufs=8)
+                h = h_all[:, s, :]
                 for half in range(2):
                     cols = slice(BANK * half, BANK * (half + 1))
                     acc = psum.tile([P, BANK], F32, name="acc", tag="ring")
@@ -165,7 +162,7 @@ def tile_list_airway_tree_step_kernel(
 
             def scatter(s):
                 nc.vector.tensor_tensor(
-                    out=pages[s % PACK][:].indirect(lists["offs2"][:]), in0=h_sb[s][:], in1=wgs_t[s % PACK], op=ALU.mult
+                    out=pages[s % PACK][:].indirect(lists["offs2"][:]), in0=h_sb[s], in1=wgs_t[s % PACK], op=ALU.mult
                 )
 
             damp = {}
@@ -176,10 +173,7 @@ def tile_list_airway_tree_step_kernel(
                 nc.vector.tensor_copy(out=d, in_=pages[t][:].indirect(lists["offs4"][:]))
                 nc.scalar.activation(out=d, in_=d, func=ACT.Ln, bias=LN_FLOOR)
                 nc.scalar.activation(out=d, in_=d, func=ACT.Sigmoid, scale=-2.0)
-
-            def gain(rows, s):
-                b, t = divmod(s, PACK)
-                nc.scalar.activation(out=rows, in_=rows, func=ACT.Copy, scale=gz_sb[:, b, t : t + 1])
+                nc.scalar.activation(out=d, in_=d, func=ACT.Copy, scale=gz_sb[:, b, t : t + 1])
 
             def parents(out, s, m0, w):
                 nc.vector.tensor_tensor(
@@ -236,30 +230,19 @@ def tile_list_airway_tree_step_kernel(
             scatter(s + 1)
             damping(s)
             parents(summed0[:, s, :], s, 0, PAIRS)
-            nc.gpsimd.tensor_tensor(out=summed0[:, s, :], in0=summed0[:, s, :], in1=damp[0][:, s, :], op=ALU.mult)
-            gain(summed0[:, s, :], s)
             if s > 0:
                 rest_sb[PACK + s] = load_rest(PACK + s)
 
-
-        def damping_with_gain(t):
-            damping(PACK + t)
-            gain(damp[1][:, t, :], PACK + t)
-
         scatter(PACK + 1)
-        damping_with_gain(0)
+        damping(PACK)
         scatter(PACK + 2)
-        damping_with_gain(1)
-        for i in range(2):
-            stage = staging()
-            nc.scalar.copy(
-                out=stage[:].rearrange("p (c i t) -> p c t i", i=2, t=PACK),
-                in_=summed0[:, :, BANK * i : BANK * (i + 1)].rearrange("p t (c i) -> p c t i", i=2),
-            )
-            quantize_z(0, stage, BANK * i, BANK)
-        damping_with_gain(2)
+        damping(PACK + 1)
+        damping(PACK + 2)
         scatter(PACK + 3)
-        damping_with_gain(3)
+        damping(PACK + 3)
+        stages = [make_z(0, summed0[:, :, BANK * i : BANK * (i + 1)], BANK * i, BANK, staging()) for i in range(2)]
+        for i in range(2):
+            quantize_z(0, stages[i], BANK * i, BANK)
 
         def pass_w3(acc_b, b, t, m0, start, stop):
             cols = slice(m0, m0 + P)
@@ -338,19 +321,19 @@ def tile_list_airway_tree_step_kernel(
                 open_tile(m0 + BANK)
 
         def chunk_front(m0, w):
-            part = late.tile([P, PACK, w], F32, name="summed1", tag="summed1", bufs=3)
+            part = late.tile([P, PACK, w], F32, name="summed1", tag="summed1", bufs=2)
             for t in range(PACK):
                 parents(part[:, t, :], PACK + t, m0, w)
             return part
 
         for m0 in range(0, BANK, P):
             open_tile(m0)
-        parts = [chunk_front(*CHUNKS[i]) for i in range(3)]
+        parts = [chunk_front(*CHUNKS[i]) for i in range(2)]
         for i, (m0, w) in enumerate(CHUNKS):
             stage = late.tile([P, PACK * w], BF16, name="z_stage", tag="z_stage", bufs=2, align_bytes=64)
             make_z(1, parts[i][:], m0, w, stage)
-            if i + 3 < len(CHUNKS):
-                parts.append(chunk_front(*CHUNKS[i + 3]))
+            if i + 2 < len(CHUNKS):
+                parts.append(chunk_front(*CHUNKS[i + 2]))
             quantize_z(1, stage, m0, w)
             if i > 0:
                 before, width = CHUNKS[i - 1]

@@ -44,7 +44,7 @@ def tile_list_airway_tree_step_kernel(
             nc.gpsimd.memset(w2_s_raw[:].bitcast(I32), 0)
             pages = [keep.tile([P, T2], F32, name="page%d" % i) for i in range(PACK)]
             for page in pages:
-                nc.vector.memset(page[:], 0.0)
+                nc.vector.memset(page[:].bitcast(I32), 0)
 
             def load_weight(w, a, b):
                 raw = early.tile([P, PACK, KP], F32, name="w_raw", tag="w_raw", bufs=4)
@@ -84,28 +84,14 @@ def tile_list_airway_tree_step_kernel(
                 )
             w1_raw = {(a, 0): load_weight(w1, a, 0) for a in range(2)}
             tab_w = [load_table(a) for a in range(2)]
-            w2_s_dram = w2_scales.bitcast(I32)
-            for q in range(4):
-                nc.sync.dma_start(
-                    out=w2_s_raw[32 * q : 32 * q + 4, :].bitcast(I32).rearrange("r (a c) -> r a c", a=2),
-                    in_=w2_s_dram[:, 4 * q : 4 * q + 4, :].rearrange("a r c -> r a c"),
-                )
             nc.sync.dma_start(lists["offs2"][:], offs2)
-            wgs_rows = wgs.rearrange("(i t) j -> i t j", t=PACK)
-            wgs_first = keep.tile([P, S], F32, name="wgs_first")
-            wgs_later = keep.tile([P, (PACK - 1) * S], F32, name="wgs_later")
-            for q in range(4):
-                nc.sync.dma_start(out=wgs_first[32 * q : 32 * (q + 1), :], in_=wgs_rows[:, 0, :])
-            nc.sync.dma_start(lists["offs4"][:], offs4)
-            nc.sync.dma_start(lists["offs3"][:], offs3)
-            for q in range(4):
-                nc.sync.dma_start(
-                    out=wgs_later[32 * q : 32 * (q + 1), :],
-                    in_=wgs_rows[:, 1:PACK, :].rearrange("i t j -> i (t j)"),
-                )
-            wgs_t = [wgs_first[:]] + [wgs_later[:, S * t : S * (t + 1)] for t in range(PACK - 1)]
-            gz_sb = keep.tile([P, 2, PACK], F32, name="gz_sb")
-            nc.sync.dma_start(out=gz_sb[:], in_=gz.rearrange("(b p t) -> p b t", b=2, t=PACK))
+            wgs_rows = wgs.rearrange("(i t) j -> t i j", t=PACK)
+
+            def load_wgs(t):
+                tile = keep.tile([P, S], F32, name="wgs%d" % t)
+                for q in range(4):
+                    nc.sync.dma_start(out=tile[32 * q : 32 * (q + 1), :], in_=wgs_rows[t])
+                return tile
 
             rest_rows = rest.rearrange("(b p t) m -> b t p m", b=2, t=PACK)
 
@@ -114,7 +100,20 @@ def tile_list_airway_tree_step_kernel(
                 nc.sync.dma_start(out=tile[:], in_=rest_rows[s // PACK, s % PACK])
                 return tile
 
+            wgs_t = [load_wgs(t) for t in range(2)]
+            w2_s_dram = w2_scales.bitcast(I32)
+            for q in range(4):
+                nc.sync.dma_start(
+                    out=w2_s_raw[32 * q : 32 * q + 4, :].bitcast(I32).rearrange("r (a c) -> r a c", a=2),
+                    in_=w2_s_dram[:, 4 * q : 4 * q + 4, :].rearrange("a r c -> r a c"),
+                )
+            nc.sync.dma_start(lists["offs4"][:], offs4)
+            nc.sync.dma_start(lists["offs3"][:], offs3)
             rest_sb = {0: load_rest(0)}
+            wgs_t.append(load_wgs(2))
+            gz_sb = keep.tile([P, 2, PACK], F32, name="gz_sb")
+            nc.sync.dma_start(out=gz_sb[:], in_=gz.rearrange("(b p t) -> p b t", b=2, t=PACK))
+            wgs_t.append(load_wgs(3))
 
             w2_w = keep.tile([P, 2 * 2 * N], U8, name="w2_w", align_bytes=64)
             w2_s = keep.tile([P, 2 * N], U8, name="w2_s", align_bytes=64)
@@ -162,7 +161,7 @@ def tile_list_airway_tree_step_kernel(
 
             def scatter(s):
                 nc.vector.tensor_tensor(
-                    out=pages[s % PACK][:].indirect(lists["offs2"][:]), in0=h_sb[s], in1=wgs_t[s % PACK], op=ALU.mult
+                    out=pages[s % PACK][:].indirect(lists["offs2"][:]), in0=h_sb[s], in1=wgs_t[s % PACK][:], op=ALU.mult
                 )
 
             damp = {}
@@ -223,7 +222,7 @@ def tile_list_airway_tree_step_kernel(
             nc.vector.tensor_tensor(
                 out=pages[0][:].indirect(lists["offs2"][:, 32 * half : 32 * (half + 1)]),
                 in0=h_sb[0][:, cols],
-                in1=wgs_first[:, cols],
+                in1=wgs_t[0][:, cols],
                 op=ALU.mult,
             )
         for s in range(PACK):

@@ -1,6 +1,7 @@
 from contextlib import ExitStack
 
 import concourse.mybir as mybir
+from concourse.masks import make_identity
 
 K, T, S, H, T2, PAIRS, N = 1024, 2048, 1024, 1024, 2048, 1024, 512
 FLOPS = 2 * K * H * S + 2 * 2 * H * N * PAIRS
@@ -21,6 +22,7 @@ PACK = 4
 KP = P * PACK
 BANK = 512
 LN_FLOOR = 2.0 ** -60
+WHOLE = ((0, PAIRS),)
 CHUNKS = ((0, 256), (256, 256), (512, 256), (768, 128), (896, 128))
 
 
@@ -31,7 +33,7 @@ def tile_list_airway_tree_step_kernel(
     nc = tc.nc
     with ExitStack() as ctx:
         keep = ctx.enter_context(tc.tile_pool(name="keep", bufs=1))
-        psum = ctx.enter_context(tc.psum_pool(name="psum", bufs=8))
+        psum = ctx.enter_context(tc.psum_pool(name="psum", bufs=1))
 
         lists = {}
         for name in ("offs", "offs2", "offs3", "offs4"):
@@ -39,9 +41,11 @@ def tile_list_airway_tree_step_kernel(
 
         with tc.tile_pool(name="early", bufs=1) as early:
             tab_s = early.tile([P, T], U8, name="tab_s")
-            w2_s_raw = early.tile([P, 2 * N], U8, name="w2_s_raw")
+            w2_s = keep.tile([P, 2 * N], U8, name="w2_s", align_bytes=64)
+            ident = keep.tile([P, P], F32, name="ident")
             nc.gpsimd.memset(tab_s[:].bitcast(I32), 0)
-            nc.gpsimd.memset(w2_s_raw[:].bitcast(I32), 0)
+            nc.gpsimd.memset(w2_s[:].bitcast(I32), 0)
+            make_identity(nc, ident[:])
             pages = [keep.tile([P, T2], F32, name="page%d" % i) for i in range(PACK)]
             for page in pages:
                 nc.vector.memset(page[:].bitcast(I32), 0)
@@ -57,12 +61,18 @@ def tile_list_airway_tree_step_kernel(
             def staging():
                 return keep.tile([P, PACK * KP], BF16, name="stage", tag="stage", bufs=3, align_bytes=64)
 
-            def quantize_weight(raw, name):
+            def quantize_weight(raw, name, dealt):
                 stage = staging()
-                nc.scalar.copy(
-                    out=stage[:].rearrange("p (t m j) -> p m t j", t=PACK, j=PACK),
-                    in_=raw[:].rearrange("p j (m t) -> p m t j", t=PACK),
-                )
+                if dealt:
+                    nc.scalar.copy(
+                        out=stage[:].rearrange("p (t m j) -> p m t j", t=PACK, j=PACK),
+                        in_=raw[:].rearrange("p j (m t) -> p m t j", t=PACK),
+                    )
+                else:
+                    nc.scalar.copy(
+                        out=stage[:].rearrange("p (c i j) -> p c j i", i=PACK, j=PACK),
+                        in_=raw[:].rearrange("p j (c i) -> p c j i", i=PACK),
+                    )
                 codes = keep.tile([P, KP], U32, name=name + "_c", align_bytes=64)
                 scales = keep.tile([P, KP], U8, name=name + "_s", align_bytes=64)
                 nc.vector.quantize_mx(out=codes[:].bitcast(FP8X4), scales=scales[:], in_=stage[:])
@@ -74,8 +84,6 @@ def tile_list_airway_tree_step_kernel(
                 return tw
 
             nc.sync.dma_start(lists["offs"][:], offs)
-            w2_w_raw = early.tile([P, 2, 2 * N], U8, name="w2_w_raw")
-            nc.sync.dma_start(out=w2_w_raw[:].bitcast(I32), in_=w2_words.bitcast(I32).rearrange("a p c -> p a c"))
             tab_s_dram = tab_scales.bitcast(I32)
             for q in range(4):
                 nc.sync.dma_start(
@@ -88,7 +96,7 @@ def tile_list_airway_tree_step_kernel(
             wgs_rows = wgs.rearrange("(i t) j -> t i j", t=PACK)
 
             def load_wgs(t):
-                tile = keep.tile([P, S], F32, name="wgs%d" % t)
+                tile = keep.tile([P, S], F32, name="wgs%d" % t, tag="wgs%d" % t)
                 for q in range(4):
                     nc.sync.dma_start(out=tile[32 * q : 32 * (q + 1), :], in_=wgs_rows[t])
                 return tile
@@ -101,50 +109,32 @@ def tile_list_airway_tree_step_kernel(
                 return tile
 
             wgs_t = [load_wgs(t) for t in range(2)]
-            w2_s_dram = w2_scales.bitcast(I32)
-            for q in range(4):
-                nc.sync.dma_start(
-                    out=w2_s_raw[32 * q : 32 * q + 4, :].bitcast(I32).rearrange("r (a c) -> r a c", a=2),
-                    in_=w2_s_dram[:, 4 * q : 4 * q + 4, :].rearrange("a r c -> r a c"),
-                )
-            nc.sync.dma_start(lists["offs4"][:], offs4)
-            nc.sync.dma_start(lists["offs3"][:], offs3)
-            rest_sb = {0: load_rest(0)}
-            wgs_t.append(load_wgs(2))
-            gz_sb = keep.tile([P, 2, PACK], F32, name="gz_sb")
-            nc.sync.dma_start(out=gz_sb[:], in_=gz.rearrange("(b p t) -> p b t", b=2, t=PACK))
-            wgs_t.append(load_wgs(3))
 
-            w2_w = keep.tile([P, 2 * 2 * N], U8, name="w2_w", align_bytes=64)
-            w2_s = keep.tile([P, 2 * N], U8, name="w2_s", align_bytes=64)
-            nc.vector.tensor_copy(
-                out=w2_w[:].rearrange("p (a t m e) -> p a t m e", a=2, t=PACK, e=2),
-                in_=w2_w_raw[:].rearrange("p a (m t e) -> p a t m e", t=PACK, e=2),
-            )
-            v_s = keep.tile([P, S], U8, name="v_s", align_bytes=64)
+            v_s = keep.tile([P, S], U8, name="v_s", tag="summed0", align_bytes=64)
             nc.vector.tensor_copy(out=v_s[:], in_=tab_s[:].indirect(lists["offs"][:]))
-            w1_q = {(a, 0): quantize_weight(w1_raw[a, 0], "w1_%d0" % a) for a in range(2)}
-            v_w = [keep.tile([P, S], U32, name="v_w%d" % a, align_bytes=64) for a in range(2)]
-            nc.vector.tensor_copy(out=v_w[0][:], in_=tab_w[0][:].indirect(lists["offs"][:]))
+            w1_q = {(a, 0): quantize_weight(w1_raw[a, 0], "w1_%d0" % a, True) for a in range(2)}
+            v_both = keep.tile([P, 2, S], U32, name="v_both", tag="damp0", align_bytes=64)
+            v_w = [v_both[:, a, :] for a in range(2)]
+            nc.vector.tensor_copy(out=v_w[0], in_=tab_w[0][:].indirect(lists["offs"][:]))
             for half in range(2):
                 nc.vector.tensor_copy(
                     out=v_w[1][:, BANK * half : BANK * (half + 1)],
                     in_=tab_w[1][:].indirect(lists["offs"][:, 32 * half : 32 * (half + 1)]),
                 )
-            nc.vector.tensor_copy(
-                out=w2_s[:].rearrange("p (a t m) -> p a t m", a=2, t=PACK),
-                in_=w2_s_raw[:].rearrange("p (a m t) -> p a t m", a=2, t=PACK),
-            )
 
-            h_all = keep.tile([P, 2 * PACK, S], F32, name="h_all")
+            h_all = keep.tile([P, 2 * PACK - 1, S], F32, name="h_all")
             h_sb = {}
 
             def features(s):
                 b, t = divmod(s, PACK)
-                h = h_all[:, s, :]
+                if s < 2 * PACK - 1:
+                    h = h_all[:, s, :]
+                else:
+                    h_late = keep.tile([P, S], F32, name="h_late", tag="h_late", bufs=1, align_bytes=64)
+                    h = h_late[:]
                 for half in range(2):
                     cols = slice(BANK * half, BANK * (half + 1))
-                    acc = psum.tile([P, BANK], F32, name="acc", tag="ring")
+                    acc = psum.tile([P, BANK], F32, name="acc", tag="sums", bufs=6)
                     for a in range(2):
                         codes, scales = w1_q[a, b]
                         nc.tensor.matmul_mx(
@@ -165,14 +155,36 @@ def tile_list_airway_tree_step_kernel(
                 )
 
             damp = {}
+            gathered = {}
 
-            def damping(s):
+            def daughters(s):
                 b, t = divmod(s, PACK)
-                d = damp[b][:, t, :]
-                nc.vector.tensor_copy(out=d, in_=pages[t][:].indirect(lists["offs4"][:]))
-                nc.scalar.activation(out=d, in_=d, func=ACT.Ln, bias=LN_FLOOR)
-                nc.scalar.activation(out=d, in_=d, func=ACT.Sigmoid, scale=-2.0)
-                nc.scalar.activation(out=d, in_=d, func=ACT.Copy, scale=gz_sb[:, b, t : t + 1])
+                w = PAIRS // 2 if s == 2 * PACK - 1 else PAIRS
+                gathered[s] = [slice(m0, m0 + w) for m0 in range(0, PAIRS, w)]
+                for cols in gathered[s]:
+                    nc.vector.tensor_copy(
+                        out=damp[b][:, t, cols],
+                        in_=pages[t][:].indirect(lists["offs4"][:, cols.start // 16 : cols.stop // 16]),
+                    )
+
+            def damping(s, count, pieces):
+                b, t0 = divmod(s, PACK)
+                logs = keep.tile([P, count, PAIRS], F32, name="logs", tag="logs", bufs=1)
+                for t in range(t0, t0 + count):
+                    for cols in gathered[PACK * b + t]:
+                        nc.scalar.activation(
+                            out=logs[:, t - t0, cols], in_=damp[b][:, t, cols], func=ACT.Ln, bias=LN_FLOOR
+                        )
+                for m0, w in pieces:
+                    d = logs[:, :, m0 : m0 + w]
+                    nc.scalar.activation(out=d, in_=d, func=ACT.Sigmoid, scale=-2.0)
+                    for t in range(t0, t0 + count):
+                        nc.scalar.activation(
+                            out=damp[b][:, t, m0 : m0 + w],
+                            in_=logs[:, t - t0, m0 : m0 + w],
+                            func=ACT.Copy,
+                            scale=gz_sb[:, b, t : t + 1],
+                        )
 
             def parents(out, s, m0, w):
                 nc.vector.tensor_tensor(
@@ -203,20 +215,34 @@ def tile_list_airway_tree_step_kernel(
                 features(s)
             for a in range(2):
                 w1_raw[a, 1] = load_weight(w1, a, 1)
-            for s in range(1, PACK):
-                rest_sb[s] = load_rest(s)
-            for a in range(2):
-                w1_q[a, 1] = quantize_weight(w1_raw[a, 1], "w1_%d1" % a)
+            wgs_t.extend(load_wgs(t) for t in range(2, PACK))
+            nc.sync.dma_start(lists["offs4"][:], offs4)
+            gz_sb = keep.tile([P, 2, PACK], F32, name="gz_sb")
+            nc.sync.dma_start(out=gz_sb[:], in_=gz.rearrange("(b p t) -> p b t", b=2, t=PACK))
+            nc.sync.dma_start(lists["offs3"][:], offs3)
             w3_raw = [load_weight(w3, a, 0) for a in range(2)]
-            rest_sb[PACK] = load_rest(PACK)
+            rest_sb = {s: load_rest(s) for s in range(PACK + 1)}
+            for a in range(2):
+                w1_q[a, 1] = quantize_weight(w1_raw[a, 1], "w1_%d1" % a, True)
+            w2_w = keep.tile([P, 2 * 2 * N], U8, name="w2_w", align_bytes=64)
+            nc.sync.dma_start(
+                out=w2_w[:].bitcast(I32).rearrange("p (a c) -> p a c", a=2),
+                in_=w2_words.bitcast(I32).rearrange("a p c -> p a c"),
+            )
+            w2_s_dram = w2_scales.bitcast(I32)
+            for q in range(4):
+                nc.sync.dma_start(
+                    out=w2_s[32 * q : 32 * q + 4, :].bitcast(I32).rearrange("r (a c) -> r a c", a=2),
+                    in_=w2_s_dram[:, 4 * q : 4 * q + 4, :].rearrange("a r c -> r a c"),
+                )
             for s in range(PACK, 2 * PACK):
                 features(s)
-            w3_q = [quantize_weight(w3_raw[a], "w3_%d" % a) for a in range(2)]
+            w3_q = [quantize_weight(w3_raw[a], "w3_%d" % a, False) for a in range(2)]
         late = ctx.enter_context(tc.tile_pool(name="late", bufs=1))
 
-        damp[0] = keep.tile([P, PACK, PAIRS], F32, name="damp0")
+        damp[0] = keep.tile([P, PACK, PAIRS], F32, name="damp0", tag="damp0", align_bytes=64)
         damp[1] = keep.tile([P, PACK, PAIRS], F32, name="damp1")
-        summed0 = keep.tile([P, PACK, PAIRS], F32, name="summed0")
+        summed0 = keep.tile([P, PACK, PAIRS], F32, name="summed0", tag="summed0", align_bytes=64)
         for half in range(2):
             cols = slice(BANK * half, BANK * (half + 1))
             nc.vector.tensor_tensor(
@@ -225,47 +251,53 @@ def tile_list_airway_tree_step_kernel(
                 in1=wgs_t[0][:, cols],
                 op=ALU.mult,
             )
+        for s in range(1, PACK):
+            scatter(s)
         for s in range(PACK):
-            scatter(s + 1)
-            damping(s)
+            daughters(s)
+            if s % 2 == 1:
+                damping(s - 1, 2, WHOLE)
+
+        def first_parents(s):
             parents(summed0[:, s, :], s, 0, PAIRS)
-            if s > 0:
-                rest_sb[PACK + s] = load_rest(PACK + s)
+            if s < PACK - 1:
+                rest_sb[PACK + 1 + s] = load_rest(PACK + 1 + s)
 
+        first_parents(0)
+        first_parents(1)
+        scatter(PACK)
         scatter(PACK + 1)
-        damping(PACK)
+        daughters(PACK)
+        damping(PACK, 1, WHOLE)
+        first_parents(2)
         scatter(PACK + 2)
-        damping(PACK + 1)
-        damping(PACK + 2)
+        daughters(PACK + 1)
+        daughters(PACK + 2)
+        damping(PACK + 1, 2, WHOLE)
+        first_parents(3)
         scatter(PACK + 3)
-        damping(PACK + 3)
-        stages = [make_z(0, summed0[:, :, BANK * i : BANK * (i + 1)], BANK * i, BANK, staging()) for i in range(2)]
-        for i in range(2):
-            quantize_z(0, stages[i], BANK * i, BANK)
+        daughters(PACK + 3)
+        damping(PACK + 3, 1, ((0, 256), (256, 256), (512, 512)))
 
-        def pass_w3(acc_b, b, t, m0, start, stop):
+        def passes(acc_a, acc_b, b, m0):
             cols = slice(m0, m0 + P)
             nc.tensor.matmul_mx(
-                out=acc_b,
-                lhsT=w3_q[b][0][:, P * t : P * (t + 1)].bitcast(FP8X4),
-                lhsT_scale=w3_q[b][1][:, P * t : P * (t + 1)],
-                rhs=z_c[b][:, cols].bitcast(FP8X4),
-                rhs_scale=z_s[b][:, cols],
-                start=start,
-                stop=stop,
+                out=acc_b[:],
+                lhsT=z_c[b][:, cols].bitcast(FP8X4),
+                lhsT_scale=z_s[b][:, cols],
+                rhs=w3_q[b][0][:].bitcast(FP8X4),
+                rhs_scale=w3_q[b][1][:],
+                start=(b == 0),
+                stop=(b == 1),
             )
-
-        def pass_w2(acc_a, b, t, m0, start, stop):
-            cols = slice(m0, m0 + P)
-            c0 = N * b + P * t
             nc.tensor.matmul_mx(
-                out=acc_a,
-                lhsT=w2_w[:, 2 * c0 : 2 * (c0 + P)].bitcast(FP4X4),
-                lhsT_scale=w2_s[:, c0 : c0 + P],
-                rhs=z_c[b][:, cols].bitcast(FP8X4),
-                rhs_scale=z_s[b][:, cols],
-                start=start,
-                stop=stop,
+                out=acc_a[:],
+                lhsT=z_c[b][:, cols].bitcast(FP8X4),
+                lhsT_scale=z_s[b][:, cols],
+                rhs=w2_w[:, 2 * N * b : 2 * N * (b + 1)].bitcast(FP4X4),
+                rhs_scale=w2_s[:, N * b : N * (b + 1)],
+                start=(b == 0),
+                stop=(b == 1),
             )
 
         y_c = late.tile([P, PAIRS], U32, name="y_c", align_bytes=64)
@@ -274,73 +306,110 @@ def tile_list_airway_tree_step_kernel(
         out_words = out_1[0].rearrange("p m t -> p (m t)").bitcast(I32)
         out_scales = out_2[0].bitcast(I32)
 
-        def subtract(y, acc_a, acc_b):
-            gate = late.tile([P, BANK], F32, name="gate", tag="gate", bufs=3)
-            nc.scalar.activation(out=gate[:], in_=acc_b, func=ACT.Silu)
-            nc.vector.tensor_tensor(out=y, in0=acc_a, in1=gate[:], op=ALU.subtract)
-
-        def hand_out(y, m0, w, on_vector):
-            nc.sync.dma_start(out=out_rows[:, :, m0 : m0 + w], in_=y[:])
-            stage = late.tile([P, PACK * w], BF16, name="y_stage", tag="y_stage", bufs=3, align_bytes=64)
-            dst = stage[:, 0 : PACK * w].rearrange("p (c i t) -> p c t i", i=2, t=PACK)
-            src = y[:].rearrange("p t (c i) -> p c t i", i=2)
-            if on_vector:
-                nc.vector.tensor_copy(out=dst, in_=src)
-            else:
-                nc.scalar.copy(out=dst, in_=src)
-            nc.vector.quantize_mx(
-                out=y_c[:, m0 : m0 + w].bitcast(FP8X4), scales=y_s[:, m0 : m0 + w], in_=stage[:, 0 : PACK * w]
-            )
-            nc.sync.dma_start(out=out_words[:, m0 : m0 + w], in_=y_c[:, m0 : m0 + w].bitcast(I32))
-
         opened = {}
 
         def open_tile(m0):
-            acc_a = psum.tile([P, BANK], F32, name="acc", tag="ring")
-            acc_b = psum.tile([P, BANK], F32, name="acc", tag="ring")
-            for t in range(PACK):
-                cols = slice(P * t, P * (t + 1))
-                pass_w3(acc_b[:, cols], 0, t, m0, t == 0, False)
-                pass_w2(acc_a[:, cols], 0, t, m0, t == 0, False)
+            acc_b = psum.tile([P, BANK], F32, name="acc", tag="sums", bufs=6)
+            acc_a = psum.tile([P, BANK], F32, name="acc", tag="sums", bufs=6)
+            passes(acc_a, acc_b, 0, m0)
             opened[m0] = (acc_a, acc_b)
 
         def close_tile(m0):
+            passes(*opened[m0], 1, m0)
+
+        turned = {}
+
+        def turn_tile(m0):
             acc_a, acc_b = opened[m0]
-            for t in range(PACK):
-                pass_w3(acc_b[:, P * t : P * (t + 1)], 1, t, m0, False, t == PACK - 1)
-            for t in range(PACK):
-                pass_w2(acc_a[:, P * t : P * (t + 1)], 1, t, m0, False, t == PACK - 1)
+            gate = late.tile([P, PACK, P], F32, name="gate", tag="gate", bufs=2)
+            minus_a = late.tile([P, PACK, P], F32, name="minus_a", tag="minus_a", bufs=2)
+            nc.scalar.activation(out=gate[:], in_=acc_b[:].rearrange("p (m t) -> p t m", t=PACK), func=ACT.Silu)
+            dealt_a = acc_a[:].rearrange("p (m t) -> p t m", t=PACK)
+            if m0 == PAIRS - P:
+                nc.vector.tensor_scalar(out=minus_a[:], in0=dealt_a, scalar1=-1.0, scalar2=None, op0=ALU.mult)
+            else:
+                nc.scalar.activation(out=minus_a[:], in_=dealt_a, func=ACT.Copy, scale=-1.0)
+            per_bank = 2 if m0 == PAIRS - P else PACK
+            banks = [
+                psum.tile([P, per_bank * P], F32, name="minus_y", tag="minus_y", bufs=2)
+                for i in range(PACK // per_bank)
+            ]
+            for k, term in enumerate((gate, minus_a)):
+                for t in range(PACK):
+                    i, u = divmod(t, per_bank)
+                    nc.tensor.matmul(
+                        banks[i][:, P * u : P * (u + 1)],
+                        lhsT=term[:, t, :],
+                        rhs=ident[:],
+                        is_transpose=True,
+                        start=(k == 0 and u == 0),
+                        stop=(k == 1 and u == per_bank - 1),
+                    )
+            turned[m0] = banks
 
         def finish_tile(m0):
-            acc_a, acc_b = opened[m0]
-            y = late.tile([P, PACK, P], F32, name="y", tag="y", bufs=4)
-            subtract(y[:].rearrange("p t m -> p (t m)"), acc_a[:], acc_b[:])
-            hand_out(y, m0, P, m0 >= PAIRS - 2 * P)
-            if m0 + BANK < PAIRS:
-                open_tile(m0 + BANK)
+            banks = turned[m0]
+            stage = late.tile([P, PACK * P], BF16, name="y_stage", tag="y_stage", bufs=4, align_bytes=64)
+            y = late.tile([P, PACK, P], F32, name="y", tag="y", bufs=3)
+            if m0 == PAIRS - P:
+                nc.scalar.activation(
+                    out=y[:, 0:2, :].rearrange("p t m -> p (t m)"), in_=banks[0][:], func=ACT.Copy, scale=-1.0
+                )
+                nc.vector.tensor_scalar(
+                    out=y[:, 2:4, :].rearrange("p t m -> p (t m)"),
+                    in0=banks[1][:],
+                    scalar1=-1.0,
+                    scalar2=None,
+                    op0=ALU.mult,
+                )
+                nc.vector.tensor_copy(
+                    out=stage[:].rearrange("p (c i t) -> p c t i", i=2, t=PACK),
+                    in_=y[:].rearrange("p t (c i) -> p c t i", i=2),
+                )
+            else:
+                nc.scalar.activation(
+                    out=stage[:].rearrange("p (m t) -> p m t", t=PACK),
+                    in_=banks[0][:].rearrange("p (t m) -> p m t", t=PACK),
+                    func=ACT.Copy,
+                    scale=-1.0,
+                )
+                nc.scalar.activation(
+                    out=y[:].rearrange("p t m -> p (t m)"), in_=banks[0][:], func=ACT.Copy, scale=-1.0
+                )
+            nc.vector.quantize_mx(out=y_c[:, m0 : m0 + P].bitcast(FP8X4), scales=y_s[:, m0 : m0 + P], in_=stage[:])
+            nc.sync.dma_start(out=out_words[:, m0 : m0 + P], in_=y_c[:, m0 : m0 + P].bitcast(I32))
+            nc.sync.dma_start(out=out_rows[:, :, m0 : m0 + P], in_=y[:])
 
         def chunk_front(m0, w):
-            part = late.tile([P, PACK, w], F32, name="summed1", tag="summed1", bufs=2)
-            for t in range(PACK):
+            part = keep.tile([P, PACK, w], F32, name="summed1", tag="wgs3")
+            stage = keep.tile([P, 2, PACK * w], BF16, name="z_stage", tag="h_late", bufs=1, align_bytes=64)
+            parents(part[:, 0, :], PACK, m0, w)
+            make_z(0, summed0[:, :, m0 : m0 + w], m0, w, stage[:, 0, :])
+            parents(part[:, 1, :], PACK + 1, m0, w)
+            quantize_z(0, stage[:, 0, :], m0, w)
+            for t in range(2, PACK):
                 parents(part[:, t, :], PACK + t, m0, w)
-            return part
+            return part, stage
 
-        for m0 in range(0, BANK, P):
+        parts = [chunk_front(*CHUNKS[0])]
+        for m0 in range(0, 2 * P, P):
             open_tile(m0)
-        parts = [chunk_front(*CHUNKS[i]) for i in range(2)]
         for i, (m0, w) in enumerate(CHUNKS):
-            stage = late.tile([P, PACK * w], BF16, name="z_stage", tag="z_stage", bufs=2, align_bytes=64)
-            make_z(1, parts[i][:], m0, w, stage)
-            if i + 2 < len(CHUNKS):
-                parts.append(chunk_front(*CHUNKS[i + 2]))
-            quantize_z(1, stage, m0, w)
-            if i > 0:
-                before, width = CHUNKS[i - 1]
-                for m1 in range(before, before + width, P):
-                    finish_tile(m1)
+            part, stage = parts[i]
+            make_z(1, part[:], m0, w, stage[:, 1, :])
+            ahead = []
+            quantize_z(1, stage[:, 1, :], m0, w)
+            if i + 1 < len(CHUNKS):
+                parts.append(chunk_front(*CHUNKS[i + 1]))
+                ahead = list(range(m0 + w, m0 + w + CHUNKS[i + 1][1], P))
             for m1 in range(m0, m0 + w, P):
                 close_tile(m1)
-        finish_tile(CHUNKS[-1][0])
+                turn_tile(m1)
+                if m1 > 0:
+                    finish_tile(m1 - P)
+                if m1 + w in ahead:
+                    open_tile(m1 + w)
+        finish_tile(PAIRS - P)
         for q in range(4):
             queue = nc.sync if q % 2 == 0 else nc.scalar
             queue.dma_start(out=out_scales[4 * q : 4 * q + 4, :], in_=y_s[32 * q : 32 * q + 4, :].bitcast(I32))

@@ -61,18 +61,16 @@ def tile_list_airway_tree_step_kernel(
             def staging():
                 return keep.tile([P, PACK * KP], BF16, name="stage", tag="stage", bufs=3, align_bytes=64)
 
-            def quantize_weight(raw, name, dealt):
+            def round_weight(raw):
                 stage = staging()
-                if dealt:
-                    nc.scalar.copy(
-                        out=stage[:].rearrange("p (t m j) -> p m t j", t=PACK, j=PACK),
-                        in_=raw[:].rearrange("p j (m t) -> p m t j", t=PACK),
-                    )
-                else:
-                    nc.scalar.copy(
-                        out=stage[:].rearrange("p (c i j) -> p c j i", i=PACK, j=PACK),
-                        in_=raw[:].rearrange("p j (c i) -> p c j i", i=PACK),
-                    )
+                nc.scalar.copy(
+                    out=stage[:].rearrange("p (t m j) -> p m t j", t=PACK, j=PACK),
+                    in_=raw[:].rearrange("p j (m t) -> p m t j", t=PACK),
+                )
+                return stage
+
+            def quantize_weight(raw, name):
+                stage = round_weight(raw)
                 codes = keep.tile([P, KP], U32, name=name + "_c", align_bytes=64)
                 scales = keep.tile([P, KP], U8, name=name + "_s", align_bytes=64)
                 nc.vector.quantize_mx(out=codes[:].bitcast(FP8X4), scales=scales[:], in_=stage[:])
@@ -96,7 +94,7 @@ def tile_list_airway_tree_step_kernel(
             wgs_rows = wgs.rearrange("(i t) j -> t i j", t=PACK)
 
             def load_wgs(t):
-                tile = keep.tile([P, S], F32, name="wgs%d" % t, tag="wgs%d" % t)
+                tile = keep.tile([P, S], F32, name="wgs%d" % t, tag="wgs%d" % (t // 2), bufs=2)
                 for q in range(4):
                     nc.sync.dma_start(out=tile[32 * q : 32 * (q + 1), :], in_=wgs_rows[t])
                 return tile
@@ -112,7 +110,7 @@ def tile_list_airway_tree_step_kernel(
 
             v_s = keep.tile([P, S], U8, name="v_s", tag="summed0", align_bytes=64)
             nc.vector.tensor_copy(out=v_s[:], in_=tab_s[:].indirect(lists["offs"][:]))
-            w1_q = {(a, 0): quantize_weight(w1_raw[a, 0], "w1_%d0" % a, True) for a in range(2)}
+            w1_q = {(a, 0): quantize_weight(w1_raw[a, 0], "w1_%d0" % a) for a in range(2)}
             v_both = keep.tile([P, 2, S], U32, name="v_both", tag="damp0", align_bytes=64)
             v_w = [v_both[:, a, :] for a in range(2)]
             nc.vector.tensor_copy(out=v_w[0], in_=tab_w[0][:].indirect(lists["offs"][:]))
@@ -122,15 +120,15 @@ def tile_list_airway_tree_step_kernel(
                     in_=tab_w[1][:].indirect(lists["offs"][:, 32 * half : 32 * (half + 1)]),
                 )
 
-            h_all = keep.tile([P, 2 * PACK - 1, S], F32, name="h_all")
+            h_all = keep.tile([P, 2 * PACK - 2, S], F32, name="h_all")
             h_sb = {}
 
             def features(s):
                 b, t = divmod(s, PACK)
-                if s < 2 * PACK - 1:
+                if s < 2 * PACK - 2:
                     h = h_all[:, s, :]
                 else:
-                    h_late = keep.tile([P, S], F32, name="h_late", tag="h_late", bufs=1, align_bytes=64)
+                    h_late = keep.tile([P, S], F32, name="h_late", tag="h%d" % s, bufs=1, align_bytes=64)
                     h = h_late[:]
                 for half in range(2):
                     cols = slice(BANK * half, BANK * (half + 1))
@@ -223,7 +221,7 @@ def tile_list_airway_tree_step_kernel(
             w3_raw = [load_weight(w3, a, 0) for a in range(2)]
             rest_sb = {s: load_rest(s) for s in range(PACK + 1)}
             for a in range(2):
-                w1_q[a, 1] = quantize_weight(w1_raw[a, 1], "w1_%d1" % a, True)
+                w1_q[a, 1] = quantize_weight(w1_raw[a, 1], "w1_%d1" % a)
             w2_w = keep.tile([P, 2 * 2 * N], U8, name="w2_w", align_bytes=64)
             nc.sync.dma_start(
                 out=w2_w[:].bitcast(I32).rearrange("p (a c) -> p a c", a=2),
@@ -237,7 +235,7 @@ def tile_list_airway_tree_step_kernel(
                 )
             for s in range(PACK, 2 * PACK):
                 features(s)
-            w3_q = [quantize_weight(w3_raw[a], "w3_%d" % a, False) for a in range(2)]
+            w3_bf = [round_weight(w3_raw[a]) for a in range(2)]
         late = ctx.enter_context(tc.tile_pool(name="late", bufs=1))
 
         damp[0] = keep.tile([P, PACK, PAIRS], F32, name="damp0", tag="damp0", align_bytes=64)
@@ -278,6 +276,10 @@ def tile_list_airway_tree_step_kernel(
         scatter(PACK + 3)
         daughters(PACK + 3)
         damping(PACK + 3, 1, ((0, 256), (256, 256), (512, 512)))
+        w3_c = keep.tile([P, 2, KP], U32, name="w3_c", tag="h6", bufs=1, align_bytes=64)
+        w3_s = keep.tile([P, 2, KP], U8, name="w3_s", align_bytes=64)
+        for a in range(2):
+            nc.vector.quantize_mx(out=w3_c[:, a, :].bitcast(FP8X4), scales=w3_s[:, a, :], in_=w3_bf[a][:])
 
         def passes(acc_a, acc_b, b, m0):
             cols = slice(m0, m0 + P)
@@ -285,8 +287,8 @@ def tile_list_airway_tree_step_kernel(
                 out=acc_b[:],
                 lhsT=z_c[b][:, cols].bitcast(FP8X4),
                 lhsT_scale=z_s[b][:, cols],
-                rhs=w3_q[b][0][:].bitcast(FP8X4),
-                rhs_scale=w3_q[b][1][:],
+                rhs=w3_c[:, b, :].bitcast(FP8X4),
+                rhs_scale=w3_s[:, b, :],
                 start=(b == 0),
                 stop=(b == 1),
             )
@@ -323,12 +325,13 @@ def tile_list_airway_tree_step_kernel(
             acc_a, acc_b = opened[m0]
             gate = late.tile([P, PACK, P], F32, name="gate", tag="gate", bufs=2)
             minus_a = late.tile([P, PACK, P], F32, name="minus_a", tag="minus_a", bufs=2)
-            nc.scalar.activation(out=gate[:], in_=acc_b[:].rearrange("p (m t) -> p t m", t=PACK), func=ACT.Silu)
-            dealt_a = acc_a[:].rearrange("p (m t) -> p t m", t=PACK)
+            nc.scalar.activation(out=gate[:].rearrange("p t m -> p (t m)"), in_=acc_b[:], func=ACT.Silu)
+            src = acc_a[:].rearrange("p (m u e) -> p u m e", u=2, e=2)
+            dst = minus_a[:].rearrange("p (u e) m -> p u m e", e=2)
             if m0 == PAIRS - P:
-                nc.vector.tensor_scalar(out=minus_a[:], in0=dealt_a, scalar1=-1.0, scalar2=None, op0=ALU.mult)
+                nc.vector.tensor_scalar(out=dst, in0=src, scalar1=-1.0, scalar2=None, op0=ALU.mult)
             else:
-                nc.scalar.activation(out=minus_a[:], in_=dealt_a, func=ACT.Copy, scale=-1.0)
+                nc.scalar.activation(out=dst, in_=src, func=ACT.Copy, scale=-1.0)
             per_bank = 2 if m0 == PAIRS - P else PACK
             banks = [
                 psum.tile([P, per_bank * P], F32, name="minus_y", tag="minus_y", bufs=2)
@@ -368,8 +371,8 @@ def tile_list_airway_tree_step_kernel(
                 )
             else:
                 nc.scalar.activation(
-                    out=stage[:].rearrange("p (m t) -> p m t", t=PACK),
-                    in_=banks[0][:].rearrange("p (t m) -> p m t", t=PACK),
+                    out=stage[:].rearrange("p (c i t) -> p c t i", i=2, t=PACK),
+                    in_=banks[0][:].rearrange("p (t c i) -> p c t i", i=2, t=PACK),
                     func=ACT.Copy,
                     scale=-1.0,
                 )
@@ -380,27 +383,29 @@ def tile_list_airway_tree_step_kernel(
             nc.sync.dma_start(out=out_words[:, m0 : m0 + P], in_=y_c[:, m0 : m0 + P].bitcast(I32))
             nc.sync.dma_start(out=out_rows[:, :, m0 : m0 + P], in_=y[:])
 
-        def chunk_front(m0, w):
-            part = keep.tile([P, PACK, w], F32, name="summed1", tag="wgs3")
-            stage = keep.tile([P, 2, PACK * w], BF16, name="z_stage", tag="h_late", bufs=1, align_bytes=64)
-            parents(part[:, 0, :], PACK, m0, w)
-            make_z(0, summed0[:, :, m0 : m0 + w], m0, w, stage[:, 0, :])
-            parents(part[:, 1, :], PACK + 1, m0, w)
-            quantize_z(0, stage[:, 0, :], m0, w)
-            for t in range(2, PACK):
+        def late_parents(m0, w):
+            part = keep.tile([P, PACK, w], F32, name="summed1", tag="wgs1", bufs=2)
+            for t in range(PACK):
                 parents(part[:, t, :], PACK + t, m0, w)
-            return part, stage
+            return part
 
-        parts = [chunk_front(*CHUNKS[0])]
+        def first_rows(m0, w):
+            stage = keep.tile([P, 2, PACK * w], BF16, name="z_stage", tag="h7", bufs=1, align_bytes=64)
+            make_z(0, summed0[:, :, m0 : m0 + w], m0, w, stage[:, 0, :])
+            quantize_z(0, stage[:, 0, :], m0, w)
+            return stage
+
+        parts = [late_parents(*CHUNKS[0])]
+        stages = [first_rows(*CHUNKS[0])]
         for m0 in range(0, 2 * P, P):
             open_tile(m0)
         for i, (m0, w) in enumerate(CHUNKS):
-            part, stage = parts[i]
-            make_z(1, part[:], m0, w, stage[:, 1, :])
+            make_z(1, parts[i][:], m0, w, stages[i][:, 1, :])
             ahead = []
-            quantize_z(1, stage[:, 1, :], m0, w)
+            quantize_z(1, stages[i][:, 1, :], m0, w)
             if i + 1 < len(CHUNKS):
-                parts.append(chunk_front(*CHUNKS[i + 1]))
+                stages.append(first_rows(*CHUNKS[i + 1]))
+                parts.append(late_parents(*CHUNKS[i + 1]))
                 ahead = list(range(m0 + w, m0 + w + CHUNKS[i + 1][1], P))
             for m1 in range(m0, m0 + w, P):
                 close_tile(m1)

@@ -23,7 +23,7 @@ KP = P * PACK
 BANK = 512
 LN_FLOOR = 2.0 ** -60
 WHOLE = ((0, PAIRS),)
-CHUNKS = ((0, 256), (256, 256), (512, 256), (768, 128), (896, 128))
+CHUNKS = tuple((m0, P) for m0 in range(0, PAIRS, P))
 
 
 def tile_list_airway_tree_step_kernel(
@@ -197,9 +197,9 @@ def tile_list_airway_tree_step_kernel(
 
             def make_z(b, summed, m0, w, stage):
                 nc.vector.tensor_tensor(
-                    out=stage[:, 0 : PACK * w].rearrange("p (c i t) -> p c t i", i=2, t=PACK),
-                    in0=summed.rearrange("p t (c i) -> p c t i", i=2),
-                    in1=damp[b][:, :, m0 : m0 + w].rearrange("p t (c i) -> p c t i", i=2),
+                    out=stage[:, 0 : PACK * w].rearrange("p (c i t) -> p c t i", i=PACK, t=PACK),
+                    in0=summed.rearrange("p t (c i) -> p c t i", i=PACK),
+                    in1=damp[b][:, :, m0 : m0 + w].rearrange("p t (c i) -> p c t i", i=PACK),
                     op=ALU.mult,
                 )
                 return stage
@@ -275,7 +275,7 @@ def tile_list_airway_tree_step_kernel(
         first_parents(3)
         scatter(PACK + 3)
         daughters(PACK + 3)
-        damping(PACK + 3, 1, ((0, 256), (256, 256), (512, 512)))
+        damping(PACK + 3, 1, ((0, 128), (128, 384), (512, 512)))
         w3_c = keep.tile([P, 2, KP], U32, name="w3_c", tag="h6", bufs=1, align_bytes=64)
         w3_s = keep.tile([P, 2, KP], U8, name="w3_s", align_bytes=64)
         for a in range(2):
@@ -366,13 +366,13 @@ def tile_list_airway_tree_step_kernel(
                     op0=ALU.mult,
                 )
                 nc.vector.tensor_copy(
-                    out=stage[:].rearrange("p (c i t) -> p c t i", i=2, t=PACK),
-                    in_=y[:].rearrange("p t (c i) -> p c t i", i=2),
+                    out=stage[:].rearrange("p (c i t) -> p c t i", i=PACK, t=PACK),
+                    in_=y[:].rearrange("p t (c i) -> p c t i", i=PACK),
                 )
             else:
                 nc.scalar.activation(
-                    out=stage[:].rearrange("p (c i t) -> p c t i", i=2, t=PACK),
-                    in_=banks[0][:].rearrange("p (t c i) -> p c t i", i=2, t=PACK),
+                    out=stage[:].rearrange("p (c i t) -> p c t i", i=PACK, t=PACK),
+                    in_=banks[0][:].rearrange("p (t c i) -> p c t i", i=PACK, t=PACK),
                     func=ACT.Copy,
                     scale=-1.0,
                 )
@@ -397,8 +397,7 @@ def tile_list_airway_tree_step_kernel(
 
         parts = [late_parents(*CHUNKS[0])]
         stages = [first_rows(*CHUNKS[0])]
-        for m0 in range(0, 2 * P, P):
-            open_tile(m0)
+        open_tile(0)
         for i, (m0, w) in enumerate(CHUNKS):
             make_z(1, parts[i][:], m0, w, stages[i][:, 1, :])
             ahead = []

@@ -22,8 +22,9 @@ PACK = 4
 KP = P * PACK
 BANK = 512
 LN_FLOOR = 2.0 ** -60
-WHOLE = ((0, PAIRS),)
-CHUNKS = tuple((m0, P) for m0 in range(0, PAIRS, P))
+HALVES = ((0, 512), (512, 512))
+FIRST_PIECES = ((0, 256), (256, 256), (512, 512))
+PIECE = 128
 
 
 def tile_list_airway_tree_step_kernel(
@@ -64,8 +65,8 @@ def tile_list_airway_tree_step_kernel(
             def round_weight(raw):
                 stage = staging()
                 nc.scalar.copy(
-                    out=stage[:].rearrange("p (t m j) -> p m t j", t=PACK, j=PACK),
-                    in_=raw[:].rearrange("p j (m t) -> p m t j", t=PACK),
+                    out=stage[:].rearrange("p (t m j) -> p m j t", t=PACK, j=PACK),
+                    in_=raw[:].rearrange("p j (m t) -> p m j t", t=PACK),
                 )
                 return stage
 
@@ -114,10 +115,10 @@ def tile_list_airway_tree_step_kernel(
             v_both = keep.tile([P, 2, S], U32, name="v_both", tag="damp0", align_bytes=64)
             v_w = [v_both[:, a, :] for a in range(2)]
             nc.vector.tensor_copy(out=v_w[0], in_=tab_w[0][:].indirect(lists["offs"][:]))
-            for half in range(2):
+            for j0, w in FIRST_PIECES:
                 nc.vector.tensor_copy(
-                    out=v_w[1][:, BANK * half : BANK * (half + 1)],
-                    in_=tab_w[1][:].indirect(lists["offs"][:, 32 * half : 32 * (half + 1)]),
+                    out=v_w[1][:, j0 : j0 + w],
+                    in_=tab_w[1][:].indirect(lists["offs"][:, j0 // 16 : (j0 + w) // 16]),
                 )
 
             h_all = keep.tile([P, 2 * PACK - 2, S], F32, name="h_all")
@@ -130,9 +131,9 @@ def tile_list_airway_tree_step_kernel(
                 else:
                     h_late = keep.tile([P, S], F32, name="h_late", tag="h%d" % s, bufs=1, align_bytes=64)
                     h = h_late[:]
-                for half in range(2):
-                    cols = slice(BANK * half, BANK * (half + 1))
-                    acc = psum.tile([P, BANK], F32, name="acc", tag="sums", bufs=6)
+                for j0, w in FIRST_PIECES if s == 0 else HALVES:
+                    cols = slice(j0, j0 + w)
+                    acc = psum.tile([P, w], F32, name="acc", tag="sums", bufs=6)
                     for a in range(2):
                         codes, scales = w1_q[a, b]
                         nc.tensor.matmul_mx(
@@ -153,36 +154,37 @@ def tile_list_airway_tree_step_kernel(
                 )
 
             damp = {}
-            gathered = {}
 
-            def daughters(s):
+            def daughters(s, m0, w):
                 b, t = divmod(s, PACK)
-                w = PAIRS // 2 if s == 2 * PACK - 1 else PAIRS
-                gathered[s] = [slice(m0, m0 + w) for m0 in range(0, PAIRS, w)]
-                for cols in gathered[s]:
-                    nc.vector.tensor_copy(
-                        out=damp[b][:, t, cols],
-                        in_=pages[t][:].indirect(lists["offs4"][:, cols.start // 16 : cols.stop // 16]),
-                    )
+                nc.vector.tensor_copy(
+                    out=damp[b][:, t, m0 : m0 + w],
+                    in_=pages[t][:].indirect(lists["offs4"][:, m0 // 16 : (m0 + w) // 16]),
+                )
 
-            def damping(s, count, pieces):
-                b, t0 = divmod(s, PACK)
-                logs = keep.tile([P, count, PAIRS], F32, name="logs", tag="logs", bufs=1)
-                for t in range(t0, t0 + count):
-                    for cols in gathered[PACK * b + t]:
-                        nc.scalar.activation(
-                            out=logs[:, t - t0, cols], in_=damp[b][:, t, cols], func=ACT.Ln, bias=LN_FLOOR
-                        )
-                for m0, w in pieces:
-                    d = logs[:, :, m0 : m0 + w]
-                    nc.scalar.activation(out=d, in_=d, func=ACT.Sigmoid, scale=-2.0)
-                    for t in range(t0, t0 + count):
-                        nc.scalar.activation(
-                            out=damp[b][:, t, m0 : m0 + w],
-                            in_=logs[:, t - t0, m0 : m0 + w],
-                            func=ACT.Copy,
-                            scale=gz_sb[:, b, t : t + 1],
-                        )
+            def logarithm(logs, s, m0, w):
+                b, t = divmod(s, PACK)
+                nc.scalar.activation(out=logs, in_=damp[b][:, t, m0 : m0 + w], func=ACT.Ln, bias=LN_FLOOR)
+
+            def sigmoid(logs):
+                nc.scalar.activation(out=logs, in_=logs, func=ACT.Sigmoid, scale=-2.0)
+
+            def times_gz(logs, s, m0, w):
+                b, t = divmod(s, PACK)
+                nc.scalar.activation(
+                    out=damp[b][:, t, m0 : m0 + w], in_=logs, func=ACT.Copy, scale=gz_sb[:, b, t : t + 1]
+                )
+
+            def scratch():
+                return keep.tile([P, 2 * PAIRS], F32, name="logs", tag="logs")
+
+            def damp_two(s):
+                logs = scratch()
+                for i in range(2):
+                    logarithm(logs[:, PAIRS * i : PAIRS * (i + 1)], s + i, 0, PAIRS)
+                sigmoid(logs[:])
+                for i in range(2):
+                    times_gz(logs[:, PAIRS * i : PAIRS * (i + 1)], s + i, 0, PAIRS)
 
             def parents(out, s, m0, w):
                 nc.vector.tensor_tensor(
@@ -252,9 +254,9 @@ def tile_list_airway_tree_step_kernel(
         for s in range(1, PACK):
             scatter(s)
         for s in range(PACK):
-            daughters(s)
+            daughters(s, 0, PAIRS)
             if s % 2 == 1:
-                damping(s - 1, 2, WHOLE)
+                damp_two(s - 1)
 
         def first_parents(s):
             parents(summed0[:, s, :], s, 0, PAIRS)
@@ -263,19 +265,30 @@ def tile_list_airway_tree_step_kernel(
 
         first_parents(0)
         first_parents(1)
-        scatter(PACK)
-        scatter(PACK + 1)
-        daughters(PACK)
-        damping(PACK, 1, WHOLE)
+        scatter(4)
+        scatter(5)
+        daughters(4, 0, PAIRS)
         first_parents(2)
-        scatter(PACK + 2)
-        daughters(PACK + 1)
-        daughters(PACK + 2)
-        damping(PACK + 1, 2, WHOLE)
+        daughters(5, 0, PAIRS)
+        damp_two(4)
+        scatter(6)
         first_parents(3)
-        scatter(PACK + 3)
-        daughters(PACK + 3)
-        damping(PACK + 3, 1, ((0, 128), (128, 384), (512, 512)))
+        daughters(6, 0, PAIRS)
+        logs = scratch()
+        most = PAIRS - P
+        logarithm(logs[:, 0:most], 6, 0, most)
+        sigmoid(logs[:, 0:most])
+        times_gz(logs[:, 0:most], 6, 0, most)
+        logarithm(logs[:, 0:P], 6, most, P)
+        scatter(7)
+        for m0, w in HALVES:
+            daughters(7, m0, w)
+            logarithm(logs[:, P + m0 : P + m0 + w], 7, m0, w)
+        for m0, w in ((0, 128), (128, 384), (512, 512)):
+            sigmoid(logs[:, P + m0 : P + m0 + w])
+            times_gz(logs[:, P + m0 : P + m0 + w], 7, m0, w)
+        sigmoid(logs[:, 0:P])
+        times_gz(logs[:, 0:P], 6, most, P)
         w3_c = keep.tile([P, 2, KP], U32, name="w3_c", tag="h6", bufs=1, align_bytes=64)
         w3_s = keep.tile([P, 2, KP], U8, name="w3_s", align_bytes=64)
         for a in range(2):
@@ -333,8 +346,9 @@ def tile_list_airway_tree_step_kernel(
             else:
                 nc.scalar.activation(out=dst, in_=src, func=ACT.Copy, scale=-1.0)
             per_bank = 2 if m0 == PAIRS - P else PACK
+            tag, bufs = ("sums", 6) if m0 == PAIRS - P else ("minus_y", 2)
             banks = [
-                psum.tile([P, per_bank * P], F32, name="minus_y", tag="minus_y", bufs=2)
+                psum.tile([P, per_bank * P], F32, name="minus_y", tag=tag, bufs=bufs)
                 for i in range(PACK // per_bank)
             ]
             for k, term in enumerate((gate, minus_a)):
@@ -395,24 +409,23 @@ def tile_list_airway_tree_step_kernel(
             quantize_z(0, stage[:, 0, :], m0, w)
             return stage
 
-        parts = [late_parents(*CHUNKS[0])]
-        stages = [first_rows(*CHUNKS[0])]
+        parts = [late_parents(0, PIECE)]
+        stage = first_rows(0, P)
         open_tile(0)
-        for i, (m0, w) in enumerate(CHUNKS):
-            make_z(1, parts[i][:], m0, w, stages[i][:, 1, :])
-            ahead = []
-            quantize_z(1, stages[i][:, 1, :], m0, w)
-            if i + 1 < len(CHUNKS):
-                stages.append(first_rows(*CHUNKS[i + 1]))
-                parts.append(late_parents(*CHUNKS[i + 1]))
-                ahead = list(range(m0 + w, m0 + w + CHUNKS[i + 1][1], P))
-            for m1 in range(m0, m0 + w, P):
-                close_tile(m1)
-                turn_tile(m1)
-                if m1 > 0:
-                    finish_tile(m1 - P)
-                if m1 + w in ahead:
-                    open_tile(m1 + w)
+        for m0 in range(0, PAIRS, P):
+            i, c0 = divmod(m0, PIECE)
+            make_z(1, parts[i][:, :, c0 : c0 + P], m0, P, stage[:, 1, :])
+            quantize_z(1, stage[:, 1, :], m0, P)
+            if m0 + P < PAIRS:
+                stage = first_rows(m0 + P, P)
+            if c0 == 0 and m0 + PIECE < PAIRS:
+                parts.append(late_parents(m0 + PIECE, PIECE))
+            close_tile(m0)
+            turn_tile(m0)
+            if m0 > 0:
+                finish_tile(m0 - P)
+            if m0 + P < PAIRS:
+                open_tile(m0 + P)
         finish_tile(PAIRS - P)
         for q in range(4):
             queue = nc.sync if q % 2 == 0 else nc.scalar

@@ -21,10 +21,31 @@ P = 128
 PACK = 4
 KP = P * PACK
 BANK = 512
+KB = 1024
 LN_FLOOR = 2.0 ** -60
 HALVES = ((0, 512), (512, 512))
 FIRST_PIECES = ((0, 256), (256, 256), (512, 512))
-PIECE = 128
+
+PAGE_AT = (0, 8, 16, 28)
+TAB_AT = (16, 28)
+STAGE_B_AT = (22, 34)
+SUM_AT = (24, 36, 138, 142)
+H_AT = 40
+RAW_A_AT = 72
+RAW_W3_AT = 88
+SUMS0_AT = 104
+STAGE_S0_AT = 120
+DAUGHTER_AT = (122, 126, 130, 134)
+V_AT = 146
+V_S_AT = 154
+TAB_S_AT = 155
+W1_Q_AT = 157
+STAGE_W3_AT = 167
+WGS_AT = 175
+REST_AT = 179
+Z_AT = 211
+SMALL_AT = 221
+Y_Q_AT = 227
 
 
 def tile_list_airway_tree_step_kernel(
@@ -33,246 +54,285 @@ def tile_list_airway_tree_step_kernel(
 ):
     nc = tc.nc
     with ExitStack() as ctx:
-        keep = ctx.enter_context(tc.tile_pool(name="keep", bufs=1))
+        held = ctx.enter_context(tc.tile_pool(name="held", bufs=1))
+        pool = ctx.enter_context(tc.tile_pool(name="pool", bufs=1))
         psum = ctx.enter_context(tc.psum_pool(name="psum", bufs=1))
+
+        def place(name, shape, dtype, kib, bufs=1):
+            return pool.tile(shape, dtype, name=name, tag=name, bufs=bufs, align_bytes=64, offset=int(kib * KB))
 
         lists = {}
         for name in ("offs", "offs2", "offs3", "offs4"):
-            lists[name] = keep.tile([P, S // 16], U16, name=name)
+            lists[name] = held.tile([P, S // 16], U16, name=name)
 
-        with tc.tile_pool(name="early", bufs=1) as early:
-            tab_s = early.tile([P, T], U8, name="tab_s")
-            w2_s = keep.tile([P, 2 * N], U8, name="w2_s", align_bytes=64)
-            ident = keep.tile([P, P], F32, name="ident")
-            nc.gpsimd.memset(tab_s[:].bitcast(I32), 0)
-            nc.gpsimd.memset(w2_s[:].bitcast(I32), 0)
-            make_identity(nc, ident[:])
-            pages = [keep.tile([P, T2], F32, name="page%d" % i) for i in range(PACK)]
-            for page in pages:
-                nc.vector.memset(page[:].bitcast(I32), 0)
+        def entries(name, j0, w):
+            return lists[name][:, j0 // 16 : (j0 + w) // 16]
 
-            def load_weight(w, a, b):
-                raw = early.tile([P, PACK, KP], F32, name="w_raw", tag="w_raw", bufs=4)
-                nc.sync.dma_start(
-                    out=raw[:],
-                    in_=w[KP * a : KP * (a + 1), KP * b : KP * (b + 1)].rearrange("(p j) c -> p j c", j=PACK),
-                )
-                return raw
+        tab_s = place("tab_s", [P, T], U8, TAB_S_AT)
+        w2_s = place("w2_s", [P, 2 * N], U8, SMALL_AT + 3)
+        ident = place("ident", [P, P], F32, SMALL_AT + 4)
+        nc.gpsimd.memset(tab_s[:].bitcast(I32), 0)
+        nc.gpsimd.memset(w2_s[:].bitcast(I32), 0)
+        make_identity(nc, ident[:])
+        pages = [None] * PACK
+        for i in range(2):
+            pages[i] = place("page%d" % i, [P, T2], F32, PAGE_AT[i])
+            nc.vector.memset(pages[i][:].bitcast(I32), 0)
 
-            def staging():
-                return keep.tile([P, PACK * KP], BF16, name="stage", tag="stage", bufs=3, align_bytes=64)
-
-            def round_weight(raw):
-                stage = staging()
-                nc.scalar.copy(
-                    out=stage[:].rearrange("p (t m j) -> p m j t", t=PACK, j=PACK),
-                    in_=raw[:].rearrange("p j (m t) -> p m j t", t=PACK),
-                )
-                return stage
-
-            def quantize_weight(raw, name):
-                stage = round_weight(raw)
-                codes = keep.tile([P, KP], U32, name=name + "_c", align_bytes=64)
-                scales = keep.tile([P, KP], U8, name=name + "_s", align_bytes=64)
-                nc.vector.quantize_mx(out=codes[:].bitcast(FP8X4), scales=scales[:], in_=stage[:])
-                return codes, scales
-
-            def load_table(a):
-                tw = early.tile([P, T], U32, name="tab_w", tag="w_raw", bufs=4)
-                nc.sync.dma_start(out=tw[:].bitcast(I32), in_=tab_words[a].rearrange("p t i -> p (t i)").bitcast(I32))
-                return tw
-
-            nc.sync.dma_start(lists["offs"][:], offs)
-            tab_s_dram = tab_scales.bitcast(I32)
-            for q in range(4):
-                nc.sync.dma_start(
-                    out=tab_s[32 * q : 32 * q + 8, :].bitcast(I32),
-                    in_=tab_s_dram[:, 4 * q : 4 * q + 4, :],
-                )
-            w1_raw = {(a, 0): load_weight(w1, a, 0) for a in range(2)}
-            tab_w = [load_table(a) for a in range(2)]
-            nc.sync.dma_start(lists["offs2"][:], offs2)
-            wgs_rows = wgs.rearrange("(i t) j -> t i j", t=PACK)
-
-            def load_wgs(t):
-                tile = keep.tile([P, S], F32, name="wgs%d" % t, tag="wgs%d" % (t // 2), bufs=2)
-                for q in range(4):
-                    nc.sync.dma_start(out=tile[32 * q : 32 * (q + 1), :], in_=wgs_rows[t])
-                return tile
-
-            rest_rows = rest.rearrange("(b p t) m -> b t p m", b=2, t=PACK)
-
-            def load_rest(s):
-                tile = keep.tile([P, PAIRS], F32, name="rest_sb", tag="rest_sb", bufs=5)
-                nc.sync.dma_start(out=tile[:], in_=rest_rows[s // PACK, s % PACK])
-                return tile
-
-            wgs_t = [load_wgs(t) for t in range(2)]
-
-            v_s = keep.tile([P, S], U8, name="v_s", tag="summed0", align_bytes=64)
-            nc.vector.tensor_copy(out=v_s[:], in_=tab_s[:].indirect(lists["offs"][:]))
-            w1_q = {(a, 0): quantize_weight(w1_raw[a, 0], "w1_%d0" % a) for a in range(2)}
-            v_both = keep.tile([P, 2, S], U32, name="v_both", tag="damp0", align_bytes=64)
-            v_w = [v_both[:, a, :] for a in range(2)]
-            nc.vector.tensor_copy(out=v_w[0], in_=tab_w[0][:].indirect(lists["offs"][:]))
-            for j0, w in FIRST_PIECES:
-                nc.vector.tensor_copy(
-                    out=v_w[1][:, j0 : j0 + w],
-                    in_=tab_w[1][:].indirect(lists["offs"][:, j0 // 16 : (j0 + w) // 16]),
-                )
-
-            h_all = keep.tile([P, 2 * PACK - 2, S], F32, name="h_all")
-            h_sb = {}
-
-            def features(s):
-                b, t = divmod(s, PACK)
-                if s < 2 * PACK - 2:
-                    h = h_all[:, s, :]
-                else:
-                    h_late = keep.tile([P, S], F32, name="h_late", tag="h%d" % s, bufs=1, align_bytes=64)
-                    h = h_late[:]
-                for j0, w in FIRST_PIECES if s == 0 else HALVES:
-                    cols = slice(j0, j0 + w)
-                    acc = psum.tile([P, w], F32, name="acc", tag="sums", bufs=6)
-                    for a in range(2):
-                        codes, scales = w1_q[a, b]
-                        nc.tensor.matmul_mx(
-                            out=acc[:],
-                            lhsT=codes[:, P * t : P * (t + 1)].bitcast(FP8X4),
-                            lhsT_scale=scales[:, P * t : P * (t + 1)],
-                            rhs=v_w[a][:, cols].bitcast(FP8X4),
-                            rhs_scale=v_s[4 * a : P, cols],
-                            start=(a == 0),
-                            stop=(a == 1),
-                        )
-                    nc.scalar.activation(out=h[:, cols], in_=acc[:], func=ACT.Exp)
-                h_sb[s] = h
-
-            def scatter(s):
-                nc.vector.tensor_tensor(
-                    out=pages[s % PACK][:].indirect(lists["offs2"][:]), in0=h_sb[s], in1=wgs_t[s % PACK][:], op=ALU.mult
-                )
-
-            damp = {}
-
-            def daughters(s, m0, w):
-                b, t = divmod(s, PACK)
-                nc.vector.tensor_copy(
-                    out=damp[b][:, t, m0 : m0 + w],
-                    in_=pages[t][:].indirect(lists["offs4"][:, m0 // 16 : (m0 + w) // 16]),
-                )
-
-            def logarithm(logs, s, m0, w):
-                b, t = divmod(s, PACK)
-                nc.scalar.activation(out=logs, in_=damp[b][:, t, m0 : m0 + w], func=ACT.Ln, bias=LN_FLOOR)
-
-            def sigmoid(logs):
-                nc.scalar.activation(out=logs, in_=logs, func=ACT.Sigmoid, scale=-2.0)
-
-            def times_gz(logs, s, m0, w):
-                b, t = divmod(s, PACK)
-                nc.scalar.activation(
-                    out=damp[b][:, t, m0 : m0 + w], in_=logs, func=ACT.Copy, scale=gz_sb[:, b, t : t + 1]
-                )
-
-            def scratch():
-                return keep.tile([P, 2 * PAIRS], F32, name="logs", tag="logs")
-
-            def damp_two(s):
-                logs = scratch()
-                for i in range(2):
-                    logarithm(logs[:, PAIRS * i : PAIRS * (i + 1)], s + i, 0, PAIRS)
-                sigmoid(logs[:])
-                for i in range(2):
-                    times_gz(logs[:, PAIRS * i : PAIRS * (i + 1)], s + i, 0, PAIRS)
-
-            def parents(out, s, m0, w):
-                nc.vector.tensor_tensor(
-                    out=out,
-                    in0=pages[s % PACK][:].indirect(lists["offs3"][:, m0 // 16 : (m0 + w) // 16]),
-                    in1=rest_sb[s][:, m0 : m0 + w],
-                    op=ALU.add,
-                )
-
-            z_c = [keep.tile([P, PAIRS], U32, name="z_c%d" % b, align_bytes=64) for b in range(2)]
-            z_s = [keep.tile([P, PAIRS], U8, name="z_s%d" % b, align_bytes=64) for b in range(2)]
-
-            def make_z(b, summed, m0, w, stage):
-                nc.vector.tensor_tensor(
-                    out=stage[:, 0 : PACK * w].rearrange("p (c i t) -> p c t i", i=PACK, t=PACK),
-                    in0=summed.rearrange("p t (c i) -> p c t i", i=PACK),
-                    in1=damp[b][:, :, m0 : m0 + w].rearrange("p t (c i) -> p c t i", i=PACK),
-                    op=ALU.mult,
-                )
-                return stage
-
-            def quantize_z(b, stage, m0, w):
-                nc.vector.quantize_mx(
-                    out=z_c[b][:, m0 : m0 + w].bitcast(FP8X4), scales=z_s[b][:, m0 : m0 + w], in_=stage[:, 0 : PACK * w]
-                )
-
-            for s in range(PACK):
-                features(s)
-            for a in range(2):
-                w1_raw[a, 1] = load_weight(w1, a, 1)
-            wgs_t.extend(load_wgs(t) for t in range(2, PACK))
-            nc.sync.dma_start(lists["offs4"][:], offs4)
-            gz_sb = keep.tile([P, 2, PACK], F32, name="gz_sb")
-            nc.sync.dma_start(out=gz_sb[:], in_=gz.rearrange("(b p t) -> p b t", b=2, t=PACK))
-            nc.sync.dma_start(lists["offs3"][:], offs3)
-            w3_raw = [load_weight(w3, a, 0) for a in range(2)]
-            rest_sb = {s: load_rest(s) for s in range(PACK + 1)}
-            for a in range(2):
-                w1_q[a, 1] = quantize_weight(w1_raw[a, 1], "w1_%d1" % a)
-            w2_w = keep.tile([P, 2 * 2 * N], U8, name="w2_w", align_bytes=64)
+        def load_weight(w, a, c0, width, name, kib):
+            raw = place(name, [P, PACK, width], F32, kib)
             nc.sync.dma_start(
-                out=w2_w[:].bitcast(I32).rearrange("p (a c) -> p a c", a=2),
-                in_=w2_words.bitcast(I32).rearrange("a p c -> p a c"),
+                out=raw[:],
+                in_=w[KP * a : KP * (a + 1), c0 : c0 + width].rearrange("(p j) c -> p j c", j=PACK),
             )
-            w2_s_dram = w2_scales.bitcast(I32)
-            for q in range(4):
-                nc.sync.dma_start(
-                    out=w2_s[32 * q : 32 * q + 4, :].bitcast(I32).rearrange("r (a c) -> r a c", a=2),
-                    in_=w2_s_dram[:, 4 * q : 4 * q + 4, :].rearrange("a r c -> r a c"),
+            return raw
+
+        def round_plain(raw, stage):
+            nc.scalar.copy(
+                out=stage.rearrange("p (c i j) -> p c j i", i=PACK, j=PACK),
+                in_=raw[:].rearrange("p j (c i) -> p c j i", i=PACK),
+            )
+
+        def round_dealt(raw, stage):
+            nc.scalar.copy(
+                out=stage.rearrange("p (t m j) -> p m j t", t=PACK, j=PACK),
+                in_=raw[:].rearrange("p j (m t) -> p m j t", t=PACK),
+            )
+
+        def quantize(stage, words, name, kib):
+            codes = place(name + "_c", [P, words], U32, kib)
+            scales = place(name + "_s", [P, words], U8, kib + words * 4 / KB)
+            nc.vector.quantize_mx(out=codes[:].bitcast(FP8X4), scales=scales[:], in_=stage)
+            return codes, scales
+
+        def load_table(a):
+            tw = place("tab_w%d" % a, [P, T], U32, TAB_AT[a])
+            nc.sync.dma_start(out=tw[:].bitcast(I32), in_=tab_words[a].rearrange("p t i -> p (t i)").bitcast(I32))
+            return tw
+
+        nc.sync.dma_start(lists["offs"][:], offs)
+        tab_s_dram = tab_scales.bitcast(I32)
+        for q in range(4):
+            nc.scalar.dma_start(
+                out=tab_s[32 * q : 32 * q + 8, :].bitcast(I32),
+                in_=tab_s_dram[:, 4 * q : 4 * q + 4, :],
+            )
+        tab_w = [load_table(0)]
+        raw_s0 = [load_weight(w1, a, 0, P, "raw_s0_%d" % a, RAW_A_AT + 2 * a) for a in range(2)]
+        tab_w.append(load_table(1))
+        nc.sync.dma_start(lists["offs2"][:], offs2)
+        wgs_plain = place("wgs_plain", [P, S], F32, WGS_AT)
+        nc.sync.dma_start(out=wgs_plain[:], in_=wgs)
+        raw_s1 = [load_weight(w1, a, P, P, "raw_s1_%d" % a, RAW_A_AT + 4 + 2 * a) for a in range(2)]
+        raw_s23 = [load_weight(w1, a, 2 * P, 2 * P, "raw_s23_%d" % a, RAW_A_AT + 8 + 4 * a) for a in range(2)]
+        raw_b = [load_weight(w1, a, KP, KP, "raw_b_%d" % a, H_AT + 16 - 8 * a) for a in range(2)]
+        nc.sync.dma_start(lists["offs4"][:], offs4)
+        nc.sync.dma_start(lists["offs3"][:], offs3)
+        gz_sb = [place("gz_sb%d" % b, [P, PACK], F32, SMALL_AT + 4.5 + b / 16) for b in range(2)]
+        with nc.allow_non_contiguous_dma(reason="one factor a partition"):
+            nc.sync.dma_start(out=gz_sb[0][:], in_=gz[0:KP].rearrange("(s p) -> p s", p=P))
+        nc.sync.dma_start(out=gz_sb[1][:], in_=gz[KP : 2 * KP].rearrange("(p t) -> p t", t=PACK))
+
+        rest_dealt = rest[KP : 2 * KP, :].rearrange("(p t) m -> t p m", t=PACK)
+        rest_sb = {}
+
+        def load_rest(s):
+            rest_sb[s] = place("rest%d" % s, [P, PAIRS], F32, REST_AT + 4 * s)
+            rows = rest[P * s : P * (s + 1), :] if s < PACK else rest_dealt[s - PACK]
+            nc.sync.dma_start(out=rest_sb[s][:], in_=rows)
+
+        v_s = place("v_s", [P, S], U8, V_S_AT)
+        nc.vector.tensor_copy(out=v_s[:], in_=tab_s[:].indirect(lists["offs"][:]))
+        v_w = [place("v_w%d" % a, [P, S], U32, V_AT + 4 * a) for a in range(2)]
+        nc.vector.tensor_copy(out=v_w[0][:], in_=tab_w[0][:].indirect(lists["offs"][:]))
+
+        w1_q = {}
+
+        def plain_weights(raws, first, count, name, stage_kib, kib):
+            width = P * count
+            stage = place("stage_" + name, [P, 2 * PACK * width], BF16, stage_kib)
+            for a in range(2):
+                round_plain(raws[a], stage[:, PACK * width * a : PACK * width * (a + 1)])
+            codes, scales = quantize(stage[:], 2 * width, "w1_" + name, kib)
+            for a in range(2):
+                for i in range(count):
+                    cols = slice(width * a + P * i, width * a + P * (i + 1))
+                    w1_q[a, first + i] = (codes[:, cols], scales[:, cols])
+
+        plain_weights(raw_s0, 0, 1, "s0", STAGE_S0_AT, W1_Q_AT)
+        for j0, w in ((0, 256), (256, 768)):
+            nc.vector.tensor_copy(out=v_w[1][:, j0 : j0 + w], in_=tab_w[1][:].indirect(entries("offs", j0, w)))
+
+        h_sb = {}
+
+        def features(s, j0, w):
+            cols = slice(j0, j0 + w)
+            acc = psum.tile([P, w], F32, name="acc", tag="sums", bufs=6)
+            for a in range(2):
+                codes, scales = w1_q[a, s]
+                nc.tensor.matmul_mx(
+                    out=acc[:],
+                    lhsT=codes.bitcast(FP8X4),
+                    lhsT_scale=scales,
+                    rhs=v_w[a][:, cols].bitcast(FP8X4),
+                    rhs_scale=v_s[4 * a : P, cols],
+                    start=(a == 0),
+                    stop=(a == 1),
                 )
-            for s in range(PACK, 2 * PACK):
-                features(s)
-            w3_bf = [round_weight(w3_raw[a]) for a in range(2)]
-        late = ctx.enter_context(tc.tile_pool(name="late", bufs=1))
+            nc.scalar.activation(out=h_sb[s, j0], in_=acc[:], func=ACT.Exp)
 
-        damp[0] = keep.tile([P, PACK, PAIRS], F32, name="damp0", tag="damp0", align_bytes=64)
-        damp[1] = keep.tile([P, PACK, PAIRS], F32, name="damp1")
-        summed0 = keep.tile([P, PACK, PAIRS], F32, name="summed0", tag="summed0", align_bytes=64)
-        for half in range(2):
-            cols = slice(BANK * half, BANK * (half + 1))
+        def whole_features(s):
+            h = place("h%d" % s, [P, S], F32, H_AT + 4 * s)
+            for j0, w in HALVES:
+                h_sb[s, j0] = h[:, j0 : j0 + w]
+                features(s, j0, w)
+            h_sb[s] = h
+
+        def page_of(s):
+            return pages[(0, 1, 0, 1, 2, 3, 0, 1)[s]]
+
+        def scatter_first(j0, w):
             nc.vector.tensor_tensor(
-                out=pages[0][:].indirect(lists["offs2"][:, 32 * half : 32 * (half + 1)]),
-                in0=h_sb[0][:, cols],
-                in1=wgs_t[0][:, cols],
-                op=ALU.mult,
+                out=pages[0][:].indirect(entries("offs2", j0, w)),
+                in0=h_sb[0, j0], in1=wgs_plain[:, j0 : j0 + w], op=ALU.mult,
             )
-        for s in range(1, PACK):
-            scatter(s)
-        for s in range(PACK):
+
+        def scatter(s):
+            factor = wgs_plain if s < PACK else wgs_t[s - PACK]
+            nc.vector.tensor_tensor(
+                out=page_of(s)[:].indirect(lists["offs2"][:]), in0=h_sb[s][:], in1=factor[:], op=ALU.mult
+            )
+
+        def first_features(j0, w):
+            piece = place("h0_%d" % j0, [P, w], F32, H_AT + j0 * 4 / KB)
+            h_sb[0, j0] = piece[:]
+            features(0, j0, w)
+
+        for j0, w in FIRST_PIECES[0:2]:
+            first_features(j0, w)
+        scatter_first(*FIRST_PIECES[0])
+        plain_weights(raw_s1, 1, 1, "s1", H_AT + 2, W1_Q_AT + 1.25)
+        scatter_first(*FIRST_PIECES[1])
+        first_features(*FIRST_PIECES[2])
+        scatter_first(*FIRST_PIECES[2])
+        whole_features(1)
+        scatter(1)
+        plain_weights(raw_s23, 2, 2, "s23", DAUGHTER_AT[0], W1_Q_AT + 2.5)
+
+        load_rest(0)
+        load_rest(1)
+        wgs_rows = wgs.rearrange("(i t) j -> t i j", t=PACK)
+        wgs_t = {}
+
+        def load_wgs(t):
+            wgs_t[t] = place("wgs%d" % t, [P, S], F32, RAW_A_AT + 4 * t)
+            for q in (0, 2, 1, 3):
+                nc.sync.dma_start(out=wgs_t[t][32 * q : 32 * (q + 1), :], in_=wgs_rows[t])
+
+        load_wgs(0)
+        load_wgs(1)
+        load_rest(2)
+        load_rest(3)
+        load_wgs(2)
+        load_wgs(3)
+        w3_raw = [load_weight(w3, a, 0, N, "raw_w3_%d" % a, RAW_W3_AT + 8 * a) for a in range(2)]
+        w2_w = place("w2_w", [P, 2 * 2 * N], U8, SMALL_AT + 1)
+        nc.sync.dma_start(
+            out=w2_w[:].bitcast(I32).rearrange("p (a c) -> p a c", a=2),
+            in_=w2_words.bitcast(I32).rearrange("a p c -> p a c"),
+        )
+        w2_s_dram = w2_scales.bitcast(I32)
+        for q in range(4):
+            nc.sync.dma_start(
+                out=w2_s[32 * q : 32 * q + 4, :].bitcast(I32).rearrange("r (a c) -> r a c", a=2),
+                in_=w2_s_dram[:, 4 * q : 4 * q + 4, :].rearrange("a r c -> r a c"),
+            )
+        for s in range(PACK, 2 * PACK):
+            load_rest(s)
+
+        damp = {}
+
+        def daughters(s, m0, w):
+            nc.vector.tensor_copy(out=damp[s][:, m0 : m0 + w], in_=page_of(s)[:].indirect(entries("offs4", m0, w)))
+
+        def plain_daughters(s):
+            damp[s] = place("d%d" % s, [P, PAIRS], F32, DAUGHTER_AT[s])[:]
             daughters(s, 0, PAIRS)
-            if s % 2 == 1:
-                damp_two(s - 1)
 
-        def first_parents(s):
-            parents(summed0[:, s, :], s, 0, PAIRS)
-            if s < PACK - 1:
-                rest_sb[PACK + 1 + s] = load_rest(PACK + 1 + s)
+        def parents(out, s, m0, w):
+            nc.vector.tensor_tensor(
+                out=out,
+                in0=page_of(s)[:].indirect(entries("offs3", m0, w)),
+                in1=rest_sb[s][:, m0 : m0 + w],
+                op=ALU.add,
+            )
 
-        first_parents(0)
-        first_parents(1)
+        sums0 = place("sums0", [P, PACK, PAIRS], F32, SUMS0_AT)
+
+        def plain_parents(s):
+            summed = place("sum%d" % s, [P, PAIRS], F32, SUM_AT[s])
+            parents(summed[:], s, 0, PAIRS)
+            nc.sync.dma_start(out=sums0[32 * s : 32 * (s + 1), :, :], in_=summed[:])
+
+        plain_daughters(0)
+        plain_daughters(1)
+        for a in range(2):
+            stage = place("stage_b%d" % a, [P, PACK * KP], BF16, STAGE_B_AT[a])
+            round_dealt(raw_b[a], stage[:])
+            codes, scales = quantize(stage[:], KP, "w1_b%d" % a, W1_Q_AT + 5 + 2.5 * a)
+            for t in range(PACK):
+                w1_q[a, PACK + t] = (codes[:, P * t : P * (t + 1)], scales[:, P * t : P * (t + 1)])
+            pages[2 + a] = place("page%d" % (2 + a), [P, T2], F32, PAGE_AT[2 + a])
+            nc.gpsimd.memset(pages[2 + a][:].bitcast(I32), 0)
+            plain_parents(a)
+        for s in range(2, 2 * PACK):
+            whole_features(s)
+        w3_bf = place("stage_w3", [P, 2, PACK * KP], BF16, STAGE_W3_AT)
+        for a in range(2):
+            round_dealt(w3_raw[a], w3_bf[:, a, :])
+
+        def logarithm(logs, s, m0, w):
+            nc.scalar.activation(out=logs, in_=damp[s][:, m0 : m0 + w], func=ACT.Ln, bias=LN_FLOOR)
+
+        def sigmoid(logs):
+            nc.scalar.activation(out=logs, in_=logs, func=ACT.Sigmoid, scale=-2.0)
+
+        def times_gz(logs, s, m0, w):
+            b, t = divmod(s, PACK)
+            nc.scalar.activation(out=damp[s][:, m0 : m0 + w], in_=logs, func=ACT.Copy, scale=gz_sb[b][:, t : t + 1])
+
+        def scratch():
+            return place("logs", [P, 2 * PAIRS], F32, V_AT)
+
+        damp0 = place("damp0", [P, PACK, PAIRS], F32, RAW_W3_AT)
+
+        def damp_two(s):
+            logs = scratch()
+            for i in range(2):
+                logarithm(logs[:, PAIRS * i : PAIRS * (i + 1)], s + i, 0, PAIRS)
+            sigmoid(logs[:])
+            for i in range(2):
+                times_gz(logs[:, PAIRS * i : PAIRS * (i + 1)], s + i, 0, PAIRS)
+                if s < PACK:
+                    nc.sync.dma_start(out=damp0[32 * (s + i) : 32 * (s + i + 1), :, :], in_=damp[s + i])
+
+        damp_two(0)
+        scatter(2)
+        scatter(3)
+        plain_daughters(2)
         scatter(4)
+        plain_daughters(3)
+        damp_two(2)
+        damp1 = place("damp1", [P, PACK, PAIRS], F32, H_AT)
+        for t in range(PACK):
+            damp[PACK + t] = damp1[:, t, :]
         scatter(5)
         daughters(4, 0, PAIRS)
-        first_parents(2)
+        plain_parents(2)
         daughters(5, 0, PAIRS)
         damp_two(4)
         scatter(6)
-        first_parents(3)
+        plain_parents(3)
         daughters(6, 0, PAIRS)
         logs = scratch()
         most = PAIRS - P
@@ -289,10 +349,26 @@ def tile_list_airway_tree_step_kernel(
             times_gz(logs[:, P + m0 : P + m0 + w], 7, m0, w)
         sigmoid(logs[:, 0:P])
         times_gz(logs[:, 0:P], 6, most, P)
-        w3_c = keep.tile([P, 2, KP], U32, name="w3_c", tag="h6", bufs=1, align_bytes=64)
-        w3_s = keep.tile([P, 2, KP], U8, name="w3_s", align_bytes=64)
+        w3_c = place("w3_c", [P, 2, KP], U32, H_AT + 24)
+        w3_s = place("w3_s", [P, 2, KP], U8, SMALL_AT)
         for a in range(2):
-            nc.vector.quantize_mx(out=w3_c[:, a, :].bitcast(FP8X4), scales=w3_s[:, a, :], in_=w3_bf[a][:])
+            nc.vector.quantize_mx(out=w3_c[:, a, :].bitcast(FP8X4), scales=w3_s[:, a, :], in_=w3_bf[:, a, :])
+
+        z_c = [place("z_c%d" % b, [P, PAIRS], U32, Z_AT + 4 * b) for b in range(2)]
+        z_s = [place("z_s%d" % b, [P, PAIRS], U8, Z_AT + 8 + b) for b in range(2)]
+
+        def make_z(summed, factor, w, stage):
+            nc.vector.tensor_tensor(
+                out=stage.rearrange("p (c i t) -> p c t i", i=PACK, t=PACK),
+                in0=summed.rearrange("p t (c i) -> p c t i", i=PACK),
+                in1=factor.rearrange("p t (c i) -> p c t i", i=PACK),
+                op=ALU.mult,
+            )
+
+        def quantize_z(b, stage, m0, w):
+            nc.vector.quantize_mx(
+                out=z_c[b][:, m0 : m0 + w].bitcast(FP8X4), scales=z_s[b][:, m0 : m0 + w], in_=stage
+            )
 
         def passes(acc_a, acc_b, b, m0):
             cols = slice(m0, m0 + P)
@@ -315,8 +391,8 @@ def tile_list_airway_tree_step_kernel(
                 stop=(b == 1),
             )
 
-        y_c = late.tile([P, PAIRS], U32, name="y_c", align_bytes=64)
-        y_s = late.tile([P, PAIRS], U8, name="y_s", align_bytes=64)
+        y_c = place("y_c", [P, PAIRS], U32, Y_Q_AT)
+        y_s = place("y_s", [P, PAIRS], U8, Y_Q_AT + 4)
         out_rows = out_0.rearrange("(p t) m -> p t m", t=PACK)
         out_words = out_1[0].rearrange("p m t -> p (m t)").bitcast(I32)
         out_scales = out_2[0].bitcast(I32)
@@ -336,8 +412,8 @@ def tile_list_airway_tree_step_kernel(
 
         def turn_tile(m0):
             acc_a, acc_b = opened[m0]
-            gate = late.tile([P, PACK, P], F32, name="gate", tag="gate", bufs=2)
-            minus_a = late.tile([P, PACK, P], F32, name="minus_a", tag="minus_a", bufs=2)
+            gate = place("gate", [P, PACK, P], F32, REST_AT, bufs=2)
+            minus_a = place("minus_a", [P, PACK, P], F32, REST_AT + 4, bufs=2)
             nc.scalar.activation(out=gate[:].rearrange("p t m -> p (t m)"), in_=acc_b[:], func=ACT.Silu)
             src = acc_a[:].rearrange("p (m u e) -> p u m e", u=2, e=2)
             dst = minus_a[:].rearrange("p (u e) m -> p u m e", e=2)
@@ -366,8 +442,8 @@ def tile_list_airway_tree_step_kernel(
 
         def finish_tile(m0):
             banks = turned[m0]
-            stage = late.tile([P, PACK * P], BF16, name="y_stage", tag="y_stage", bufs=4, align_bytes=64)
-            y = late.tile([P, PACK, P], F32, name="y", tag="y", bufs=3)
+            stage = place("y_stage", [P, PACK * P], BF16, W1_Q_AT, bufs=4)
+            y = place("y", [P, PACK, P], F32, REST_AT + 8, bufs=3)
             if m0 == PAIRS - P:
                 nc.scalar.activation(
                     out=y[:, 0:2, :].rearrange("p t m -> p (t m)"), in_=banks[0][:], func=ACT.Copy, scale=-1.0
@@ -397,29 +473,27 @@ def tile_list_airway_tree_step_kernel(
             nc.sync.dma_start(out=out_words[:, m0 : m0 + P], in_=y_c[:, m0 : m0 + P].bitcast(I32))
             nc.sync.dma_start(out=out_rows[:, :, m0 : m0 + P], in_=y[:])
 
-        def late_parents(m0, w):
-            part = keep.tile([P, PACK, w], F32, name="summed1", tag="wgs1", bufs=2)
+        def late_parents(m0):
+            part = place("sums1_%d" % (m0 // P % 2), [P, PACK, P], F32, RAW_A_AT + 8 + 4 * (m0 // P % 2))
             for t in range(PACK):
-                parents(part[:, t, :], PACK + t, m0, w)
+                parents(part[:, t, :], PACK + t, m0, P)
             return part
 
-        def first_rows(m0, w):
-            stage = keep.tile([P, 2, PACK * w], BF16, name="z_stage", tag="h7", bufs=1, align_bytes=64)
-            make_z(0, summed0[:, :, m0 : m0 + w], m0, w, stage[:, 0, :])
-            quantize_z(0, stage[:, 0, :], m0, w)
+        def first_rows(m0):
+            stage = place("z_stage", [P, 2, PACK * P], BF16, H_AT + 28)
+            make_z(sums0[:, :, m0 : m0 + P], damp0[:, :, m0 : m0 + P], P, stage[:, 0, :])
+            quantize_z(0, stage[:, 0, :], m0, P)
             return stage
 
-        parts = [late_parents(0, PIECE)]
-        stage = first_rows(0, P)
+        part = late_parents(0)
+        stage = first_rows(0)
         open_tile(0)
         for m0 in range(0, PAIRS, P):
-            i, c0 = divmod(m0, PIECE)
-            make_z(1, parts[i][:, :, c0 : c0 + P], m0, P, stage[:, 1, :])
+            make_z(part[:], damp1[:, :, m0 : m0 + P], P, stage[:, 1, :])
             quantize_z(1, stage[:, 1, :], m0, P)
             if m0 + P < PAIRS:
-                stage = first_rows(m0 + P, P)
-            if c0 == 0 and m0 + PIECE < PAIRS:
-                parts.append(late_parents(m0 + PIECE, PIECE))
+                stage = first_rows(m0 + P)
+                part = late_parents(m0 + P)
             close_tile(m0)
             turn_tile(m0)
             if m0 > 0:

@@ -33,7 +33,7 @@ SUM_AT = (24, 36, 138, 142)
 H_AT = 40
 RAW_A_AT = 72
 RAW_W3_AT = 88
-SUMS0_AT = 104
+DAMP0_AT = 104
 STAGE_S0_AT = 120
 DAUGHTER_AT = (122, 126, 130, 134)
 V_AT = 146
@@ -267,12 +267,15 @@ def tile_list_airway_tree_step_kernel(
                 op=ALU.add,
             )
 
-        sums0 = place("sums0", [P, PACK, PAIRS], F32, SUMS0_AT)
+        plain_sums = {}
 
         def plain_parents(s):
             summed = place("sum%d" % s, [P, PAIRS], F32, SUM_AT[s])
             parents(summed[:], s, 0, PAIRS)
-            nc.sync.dma_start(out=sums0[32 * s : 32 * (s + 1), :, :], in_=summed[:])
+            plain_sums[s] = summed
+
+        def deal_sums(s):
+            nc.sync.dma_start(out=sums0[32 * s : 32 * (s + 1), :, :], in_=plain_sums[s][:])
 
         plain_daughters(0)
         plain_daughters(1)
@@ -290,6 +293,9 @@ def tile_list_airway_tree_step_kernel(
         w3_bf = place("stage_w3", [P, 2, PACK * KP], BF16, STAGE_W3_AT)
         for a in range(2):
             round_dealt(w3_raw[a], w3_bf[:, a, :])
+        sums0 = place("sums0", [P, PACK, PAIRS], F32, RAW_W3_AT)
+        deal_sums(0)
+        deal_sums(1)
 
         def logarithm(logs, s, m0, w):
             nc.scalar.activation(out=logs, in_=damp[s][:, m0 : m0 + w], func=ACT.Ln, bias=LN_FLOOR)
@@ -304,7 +310,7 @@ def tile_list_airway_tree_step_kernel(
         def scratch():
             return place("logs", [P, 2 * PAIRS], F32, V_AT)
 
-        damp0 = place("damp0", [P, PACK, PAIRS], F32, RAW_W3_AT)
+        damp0 = place("damp0", [P, PACK, PAIRS], F32, DAMP0_AT)
 
         def damp_two(s):
             logs = scratch()
@@ -314,7 +320,7 @@ def tile_list_airway_tree_step_kernel(
             for i in range(2):
                 times_gz(logs[:, PAIRS * i : PAIRS * (i + 1)], s + i, 0, PAIRS)
                 if s < PACK:
-                    nc.sync.dma_start(out=damp0[32 * (s + i) : 32 * (s + i + 1), :, :], in_=damp[s + i])
+                    nc.scalar.dma_start(out=damp0[32 * (s + i) : 32 * (s + i + 1), :, :], in_=damp[s + i])
 
         damp_two(0)
         scatter(2)
@@ -329,10 +335,12 @@ def tile_list_airway_tree_step_kernel(
         scatter(5)
         daughters(4, 0, PAIRS)
         plain_parents(2)
+        deal_sums(2)
         daughters(5, 0, PAIRS)
         damp_two(4)
         scatter(6)
         plain_parents(3)
+        deal_sums(3)
         daughters(6, 0, PAIRS)
         logs = scratch()
         most = PAIRS - P

@@ -111,13 +111,13 @@ def tile_list_airway_tree_step_kernel(
             return tw
 
         nc.sync.dma_start(lists["offs"][:], offs)
+        tab_w = [load_table(0)]
         tab_s_dram = tab_scales.bitcast(I32)
         for q in range(4):
-            nc.scalar.dma_start(
+            nc.sync.dma_start(
                 out=tab_s[32 * q : 32 * q + 8, :].bitcast(I32),
                 in_=tab_s_dram[:, 4 * q : 4 * q + 4, :],
             )
-        tab_w = [load_table(0)]
         raw_s0 = [load_weight(w1, a, 0, P, "raw_s0_%d" % a, RAW_A_AT + 2 * a) for a in range(2)]
         tab_w.append(load_table(1))
         nc.sync.dma_start(lists["offs2"][:], offs2)
@@ -141,10 +141,10 @@ def tile_list_airway_tree_step_kernel(
             rows = rest[P * s : P * (s + 1), :] if s < PACK else rest_dealt[s - PACK]
             nc.sync.dma_start(out=rest_sb[s][:], in_=rows)
 
-        v_s = place("v_s", [P, S], U8, V_S_AT)
-        nc.vector.tensor_copy(out=v_s[:], in_=tab_s[:].indirect(lists["offs"][:]))
         v_w = [place("v_w%d" % a, [P, S], U32, V_AT + 4 * a) for a in range(2)]
         nc.vector.tensor_copy(out=v_w[0][:], in_=tab_w[0][:].indirect(lists["offs"][:]))
+        v_s = place("v_s", [P, S], U8, V_S_AT)
+        nc.vector.tensor_copy(out=v_s[:], in_=tab_s[:].indirect(lists["offs"][:]))
 
         w1_q = {}
 

@@ -24,7 +24,7 @@ BANK = 512
 KB = 1024
 LN_FLOOR = 2.0 ** -60
 HALVES = ((0, 512), (512, 512))
-FIRST_PIECES = ((0, 256), (256, 256), (512, 512))
+QUARTER = 256
 
 PAGE_AT = (0, 8, 16, 28)
 TAB_AT = (16, 28)
@@ -35,6 +35,8 @@ RAW_A_AT = 72
 RAW_W3_AT = 88
 DAMP0_AT = 104
 STAGE_S0_AT = 120
+STAGE_S1_AT = 232
+H0_AT = (40, 42, RAW_A_AT + 6, 232)
 DAUGHTER_AT = (122, 126, 130, 134)
 V_AT = 146
 V_S_AT = 154
@@ -128,10 +130,6 @@ def tile_list_airway_tree_step_kernel(
         raw_b = [load_weight(w1, a, KP, KP, "raw_b_%d" % a, H_AT + 16 - 8 * a) for a in range(2)]
         nc.sync.dma_start(lists["offs4"][:], offs4)
         nc.sync.dma_start(lists["offs3"][:], offs3)
-        gz_sb = [place("gz_sb%d" % b, [P, PACK], F32, SMALL_AT + 4.5 + b / 16) for b in range(2)]
-        with nc.allow_non_contiguous_dma(reason="one factor a partition"):
-            nc.sync.dma_start(out=gz_sb[0][:], in_=gz[0:KP].rearrange("(s p) -> p s", p=P))
-        nc.sync.dma_start(out=gz_sb[1][:], in_=gz[KP : 2 * KP].rearrange("(p t) -> p t", t=PACK))
 
         rest_dealt = rest[KP : 2 * KP, :].rearrange("(p t) m -> t p m", t=PACK)
         rest_sb = {}
@@ -204,17 +202,19 @@ def tile_list_airway_tree_step_kernel(
             )
 
         def first_features(j0, w):
-            piece = place("h0_%d" % j0, [P, w], F32, H_AT + j0 * 4 / KB)
+            piece = place("h0_%d" % j0, [P, w], F32, H0_AT[j0 // QUARTER])
             h_sb[0, j0] = piece[:]
             features(0, j0, w)
 
-        for j0, w in FIRST_PIECES[0:2]:
-            first_features(j0, w)
-        scatter_first(*FIRST_PIECES[0])
-        plain_weights(raw_s1, 1, 1, "s1", H_AT + 2, W1_Q_AT + 1.25)
-        scatter_first(*FIRST_PIECES[1])
-        first_features(*FIRST_PIECES[2])
-        scatter_first(*FIRST_PIECES[2])
+        for i in range(2):
+            first_features(QUARTER * i, QUARTER)
+        scatter_first(0, QUARTER)
+        scatter_first(QUARTER, QUARTER)
+        plain_weights(raw_s1, 1, 1, "s1", STAGE_S1_AT, H_AT)
+        first_features(2 * QUARTER, QUARTER)
+        scatter_first(2 * QUARTER, QUARTER)
+        first_features(3 * QUARTER, QUARTER)
+        scatter_first(3 * QUARTER, QUARTER)
         whole_features(1)
         scatter(1)
         plain_weights(raw_s23, 2, 2, "s23", DAUGHTER_AT[0], W1_Q_AT + 2.5)
@@ -229,13 +229,17 @@ def tile_list_airway_tree_step_kernel(
             for q in (0, 2, 1, 3):
                 nc.sync.dma_start(out=wgs_t[t][32 * q : 32 * (q + 1), :], in_=wgs_rows[t])
 
+        w3_raw = [load_weight(w3, a, 0, N, "raw_w3_%d" % a, RAW_W3_AT + 8 * a) for a in range(2)]
+        gz_sb = [place("gz_sb%d" % b, [P, PACK], F32, SMALL_AT + 4.5 + b / 16) for b in range(2)]
+        with nc.allow_non_contiguous_dma(reason="one factor a partition"):
+            nc.sync.dma_start(out=gz_sb[0][:], in_=gz[0:KP].rearrange("(s p) -> p s", p=P))
+        nc.sync.dma_start(out=gz_sb[1][:], in_=gz[KP : 2 * KP].rearrange("(p t) -> p t", t=PACK))
         load_wgs(0)
         load_wgs(1)
         load_rest(2)
-        load_rest(3)
         load_wgs(2)
+        load_rest(3)
         load_wgs(3)
-        w3_raw = [load_weight(w3, a, 0, N, "raw_w3_%d" % a, RAW_W3_AT + 8 * a) for a in range(2)]
         w2_w = place("w2_w", [P, 2 * 2 * N], U8, SMALL_AT + 1)
         nc.sync.dma_start(
             out=w2_w[:].bitcast(I32).rearrange("p (a c) -> p a c", a=2),
@@ -288,11 +292,13 @@ def tile_list_airway_tree_step_kernel(
             pages[2 + a] = place("page%d" % (2 + a), [P, T2], F32, PAGE_AT[2 + a])
             nc.gpsimd.memset(pages[2 + a][:].bitcast(I32), 0)
             plain_parents(a)
-        for s in range(2, 2 * PACK):
+        for s in range(2, PACK):
             whole_features(s)
         w3_bf = place("stage_w3", [P, 2, PACK * KP], BF16, STAGE_W3_AT)
         for a in range(2):
             round_dealt(w3_raw[a], w3_bf[:, a, :])
+        for s in range(PACK, 2 * PACK):
+            whole_features(s)
         sums0 = place("sums0", [P, PACK, PAIRS], F32, RAW_W3_AT)
         deal_sums(0)
         deal_sums(1)
@@ -352,11 +358,12 @@ def tile_list_airway_tree_step_kernel(
         for m0, w in HALVES:
             daughters(7, m0, w)
             logarithm(logs[:, P + m0 : P + m0 + w], 7, m0, w)
-        for m0, w in ((0, 128), (128, 384), (512, 512)):
+        sigmoid(logs[:, 0 : 2 * P])
+        times_gz(logs[:, 0:P], 6, most, P)
+        times_gz(logs[:, P : 2 * P], 7, 0, P)
+        for m0, w in ((128, 384), (512, 512)):
             sigmoid(logs[:, P + m0 : P + m0 + w])
             times_gz(logs[:, P + m0 : P + m0 + w], 7, m0, w)
-        sigmoid(logs[:, 0:P])
-        times_gz(logs[:, 0:P], 6, most, P)
         w3_c = place("w3_c", [P, 2, KP], U32, H_AT + 24)
         w3_s = place("w3_s", [P, 2, KP], U8, SMALL_AT)
         for a in range(2):

@@ -273,13 +273,17 @@ def tile_list_airway_tree_step_kernel(
 
         plain_sums = {}
 
+        def deal(queue, dealt, s, plain):
+            for t in range(PACK):
+                queue.dma_start(out=dealt[32 * s : 32 * (s + 1), t, :], in_=plain[t:P:PACK, :])
+
         def plain_parents(s):
             summed = place("sum%d" % s, [P, PAIRS], F32, SUM_AT[s])
             parents(summed[:], s, 0, PAIRS)
             plain_sums[s] = summed
 
         def deal_sums(s):
-            nc.sync.dma_start(out=sums0[32 * s : 32 * (s + 1), :, :], in_=plain_sums[s][:])
+            deal(nc.sync, sums0, s, plain_sums[s][:])
 
         plain_daughters(0)
         plain_daughters(1)
@@ -326,7 +330,7 @@ def tile_list_airway_tree_step_kernel(
             for i in range(2):
                 times_gz(logs[:, PAIRS * i : PAIRS * (i + 1)], s + i, 0, PAIRS)
                 if s < PACK:
-                    nc.scalar.dma_start(out=damp0[32 * (s + i) : 32 * (s + i + 1), :, :], in_=damp[s + i])
+                    deal(nc.scalar, damp0, s + i, damp[s + i])
 
         damp_two(0)
         scatter(2)

@@ -25,18 +25,20 @@ KB = 1024
 LN_FLOOR = 2.0 ** -60
 HALVES = ((0, 512), (512, 512))
 QUARTER = 256
+HALF = 512
 
 PAGE_AT = (0, 8, 16, 28)
-TAB_AT = (16, 28)
-STAGE_B_AT = (22, 34)
-SUM_AT = (24, 36, 138, 142)
+TAB_AT = (104, 16)
+STAGE_B_AT = 138
+SUM_AT = (138, 142, 76, 80)
+Z_PLAIN_AT = (52, 54, 24, 26)
 H_AT = 40
 RAW_A_AT = 72
 RAW_W3_AT = 88
-DAMP0_AT = 104
+DAMP1_AT = 104
 STAGE_S0_AT = 120
-STAGE_S1_AT = 232
-H0_AT = (40, 42, RAW_A_AT + 6, 232)
+STAGE_S1_AT = 35
+H0_AT = (H_AT, RAW_A_AT + 6)
 DAUGHTER_AT = (122, 126, 130, 134)
 V_AT = 146
 V_S_AT = 154
@@ -158,9 +160,14 @@ def tile_list_airway_tree_step_kernel(
                     w1_q[a, first + i] = (codes[:, cols], scales[:, cols])
 
         plain_weights(raw_s0, 0, 1, "s0", STAGE_S0_AT, W1_Q_AT)
-        for j0, w in ((0, 256), (256, 768)):
+        for j0, w in ((0, QUARTER), (QUARTER, QUARTER), (HALF, HALF)):
             nc.vector.tensor_copy(out=v_w[1][:, j0 : j0 + w], in_=tab_w[1][:].indirect(entries("offs", j0, w)))
 
+        def clear_late_page(i):
+            pages[i] = place("page%d" % i, [P, T2], F32, PAGE_AT[i])
+            nc.gpsimd.memset(pages[i][:].bitcast(I32), 0)
+
+        clear_late_page(2)
         h_sb = {}
 
         def features(s, j0, w):
@@ -189,10 +196,10 @@ def tile_list_airway_tree_step_kernel(
         def page_of(s):
             return pages[(0, 1, 0, 1, 2, 3, 0, 1)[s]]
 
-        def scatter_first(j0, w):
+        def scatter_first(half, j0):
             nc.vector.tensor_tensor(
-                out=pages[0][:].indirect(entries("offs2", j0, w)),
-                in0=h_sb[0, j0], in1=wgs_plain[:, j0 : j0 + w], op=ALU.mult,
+                out=pages[0][:].indirect(entries("offs2", j0, HALF)),
+                in0=half[:], in1=wgs_plain[:, j0 : j0 + HALF], op=ALU.mult,
             )
 
         def scatter(s):
@@ -201,20 +208,17 @@ def tile_list_airway_tree_step_kernel(
                 out=page_of(s)[:].indirect(lists["offs2"][:]), in0=h_sb[s][:], in1=factor[:], op=ALU.mult
             )
 
-        def first_features(j0, w):
-            piece = place("h0_%d" % j0, [P, w], F32, H0_AT[j0 // QUARTER])
-            h_sb[0, j0] = piece[:]
-            features(0, j0, w)
-
-        for i in range(2):
-            first_features(QUARTER * i, QUARTER)
-        scatter_first(0, QUARTER)
-        scatter_first(QUARTER, QUARTER)
-        plain_weights(raw_s1, 1, 1, "s1", STAGE_S1_AT, H_AT)
-        first_features(2 * QUARTER, QUARTER)
-        scatter_first(2 * QUARTER, QUARTER)
-        first_features(3 * QUARTER, QUARTER)
-        scatter_first(3 * QUARTER, QUARTER)
+        first_half = place("h0_first", [P, HALF], F32, H0_AT[0])
+        for j0 in (0, QUARTER):
+            h_sb[0, j0] = first_half[:, j0 : j0 + QUARTER]
+            features(0, j0, QUARTER)
+        scatter_first(first_half, 0)
+        plain_weights(raw_s1, 1, 1, "s1", STAGE_S1_AT, W1_Q_AT + 1.25)
+        second_half = place("h0_second", [P, HALF], F32, H0_AT[1])
+        h_sb[0, HALF] = second_half[:]
+        features(0, HALF, HALF)
+        scatter_first(second_half, HALF)
+        clear_late_page(3)
         whole_features(1)
         scatter(1)
         plain_weights(raw_s23, 2, 2, "s23", DAUGHTER_AT[0], W1_Q_AT + 2.5)
@@ -282,20 +286,23 @@ def tile_list_airway_tree_step_kernel(
             parents(summed[:], s, 0, PAIRS)
             plain_sums[s] = summed
 
-        def deal_sums(s):
-            deal(nc.sync, sums0, s, plain_sums[s][:])
+        def plain_z(s):
+            z = place("z_plain%d" % s, [P, PAIRS], BF16, Z_PLAIN_AT[s])
+            nc.gpsimd.tensor_tensor(out=z[:], in0=plain_sums[s][:], in1=damp[s], op=ALU.mult)
+            deal(nc.sync, z0, s, z[:])
 
         plain_daughters(0)
         plain_daughters(1)
+        stage = place("stage_b", [P, 2 * PACK * KP], BF16, STAGE_B_AT)
         for a in range(2):
-            stage = place("stage_b%d" % a, [P, PACK * KP], BF16, STAGE_B_AT[a])
-            round_dealt(raw_b[a], stage[:])
-            codes, scales = quantize(stage[:], KP, "w1_b%d" % a, W1_Q_AT + 5 + 2.5 * a)
+            round_dealt(raw_b[a], stage[:, PACK * KP * a : PACK * KP * (a + 1)])
+        codes, scales = quantize(stage[:], 2 * KP, "w1_b", W1_Q_AT + 5)
+        for a in range(2):
             for t in range(PACK):
-                w1_q[a, PACK + t] = (codes[:, P * t : P * (t + 1)], scales[:, P * t : P * (t + 1)])
-            pages[2 + a] = place("page%d" % (2 + a), [P, T2], F32, PAGE_AT[2 + a])
-            nc.gpsimd.memset(pages[2 + a][:].bitcast(I32), 0)
-            plain_parents(a)
+                cols = slice(KP * a + P * t, KP * a + P * (t + 1))
+                w1_q[a, PACK + t] = (codes[:, cols], scales[:, cols])
+        plain_parents(0)
+        plain_parents(1)
         for s in range(2, PACK):
             whole_features(s)
         w3_bf = place("stage_w3", [P, 2, PACK * KP], BF16, STAGE_W3_AT)
@@ -303,9 +310,7 @@ def tile_list_airway_tree_step_kernel(
             round_dealt(w3_raw[a], w3_bf[:, a, :])
         for s in range(PACK, 2 * PACK):
             whole_features(s)
-        sums0 = place("sums0", [P, PACK, PAIRS], F32, RAW_W3_AT)
-        deal_sums(0)
-        deal_sums(1)
+        z0 = place("z0", [P, PACK, PAIRS], BF16, RAW_W3_AT)
 
         def logarithm(logs, s, m0, w):
             nc.scalar.activation(out=logs, in_=damp[s][:, m0 : m0 + w], func=ACT.Ln, bias=LN_FLOOR)
@@ -320,8 +325,6 @@ def tile_list_airway_tree_step_kernel(
         def scratch():
             return place("logs", [P, 2 * PAIRS], F32, V_AT)
 
-        damp0 = place("damp0", [P, PACK, PAIRS], F32, DAMP0_AT)
-
         def damp_two(s):
             logs = scratch()
             for i in range(2):
@@ -329,28 +332,28 @@ def tile_list_airway_tree_step_kernel(
             sigmoid(logs[:])
             for i in range(2):
                 times_gz(logs[:, PAIRS * i : PAIRS * (i + 1)], s + i, 0, PAIRS)
-                if s < PACK:
-                    deal(nc.scalar, damp0, s + i, damp[s + i])
 
         damp_two(0)
         scatter(2)
         scatter(3)
+        plain_z(0)
+        plain_z(1)
         plain_daughters(2)
-        scatter(4)
         plain_daughters(3)
         damp_two(2)
-        damp1 = place("damp1", [P, PACK, PAIRS], F32, H_AT)
+        damp1 = place("damp1", [P, PACK, PAIRS], F32, DAMP1_AT)
         for t in range(PACK):
             damp[PACK + t] = damp1[:, t, :]
+        scatter(4)
         scatter(5)
         daughters(4, 0, PAIRS)
         plain_parents(2)
-        deal_sums(2)
+        plain_z(2)
         daughters(5, 0, PAIRS)
         damp_two(4)
         scatter(6)
         plain_parents(3)
-        deal_sums(3)
+        plain_z(3)
         daughters(6, 0, PAIRS)
         logs = scratch()
         most = PAIRS - P
@@ -478,6 +481,14 @@ def tile_list_airway_tree_step_kernel(
                     out=stage[:].rearrange("p (c i t) -> p c t i", i=PACK, t=PACK),
                     in_=y[:].rearrange("p t (c i) -> p c t i", i=PACK),
                 )
+            elif m0 // P % 2 == 0:
+                nc.scalar.activation(
+                    out=y[:].rearrange("p t m -> p (t m)"), in_=banks[0][:], func=ACT.Copy, scale=-1.0
+                )
+                nc.vector.tensor_copy(
+                    out=stage[:].rearrange("p (c i t) -> p c t i", i=PACK, t=PACK),
+                    in_=y[:].rearrange("p t (c i) -> p c t i", i=PACK),
+                )
             else:
                 nc.scalar.activation(
                     out=stage[:].rearrange("p (c i t) -> p c t i", i=PACK, t=PACK),
@@ -500,7 +511,10 @@ def tile_list_airway_tree_step_kernel(
 
         def first_rows(m0):
             stage = place("z_stage", [P, 2, PACK * P], BF16, H_AT + 28)
-            make_z(sums0[:, :, m0 : m0 + P], damp0[:, :, m0 : m0 + P], P, stage[:, 0, :])
+            nc.vector.tensor_copy(
+                out=stage[:, 0, :].rearrange("p (c i t) -> p c t i", i=PACK, t=PACK),
+                in_=z0[:, :, m0 : m0 + P].rearrange("p t (c i) -> p c t i", i=PACK),
+            )
             quantize_z(0, stage[:, 0, :], m0, P)
             return stage
 

@@ -30,8 +30,9 @@ HALF = 512
 PAGE_AT = (0, 8, 16, 28)
 TAB_AT = (104, 16)
 STAGE_B_AT = 138
-SUM_AT = (138, 142, 76, 80)
-Z_PLAIN_AT = (52, 54, 24, 26)
+SUM_AT = (138, 142, 24, 36)
+Z_PLAIN_AT = (181, 232)
+WEIGHTED_AT = 165
 H_AT = 40
 RAW_A_AT = 72
 RAW_W3_AT = 88
@@ -44,9 +45,9 @@ V_AT = 146
 V_S_AT = 154
 TAB_S_AT = 155
 W1_Q_AT = 157
-STAGE_W3_AT = 167
+STAGE_W3_AT = 187
 WGS_AT = 175
-REST_AT = 179
+REST_AT = (167, 171, 183, 179, 195, 199, 203, 207)
 Z_AT = 211
 SMALL_AT = 221
 Y_Q_AT = 227
@@ -137,7 +138,7 @@ def tile_list_airway_tree_step_kernel(
         rest_sb = {}
 
         def load_rest(s):
-            rest_sb[s] = place("rest%d" % s, [P, PAIRS], F32, REST_AT + 4 * s)
+            rest_sb[s] = place("rest%d" % s, [P, PAIRS], F32, REST_AT[s])
             rows = rest[P * s : P * (s + 1), :] if s < PACK else rest_dealt[s - PACK]
             nc.sync.dma_start(out=rest_sb[s][:], in_=rows)
 
@@ -202,10 +203,12 @@ def tile_list_airway_tree_step_kernel(
                 in0=half[:], in1=wgs_plain[:, j0 : j0 + HALF], op=ALU.mult,
             )
 
+        def scatter_weighted(s):
+            nc.vector.tensor_copy(out=page_of(s)[:].indirect(lists["offs2"][:]), in_=weighted[:, s - PACK, :])
+
         def scatter(s):
-            factor = wgs_plain if s < PACK else wgs_t[s - PACK]
             nc.vector.tensor_tensor(
-                out=page_of(s)[:].indirect(lists["offs2"][:]), in0=h_sb[s][:], in1=factor[:], op=ALU.mult
+                out=page_of(s)[:].indirect(lists["offs2"][:]), in0=h_sb[s][:], in1=wgs_plain[:], op=ALU.mult
             )
 
         first_half = place("h0_first", [P, HALF], F32, H0_AT[0])
@@ -223,8 +226,8 @@ def tile_list_airway_tree_step_kernel(
         scatter(1)
         plain_weights(raw_s23, 2, 2, "s23", DAUGHTER_AT[0], W1_Q_AT + 2.5)
 
-        load_rest(0)
-        load_rest(1)
+        for s in range(PACK):
+            load_rest(s)
         wgs_rows = wgs.rearrange("(i t) j -> t i j", t=PACK)
         wgs_t = {}
 
@@ -238,12 +241,8 @@ def tile_list_airway_tree_step_kernel(
         with nc.allow_non_contiguous_dma(reason="one factor a partition"):
             nc.sync.dma_start(out=gz_sb[0][:], in_=gz[0:KP].rearrange("(s p) -> p s", p=P))
         nc.sync.dma_start(out=gz_sb[1][:], in_=gz[KP : 2 * KP].rearrange("(p t) -> p t", t=PACK))
-        load_wgs(0)
-        load_wgs(1)
-        load_rest(2)
-        load_wgs(2)
-        load_rest(3)
-        load_wgs(3)
+        for t in range(PACK):
+            load_wgs(t)
         w2_w = place("w2_w", [P, 2 * 2 * N], U8, SMALL_AT + 1)
         nc.sync.dma_start(
             out=w2_w[:].bitcast(I32).rearrange("p (a c) -> p a c", a=2),
@@ -286,10 +285,13 @@ def tile_list_airway_tree_step_kernel(
             parents(summed[:], s, 0, PAIRS)
             plain_sums[s] = summed
 
-        def plain_z(s):
-            z = place("z_plain%d" % s, [P, PAIRS], BF16, Z_PLAIN_AT[s])
-            nc.gpsimd.tensor_tensor(out=z[:], in0=plain_sums[s][:], in1=damp[s], op=ALU.mult)
-            deal(nc.sync, z0, s, z[:])
+        def plain_z(first):
+            z = place("z_plain%d" % first, [P, 2, PAIRS], BF16, Z_PLAIN_AT[first // 2])
+            for i in range(2):
+                nc.gpsimd.tensor_tensor(
+                    out=z[:, i, :], in0=plain_sums[first + i][:], in1=damp[first + i], op=ALU.mult
+                )
+                deal(nc.sync, z0, first + i, z[:, i, :])
 
         plain_daughters(0)
         plain_daughters(1)
@@ -336,24 +338,35 @@ def tile_list_airway_tree_step_kernel(
         damp_two(0)
         scatter(2)
         scatter(3)
-        plain_z(0)
-        plain_z(1)
+        plain_parents(2)
+        plain_parents(3)
+        weighted = place("weighted", [P, PACK, S], F32, WEIGHTED_AT)
+        for t in range(PACK):
+            nc.gpsimd.tensor_tensor(out=weighted[:, t, :], in0=h_sb[PACK + t][:], in1=wgs_t[t][:], op=ALU.mult)
         plain_daughters(2)
         plain_daughters(3)
+        plain_z(0)
         damp_two(2)
+        plain_z(2)
+        woven0 = place("woven0", [P, PAIRS, PACK], BF16, RAW_W3_AT + 8)
+        for m0, w in HALVES:
+            nc.gpsimd.tensor_scalar(
+                out=woven0[:, m0 : m0 + w, :],
+                in0=z0[:, :, m0 : m0 + w].rearrange("p t m -> p m t"),
+                scalar1=1.0,
+                scalar2=0.0,
+                op0=ALU.mult,
+                op1=ALU.add,
+            )
         damp1 = place("damp1", [P, PACK, PAIRS], F32, DAMP1_AT)
         for t in range(PACK):
             damp[PACK + t] = damp1[:, t, :]
-        scatter(4)
-        scatter(5)
+        scatter_weighted(4)
+        scatter_weighted(5)
         daughters(4, 0, PAIRS)
-        plain_parents(2)
-        plain_z(2)
         daughters(5, 0, PAIRS)
         damp_two(4)
-        scatter(6)
-        plain_parents(3)
-        plain_z(3)
+        scatter_weighted(6)
         daughters(6, 0, PAIRS)
         logs = scratch()
         most = PAIRS - P
@@ -361,7 +374,7 @@ def tile_list_airway_tree_step_kernel(
         sigmoid(logs[:, 0:most])
         times_gz(logs[:, 0:most], 6, 0, most)
         logarithm(logs[:, 0:P], 6, most, P)
-        scatter(7)
+        scatter_weighted(7)
         for m0, w in HALVES:
             daughters(7, m0, w)
             logarithm(logs[:, P + m0 : P + m0 + w], 7, m0, w)
@@ -371,12 +384,12 @@ def tile_list_airway_tree_step_kernel(
         for m0, w in ((128, 384), (512, 512)):
             sigmoid(logs[:, P + m0 : P + m0 + w])
             times_gz(logs[:, P + m0 : P + m0 + w], 7, m0, w)
-        w3_c = place("w3_c", [P, 2, KP], U32, H_AT + 24)
+        w3_c = place("w3_c", [P, 2, KP], U32, WEIGHTED_AT + 6)
         w3_s = place("w3_s", [P, 2, KP], U8, SMALL_AT)
         for a in range(2):
             nc.vector.quantize_mx(out=w3_c[:, a, :].bitcast(FP8X4), scales=w3_s[:, a, :], in_=w3_bf[:, a, :])
 
-        z_c = [place("z_c%d" % b, [P, PAIRS], U32, Z_AT + 4 * b) for b in range(2)]
+        z_c = [place("z_c%d" % b, [P, PAIRS], U32, (WEIGHTED_AT + 12, Z_AT + 4)[b]) for b in range(2)]
         z_s = [place("z_s%d" % b, [P, PAIRS], U8, Z_AT + 8 + b) for b in range(2)]
 
         def make_z(summed, factor, w, stage):
@@ -434,8 +447,8 @@ def tile_list_airway_tree_step_kernel(
 
         def turn_tile(m0):
             acc_a, acc_b = opened[m0]
-            gate = place("gate", [P, PACK, P], F32, REST_AT, bufs=2)
-            minus_a = place("minus_a", [P, PACK, P], F32, REST_AT + 4, bufs=2)
+            gate = place("gate", [P, PACK, P], F32, H_AT, bufs=2)
+            minus_a = place("minus_a", [P, PACK, P], F32, H_AT + 4, bufs=2)
             nc.scalar.activation(out=gate[:].rearrange("p t m -> p (t m)"), in_=acc_b[:], func=ACT.Silu)
             src = acc_a[:].rearrange("p (m u e) -> p u m e", u=2, e=2)
             dst = minus_a[:].rearrange("p (u e) m -> p u m e", e=2)
@@ -465,7 +478,7 @@ def tile_list_airway_tree_step_kernel(
         def finish_tile(m0):
             banks = turned[m0]
             stage = place("y_stage", [P, PACK * P], BF16, W1_Q_AT, bufs=4)
-            y = place("y", [P, PACK, P], F32, REST_AT + 8, bufs=3)
+            y = place("y", [P, PACK, P], F32, H_AT + 8, bufs=6)
             if m0 == PAIRS - P:
                 nc.scalar.activation(
                     out=y[:, 0:2, :].rearrange("p t m -> p (t m)"), in_=banks[0][:], func=ACT.Copy, scale=-1.0
@@ -477,55 +490,36 @@ def tile_list_airway_tree_step_kernel(
                     scalar2=None,
                     op0=ALU.mult,
                 )
-                nc.vector.tensor_copy(
-                    out=stage[:].rearrange("p (c i t) -> p c t i", i=PACK, t=PACK),
-                    in_=y[:].rearrange("p t (c i) -> p c t i", i=PACK),
-                )
-            elif m0 // P % 2 == 0:
-                nc.scalar.activation(
-                    out=y[:].rearrange("p t m -> p (t m)"), in_=banks[0][:], func=ACT.Copy, scale=-1.0
-                )
-                nc.vector.tensor_copy(
-                    out=stage[:].rearrange("p (c i t) -> p c t i", i=PACK, t=PACK),
-                    in_=y[:].rearrange("p t (c i) -> p c t i", i=PACK),
-                )
             else:
                 nc.scalar.activation(
-                    out=stage[:].rearrange("p (c i t) -> p c t i", i=PACK, t=PACK),
-                    in_=banks[0][:].rearrange("p (t c i) -> p c t i", i=PACK, t=PACK),
-                    func=ACT.Copy,
-                    scale=-1.0,
-                )
-                nc.scalar.activation(
                     out=y[:].rearrange("p t m -> p (t m)"), in_=banks[0][:], func=ACT.Copy, scale=-1.0
                 )
+            nc.vector.tensor_copy(
+                out=stage[:].rearrange("p (c i t) -> p c t i", i=PACK, t=PACK),
+                in_=y[:].rearrange("p t (c i) -> p c t i", i=PACK),
+            )
             nc.vector.quantize_mx(out=y_c[:, m0 : m0 + P].bitcast(FP8X4), scales=y_s[:, m0 : m0 + P], in_=stage[:])
             nc.sync.dma_start(out=out_words[:, m0 : m0 + P], in_=y_c[:, m0 : m0 + P].bitcast(I32))
             nc.sync.dma_start(out=out_rows[:, :, m0 : m0 + P], in_=y[:])
 
         def late_parents(m0):
-            part = place("sums1_%d" % (m0 // P % 2), [P, PACK, P], F32, RAW_A_AT + 8 + 4 * (m0 // P % 2))
+            if m0 == 0:
+                part = place("sums1_first", [P, PACK, P], F32, WEIGHTED_AT + 3)
+            else:
+                part = place("sums1", [P, PACK, P], F32, WEIGHTED_AT + 2, bufs=2)
             for t in range(PACK):
                 parents(part[:, t, :], PACK + t, m0, P)
             return part
 
-        def first_rows(m0):
-            stage = place("z_stage", [P, 2, PACK * P], BF16, H_AT + 28)
-            nc.vector.tensor_copy(
-                out=stage[:, 0, :].rearrange("p (c i t) -> p c t i", i=PACK, t=PACK),
-                in_=z0[:, :, m0 : m0 + P].rearrange("p t (c i) -> p c t i", i=PACK),
-            )
-            quantize_z(0, stage[:, 0, :], m0, P)
-            return stage
-
+        for m0, w in HALVES:
+            quantize_z(0, woven0[:, m0 : m0 + w, :].rearrange("p m t -> p (m t)"), m0, w)
         part = late_parents(0)
-        stage = first_rows(0)
         open_tile(0)
         for m0 in range(0, PAIRS, P):
-            make_z(part[:], damp1[:, :, m0 : m0 + P], P, stage[:, 1, :])
-            quantize_z(1, stage[:, 1, :], m0, P)
+            stage = place("z_stage", [P, PACK * P], BF16, WEIGHTED_AT, bufs=2)
+            make_z(part[:], damp1[:, :, m0 : m0 + P], P, stage[:])
+            quantize_z(1, stage[:], m0, P)
             if m0 + P < PAIRS:
-                stage = first_rows(m0 + P)
                 part = late_parents(m0 + P)
             close_tile(m0)
             turn_tile(m0)

@@ -26,6 +26,9 @@ LN_FLOOR = 2.0 ** -60
 HALVES = ((0, 512), (512, 512))
 QUARTER = 256
 HALF = 512
+AHEAD = 4
+PUT_OFF = 32
+LAST_PIECES = ((0, 512), (512, 256), (768, 256))
 
 PAGE_AT = (0, 8, 16, 28)
 TAB_AT = (104, 16)
@@ -173,7 +176,7 @@ def tile_list_airway_tree_step_kernel(
 
         def features(s, j0, w):
             cols = slice(j0, j0 + w)
-            acc = psum.tile([P, w], F32, name="acc", tag="sums", bufs=6)
+            acc = psum.tile([P, w], F32, name="acc", tag="bank", bufs=8)
             for a in range(2):
                 codes, scales = w1_q[a, s]
                 nc.tensor.matmul_mx(
@@ -365,25 +368,32 @@ def tile_list_airway_tree_step_kernel(
         scatter_weighted(5)
         daughters(4, 0, PAIRS)
         daughters(5, 0, PAIRS)
-        damp_two(4)
+        most = PAIRS - PUT_OFF
+        logs = scratch()
+        logarithm(logs[:, 0:PAIRS], 4, 0, PAIRS)
+        logarithm(logs[:, PAIRS : PAIRS + most], 5, 0, most)
+        sigmoid(logs[:, 0 : PAIRS + most])
+        times_gz(logs[:, PAIRS : PAIRS + most], 5, 0, most)
+        times_gz(logs[:, 0:PAIRS], 4, 0, PAIRS)
+        logarithm(logs[:, 0:PUT_OFF], 5, most, PUT_OFF)
         scatter_weighted(6)
         daughters(6, 0, PAIRS)
-        logs = scratch()
-        most = PAIRS - P
-        logarithm(logs[:, 0:most], 6, 0, most)
-        sigmoid(logs[:, 0:most])
-        times_gz(logs[:, 0:most], 6, 0, most)
-        logarithm(logs[:, 0:P], 6, most, P)
+        logarithm(logs[:, PUT_OFF:PAIRS], 6, 0, most)
+        sigmoid(logs[:, 0:PAIRS])
+        times_gz(logs[:, 0:PUT_OFF], 5, most, PUT_OFF)
+        times_gz(logs[:, PUT_OFF:PAIRS], 6, 0, most)
+        logarithm(logs[:, 0:PUT_OFF], 6, most, PUT_OFF)
         scatter_weighted(7)
-        for m0, w in HALVES:
+        last = logs[:, PUT_OFF : PUT_OFF + PAIRS]
+        for m0, w in LAST_PIECES:
             daughters(7, m0, w)
-            logarithm(logs[:, P + m0 : P + m0 + w], 7, m0, w)
-        sigmoid(logs[:, 0 : 2 * P])
-        times_gz(logs[:, 0:P], 6, most, P)
-        times_gz(logs[:, P : 2 * P], 7, 0, P)
+            logarithm(last[:, m0 : m0 + w], 7, m0, w)
+        sigmoid(logs[:, 0 : PUT_OFF + P])
+        times_gz(logs[:, 0:PUT_OFF], 6, most, PUT_OFF)
+        times_gz(last[:, 0:P], 7, 0, P)
         for m0, w in ((128, 384), (512, 512)):
-            sigmoid(logs[:, P + m0 : P + m0 + w])
-            times_gz(logs[:, P + m0 : P + m0 + w], 7, m0, w)
+            sigmoid(last[:, m0 : m0 + w])
+            times_gz(last[:, m0 : m0 + w], 7, m0, w)
         w3_c = place("w3_c", [P, 2, KP], U32, WEIGHTED_AT + 6)
         w3_s = place("w3_s", [P, 2, KP], U8, SMALL_AT)
         for a in range(2):
@@ -435,8 +445,8 @@ def tile_list_airway_tree_step_kernel(
         opened = {}
 
         def open_tile(m0):
-            acc_b = psum.tile([P, BANK], F32, name="acc", tag="sums", bufs=6)
-            acc_a = psum.tile([P, BANK], F32, name="acc", tag="sums", bufs=6)
+            acc_b = psum.tile([P, BANK], F32, name="acc", tag="bank", bufs=8)
+            acc_a = psum.tile([P, BANK], F32, name="acc", tag="bank", bufs=8)
             passes(acc_a, acc_b, 0, m0)
             opened[m0] = (acc_a, acc_b)
 
@@ -457,9 +467,8 @@ def tile_list_airway_tree_step_kernel(
             else:
                 nc.scalar.activation(out=dst, in_=src, func=ACT.Copy, scale=-1.0)
             per_bank = 2 if m0 == PAIRS - P else PACK
-            tag, bufs = ("sums", 6) if m0 == PAIRS - P else ("minus_y", 2)
             banks = [
-                psum.tile([P, per_bank * P], F32, name="minus_y", tag=tag, bufs=bufs)
+                psum.tile([P, per_bank * P], F32, name="minus_y", tag="bank", bufs=8)
                 for i in range(PACK // per_bank)
             ]
             for k, term in enumerate((gate, minus_a)):
@@ -514,7 +523,8 @@ def tile_list_airway_tree_step_kernel(
         for m0, w in HALVES:
             quantize_z(0, woven0[:, m0 : m0 + w, :].rearrange("p m t -> p (m t)"), m0, w)
         part = late_parents(0)
-        open_tile(0)
+        for m0 in range(0, AHEAD * P, P):
+            open_tile(m0)
         for m0 in range(0, PAIRS, P):
             stage = place("z_stage", [P, PACK * P], BF16, WEIGHTED_AT, bufs=2)
             make_z(part[:], damp1[:, :, m0 : m0 + P], P, stage[:])
@@ -525,8 +535,8 @@ def tile_list_airway_tree_step_kernel(
             turn_tile(m0)
             if m0 > 0:
                 finish_tile(m0 - P)
-            if m0 + P < PAIRS:
-                open_tile(m0 + P)
+            if 0 < m0 <= PAIRS - AHEAD * P:
+                open_tile(m0 + (AHEAD - 1) * P)
         finish_tile(PAIRS - P)
         for q in range(4):
             queue = nc.sync if q % 2 == 0 else nc.scalar

@@ -23,37 +23,47 @@ KP = P * PACK
 BANK = 512
 KB = 1024
 LN_FLOOR = 2.0 ** -60
-HALVES = ((0, 512), (512, 512))
 QUARTER = 256
 HALF = 512
+HALVES = ((0, HALF), (HALF, HALF))
 AHEAD = 4
+TURNED = 4
 PUT_OFF = 32
 LAST_PIECES = ((0, 512), (512, 256), (768, 256))
+EDGE = 1 / 16
 
-PAGE_AT = (0, 8, 16, 28)
-TAB_AT = (104, 16)
-STAGE_B_AT = 138
-SUM_AT = (138, 142, 24, 36)
-Z_PLAIN_AT = (181, 232)
-WEIGHTED_AT = 165
-H_AT = 40
-RAW_A_AT = 72
-RAW_W3_AT = 88
-DAMP1_AT = 104
-STAGE_S0_AT = 120
-STAGE_S1_AT = 35
-H0_AT = (H_AT, RAW_A_AT + 6)
-DAUGHTER_AT = (122, 126, 130, 134)
-V_AT = 146
-V_S_AT = 154
-TAB_S_AT = 155
-W1_Q_AT = 157
-STAGE_W3_AT = 187
-WGS_AT = 175
-REST_AT = (167, 171, 183, 179, 195, 199, 203, 207)
-Z_AT = 211
-SMALL_AT = 221
-Y_Q_AT = 227
+PAGE_AT = (0, 8, 16, 24)
+TAB_AT = (186, 16)
+STAGE_AT = (24, 26, 28)
+V_AT = 32
+V_S_AT = 40
+LOGS_AT = 32
+W2_DEALT_AT = 40
+W1_Q_AT = 42
+TAB_S_AT = 52
+WGS_AT = 54
+SUMS01_AT = 58
+H_AT = {3: 66, 2: 70, 4: 74, 5: 78, 6: 82, 7: 86, 1: 92}
+H0_AT = (90, 102 + EDGE)
+RAW_B_AT = 66 - EDGE
+DAMP1_AT = 66
+WGS_T_AT = 98
+RAW_A_AT = 98 + EDGE
+DAMP01_AT = 114
+RAW_W3_AT = (122, 134)
+Z0_AT = 122
+SUMS23_AT = 130
+WOVEN0_AT = 130
+DAMP23_AT = 138
+W3_BF_AT = 146
+STAGE_B_AT = 154
+WEIGHTED_AT = 162
+REST_AT = (162 + EDGE, 166 + EDGE, 170 + EDGE, 174 + EDGE, 186, 190, 194, 198)
+Z_PLAIN_AT = 178
+SMALL_AT = 202
+Z_AT = 207
+Y_Q_AT = 213
+Y_RUNS = ((0, 4, 43), (4, 3, 40), (7, 1, 47))
 
 
 def tile_list_airway_tree_step_kernel(
@@ -66,8 +76,11 @@ def tile_list_airway_tree_step_kernel(
         pool = ctx.enter_context(tc.tile_pool(name="pool", bufs=1))
         psum = ctx.enter_context(tc.psum_pool(name="psum", bufs=1))
 
-        def place(name, shape, dtype, kib, bufs=1):
-            return pool.tile(shape, dtype, name=name, tag=name, bufs=bufs, align_bytes=64, offset=int(kib * KB))
+        def place(name, shape, dtype, kib):
+            return pool.tile(shape, dtype, name=name, tag=name, bufs=1, align_bytes=64, offset=int(kib * KB))
+
+        def bank(name):
+            return psum.tile([P, BANK], F32, name=name, tag="bank", bufs=8)
 
         lists = {}
         for name in ("offs", "offs2", "offs3", "offs4"):
@@ -76,16 +89,20 @@ def tile_list_airway_tree_step_kernel(
         def entries(name, j0, w):
             return lists[name][:, j0 // 16 : (j0 + w) // 16]
 
+        pages = [None] * PACK
+
+        def clear_page(i):
+            pages[i] = place("page%d" % i, [P, T2], F32, PAGE_AT[i])
+            nc.gpsimd.memset(pages[i][:].bitcast(I32), 0)
+
         tab_s = place("tab_s", [P, T], U8, TAB_S_AT)
-        w2_s = place("w2_s", [P, 2 * N], U8, SMALL_AT + 3)
+        w2_s = place("w2_s", [P, 2 * N], U8, SMALL_AT + 2)
         ident = place("ident", [P, P], F32, SMALL_AT + 4)
         nc.gpsimd.memset(tab_s[:].bitcast(I32), 0)
+        clear_page(0)
         nc.gpsimd.memset(w2_s[:].bitcast(I32), 0)
         make_identity(nc, ident[:])
-        pages = [None] * PACK
-        for i in range(2):
-            pages[i] = place("page%d" % i, [P, T2], F32, PAGE_AT[i])
-            nc.vector.memset(pages[i][:].bitcast(I32), 0)
+        clear_page(1)
 
         def load_weight(w, a, c0, width, name, kib):
             raw = place(name, [P, PACK, width], F32, kib)
@@ -119,21 +136,22 @@ def tile_list_airway_tree_step_kernel(
             return tw
 
         nc.sync.dma_start(lists["offs"][:], offs)
-        tab_w = [load_table(0)]
         tab_s_dram = tab_scales.bitcast(I32)
         for q in range(4):
             nc.sync.dma_start(
                 out=tab_s[32 * q : 32 * q + 8, :].bitcast(I32),
                 in_=tab_s_dram[:, 4 * q : 4 * q + 4, :],
             )
-        raw_s0 = [load_weight(w1, a, 0, P, "raw_s0_%d" % a, RAW_A_AT + 2 * a) for a in range(2)]
-        tab_w.append(load_table(1))
+        raw_s0, tab_w = [], []
+        for a in range(2):
+            raw_s0.append(load_weight(w1, a, 0, P, "raw_s0_%d" % a, RAW_A_AT + 2 * a))
+            tab_w.append(load_table(a))
         nc.sync.dma_start(lists["offs2"][:], offs2)
         wgs_plain = place("wgs_plain", [P, S], F32, WGS_AT)
         nc.sync.dma_start(out=wgs_plain[:], in_=wgs)
         raw_s1 = [load_weight(w1, a, P, P, "raw_s1_%d" % a, RAW_A_AT + 4 + 2 * a) for a in range(2)]
         raw_s23 = [load_weight(w1, a, 2 * P, 2 * P, "raw_s23_%d" % a, RAW_A_AT + 8 + 4 * a) for a in range(2)]
-        raw_b = [load_weight(w1, a, KP, KP, "raw_b_%d" % a, H_AT + 16 - 8 * a) for a in range(2)]
+        raw_b = [load_weight(w1, a, KP, KP, "raw_b_%d" % a, RAW_B_AT + 8 - 8 * a) for a in range(2)]
         nc.sync.dma_start(lists["offs4"][:], offs4)
         nc.sync.dma_start(lists["offs3"][:], offs3)
 
@@ -145,10 +163,10 @@ def tile_list_airway_tree_step_kernel(
             rows = rest[P * s : P * (s + 1), :] if s < PACK else rest_dealt[s - PACK]
             nc.sync.dma_start(out=rest_sb[s][:], in_=rows)
 
-        v_w = [place("v_w%d" % a, [P, S], U32, V_AT + 4 * a) for a in range(2)]
-        nc.vector.tensor_copy(out=v_w[0][:], in_=tab_w[0][:].indirect(lists["offs"][:]))
         v_s = place("v_s", [P, S], U8, V_S_AT)
         nc.vector.tensor_copy(out=v_s[:], in_=tab_s[:].indirect(lists["offs"][:]))
+        v_w = [place("v_w%d" % a, [P, S], U32, V_AT + 4 * a) for a in range(2)]
+        nc.vector.tensor_copy(out=v_w[0][:], in_=tab_w[0][:].indirect(lists["offs"][:]))
 
         w1_q = {}
 
@@ -163,24 +181,18 @@ def tile_list_airway_tree_step_kernel(
                     cols = slice(width * a + P * i, width * a + P * (i + 1))
                     w1_q[a, first + i] = (codes[:, cols], scales[:, cols])
 
-        plain_weights(raw_s0, 0, 1, "s0", STAGE_S0_AT, W1_Q_AT)
+        plain_weights(raw_s0, 0, 1, "s0", STAGE_AT[0], W1_Q_AT)
         for j0, w in ((0, QUARTER), (QUARTER, QUARTER), (HALF, HALF)):
             nc.vector.tensor_copy(out=v_w[1][:, j0 : j0 + w], in_=tab_w[1][:].indirect(entries("offs", j0, w)))
+        clear_page(2)
 
-        def clear_late_page(i):
-            pages[i] = place("page%d" % i, [P, T2], F32, PAGE_AT[i])
-            nc.gpsimd.memset(pages[i][:].bitcast(I32), 0)
-
-        clear_late_page(2)
-        h_sb = {}
-
-        def features(s, j0, w):
+        def features(s, j0, w, out):
             cols = slice(j0, j0 + w)
-            acc = psum.tile([P, w], F32, name="acc", tag="bank", bufs=8)
+            acc = bank("acc")
             for a in range(2):
                 codes, scales = w1_q[a, s]
                 nc.tensor.matmul_mx(
-                    out=acc[:],
+                    out=acc[:, 0:w],
                     lhsT=codes.bitcast(FP8X4),
                     lhsT_scale=scales,
                     rhs=v_w[a][:, cols].bitcast(FP8X4),
@@ -188,26 +200,23 @@ def tile_list_airway_tree_step_kernel(
                     start=(a == 0),
                     stop=(a == 1),
                 )
-            nc.scalar.activation(out=h_sb[s, j0], in_=acc[:], func=ACT.Exp)
+            nc.scalar.activation(out=out, in_=acc[:, 0:w], func=ACT.Exp)
+
+        h_sb = {}
 
         def whole_features(s):
-            h = place("h%d" % s, [P, S], F32, H_AT + 4 * s)
+            h_sb[s] = place("h%d" % s, [P, S], F32, H_AT[s])
             for j0, w in HALVES:
-                h_sb[s, j0] = h[:, j0 : j0 + w]
-                features(s, j0, w)
-            h_sb[s] = h
+                features(s, j0, w, h_sb[s][:, j0 : j0 + w])
 
         def page_of(s):
-            return pages[(0, 1, 0, 1, 2, 3, 0, 1)[s]]
+            return pages[(0, 1, 0, 1, 0, 1, 2, 3)[s]]
 
         def scatter_first(half, j0):
             nc.vector.tensor_tensor(
                 out=pages[0][:].indirect(entries("offs2", j0, HALF)),
                 in0=half[:], in1=wgs_plain[:, j0 : j0 + HALF], op=ALU.mult,
             )
-
-        def scatter_weighted(s):
-            nc.vector.tensor_copy(out=page_of(s)[:].indirect(lists["offs2"][:]), in_=weighted[:, s - PACK, :])
 
         def scatter(s):
             nc.vector.tensor_tensor(
@@ -216,18 +225,16 @@ def tile_list_airway_tree_step_kernel(
 
         first_half = place("h0_first", [P, HALF], F32, H0_AT[0])
         for j0 in (0, QUARTER):
-            h_sb[0, j0] = first_half[:, j0 : j0 + QUARTER]
-            features(0, j0, QUARTER)
+            features(0, j0, QUARTER, first_half[:, j0 : j0 + QUARTER])
         scatter_first(first_half, 0)
-        plain_weights(raw_s1, 1, 1, "s1", STAGE_S1_AT, W1_Q_AT + 1.25)
+        plain_weights(raw_s1, 1, 1, "s1", STAGE_AT[1], W1_Q_AT + 1.25)
         second_half = place("h0_second", [P, HALF], F32, H0_AT[1])
-        h_sb[0, HALF] = second_half[:]
-        features(0, HALF, HALF)
+        features(0, HALF, HALF, second_half[:])
         scatter_first(second_half, HALF)
-        clear_late_page(3)
         whole_features(1)
         scatter(1)
-        plain_weights(raw_s23, 2, 2, "s23", DAUGHTER_AT[0], W1_Q_AT + 2.5)
+        plain_weights(raw_s23, 2, 2, "s23", STAGE_AT[2], W1_Q_AT + 2.5)
+        clear_page(3)
 
         for s in range(PACK):
             load_rest(s)
@@ -235,18 +242,18 @@ def tile_list_airway_tree_step_kernel(
         wgs_t = {}
 
         def load_wgs(t):
-            wgs_t[t] = place("wgs%d" % t, [P, S], F32, RAW_A_AT + 4 * t)
+            wgs_t[t] = place("wgs%d" % t, [P, S], F32, WGS_T_AT + 4 * t)
             for q in (0, 2, 1, 3):
                 nc.sync.dma_start(out=wgs_t[t][32 * q : 32 * (q + 1), :], in_=wgs_rows[t])
 
-        w3_raw = [load_weight(w3, a, 0, N, "raw_w3_%d" % a, RAW_W3_AT + 8 * a) for a in range(2)]
-        gz_sb = [place("gz_sb%d" % b, [P, PACK], F32, SMALL_AT + 4.5 + b / 16) for b in range(2)]
+        w3_raw = [load_weight(w3, a, 0, N, "raw_w3_%d" % a, RAW_W3_AT[a]) for a in range(2)]
+        gz_sb = [place("gz_sb%d" % b, [P, PACK], F32, SMALL_AT + 4.5 + b * EDGE) for b in range(2)]
         with nc.allow_non_contiguous_dma(reason="one factor a partition"):
             nc.sync.dma_start(out=gz_sb[0][:], in_=gz[0:KP].rearrange("(s p) -> p s", p=P))
         nc.sync.dma_start(out=gz_sb[1][:], in_=gz[KP : 2 * KP].rearrange("(p t) -> p t", t=PACK))
         for t in range(PACK):
             load_wgs(t)
-        w2_w = place("w2_w", [P, 2 * 2 * N], U8, SMALL_AT + 1)
+        w2_w = place("w2_w", [P, 2 * 2 * N], U8, SMALL_AT)
         nc.sync.dma_start(
             out=w2_w[:].bitcast(I32).rearrange("p (a c) -> p a c", a=2),
             in_=w2_words.bitcast(I32).rearrange("a p c -> p a c"),
@@ -260,14 +267,15 @@ def tile_list_airway_tree_step_kernel(
         for s in range(PACK, 2 * PACK):
             load_rest(s)
 
-        damp = {}
+        damp, sums = {}, {}
+
+        def two_slices(store, name, first, kib):
+            both = place(name, [P, 2, PAIRS], F32, kib)
+            for i in range(2):
+                store[first + i] = both[:, i, :]
 
         def daughters(s, m0, w):
             nc.vector.tensor_copy(out=damp[s][:, m0 : m0 + w], in_=page_of(s)[:].indirect(entries("offs4", m0, w)))
-
-        def plain_daughters(s):
-            damp[s] = place("d%d" % s, [P, PAIRS], F32, DAUGHTER_AT[s])[:]
-            daughters(s, 0, PAIRS)
 
         def parents(out, s, m0, w):
             nc.vector.tensor_tensor(
@@ -277,27 +285,9 @@ def tile_list_airway_tree_step_kernel(
                 op=ALU.add,
             )
 
-        plain_sums = {}
-
-        def deal(queue, dealt, s, plain):
-            for t in range(PACK):
-                queue.dma_start(out=dealt[32 * s : 32 * (s + 1), t, :], in_=plain[t:P:PACK, :])
-
-        def plain_parents(s):
-            summed = place("sum%d" % s, [P, PAIRS], F32, SUM_AT[s])
-            parents(summed[:], s, 0, PAIRS)
-            plain_sums[s] = summed
-
-        def plain_z(first):
-            z = place("z_plain%d" % first, [P, 2, PAIRS], BF16, Z_PLAIN_AT[first // 2])
-            for i in range(2):
-                nc.gpsimd.tensor_tensor(
-                    out=z[:, i, :], in0=plain_sums[first + i][:], in1=damp[first + i], op=ALU.mult
-                )
-                deal(nc.sync, z0, first + i, z[:, i, :])
-
-        plain_daughters(0)
-        plain_daughters(1)
+        two_slices(damp, "damp01", 0, DAMP01_AT)
+        for s in (0, 1):
+            daughters(s, 0, PAIRS)
         stage = place("stage_b", [P, 2 * PACK * KP], BF16, STAGE_B_AT)
         for a in range(2):
             round_dealt(raw_b[a], stage[:, PACK * KP * a : PACK * KP * (a + 1)])
@@ -306,16 +296,16 @@ def tile_list_airway_tree_step_kernel(
             for t in range(PACK):
                 cols = slice(KP * a + P * t, KP * a + P * (t + 1))
                 w1_q[a, PACK + t] = (codes[:, cols], scales[:, cols])
-        plain_parents(0)
-        plain_parents(1)
-        for s in range(2, PACK):
+        two_slices(sums, "sums01", 0, SUMS01_AT)
+        for s in (0, 1):
+            parents(sums[s], s, 0, PAIRS)
+        for s in (2, 3):
             whole_features(s)
-        w3_bf = place("stage_w3", [P, 2, PACK * KP], BF16, STAGE_W3_AT)
+        w3_bf = place("stage_w3", [P, 2, PACK * KP], BF16, W3_BF_AT)
         for a in range(2):
             round_dealt(w3_raw[a], w3_bf[:, a, :])
         for s in range(PACK, 2 * PACK):
             whole_features(s)
-        z0 = place("z0", [P, PACK, PAIRS], BF16, RAW_W3_AT)
 
         def logarithm(logs, s, m0, w):
             nc.scalar.activation(out=logs, in_=damp[s][:, m0 : m0 + w], func=ACT.Ln, bias=LN_FLOOR)
@@ -327,11 +317,8 @@ def tile_list_airway_tree_step_kernel(
             b, t = divmod(s, PACK)
             nc.scalar.activation(out=damp[s][:, m0 : m0 + w], in_=logs, func=ACT.Copy, scale=gz_sb[b][:, t : t + 1])
 
-        def scratch():
-            return place("logs", [P, 2 * PAIRS], F32, V_AT)
-
         def damp_two(s):
-            logs = scratch()
+            logs = place("logs", [P, 2 * PAIRS], F32, LOGS_AT)
             for i in range(2):
                 logarithm(logs[:, PAIRS * i : PAIRS * (i + 1)], s + i, 0, PAIRS)
             sigmoid(logs[:])
@@ -339,19 +326,41 @@ def tile_list_airway_tree_step_kernel(
                 times_gz(logs[:, PAIRS * i : PAIRS * (i + 1)], s + i, 0, PAIRS)
 
         damp_two(0)
-        scatter(2)
-        scatter(3)
-        plain_parents(2)
-        plain_parents(3)
-        weighted = place("weighted", [P, PACK, S], F32, WEIGHTED_AT)
-        for t in range(PACK):
-            nc.gpsimd.tensor_tensor(out=weighted[:, t, :], in0=h_sb[PACK + t][:], in1=wgs_t[t][:], op=ALU.mult)
-        plain_daughters(2)
-        plain_daughters(3)
-        plain_z(0)
+        for s in (2, 3):
+            scatter(s)
+        two_slices(sums, "sums23", 2, SUMS23_AT)
+        for s in (2, 3):
+            parents(sums[s], s, 0, PAIRS)
+        two_slices(damp, "damp23", 2, DAMP23_AT)
+        for s in (2, 3):
+            daughters(s, 0, PAIRS)
         damp_two(2)
+        w2_dealt = place("w2_dealt", [P, 2 * 2 * N], U8, W2_DEALT_AT)
+        nc.scalar.copy(
+            out=w2_dealt[:].bitcast(U16).rearrange("p (a t m) -> p a m t", a=2, t=PACK),
+            in_=w2_w[:].bitcast(U16).rearrange("p (a m t) -> p a m t", a=2, t=PACK),
+        )
+
+        weighted = place("weighted", [P, PACK, S], F32, WEIGHTED_AT)
+        z_plain = place("z_plain", [P, PACK, PAIRS], BF16, Z_PLAIN_AT)
+        z0 = place("z0", [P, PACK, PAIRS], BF16, Z0_AT)
+
+        def weigh(t):
+            nc.gpsimd.tensor_tensor(out=weighted[:, t, :], in0=h_sb[PACK + t][:], in1=wgs_t[t][:], op=ALU.mult)
+
+        def plain_z(s):
+            nc.gpsimd.tensor_tensor(out=z_plain[:, s, :], in0=sums[s], in1=damp[s], op=ALU.mult)
+            for t in range(PACK):
+                nc.sync.dma_start(out=z0[32 * s : 32 * (s + 1), t, :], in_=z_plain[t:P:PACK, s, :])
+
+        for t in range(3):
+            weigh(t)
+        plain_z(0)
+        plain_z(1)
+        weigh(3)
         plain_z(2)
-        woven0 = place("woven0", [P, PAIRS, PACK], BF16, RAW_W3_AT + 8)
+        plain_z(3)
+        woven0 = place("woven0", [P, PAIRS, PACK], BF16, WOVEN0_AT)
         for m0, w in HALVES:
             nc.gpsimd.tensor_scalar(
                 out=woven0[:, m0 : m0 + w, :],
@@ -361,6 +370,15 @@ def tile_list_airway_tree_step_kernel(
                 op0=ALU.mult,
                 op1=ALU.add,
             )
+        w2_s_dealt = place("w2_s_dealt", [P, 2 * N], U8, Z0_AT)
+        nc.gpsimd.tensor_copy(
+            out=w2_s_dealt[:].rearrange("p (a t m) -> p a m t", a=2, t=PACK),
+            in_=w2_s[:].rearrange("p (a m t) -> p a m t", a=2, t=PACK),
+        )
+
+        def scatter_weighted(s):
+            nc.vector.tensor_copy(out=page_of(s)[:].indirect(lists["offs2"][:]), in_=weighted[:, s - PACK, :])
+
         damp1 = place("damp1", [P, PACK, PAIRS], F32, DAMP1_AT)
         for t in range(PACK):
             damp[PACK + t] = damp1[:, t, :]
@@ -369,40 +387,57 @@ def tile_list_airway_tree_step_kernel(
         daughters(4, 0, PAIRS)
         daughters(5, 0, PAIRS)
         most = PAIRS - PUT_OFF
-        logs = scratch()
+        logs = place("logs45", [P, PAIRS + most], F32, LOGS_AT)
         logarithm(logs[:, 0:PAIRS], 4, 0, PAIRS)
-        logarithm(logs[:, PAIRS : PAIRS + most], 5, 0, most)
-        sigmoid(logs[:, 0 : PAIRS + most])
-        times_gz(logs[:, PAIRS : PAIRS + most], 5, 0, most)
+        logarithm(logs[:, PAIRS:], 5, 0, most)
+        sigmoid(logs[:])
+        times_gz(logs[:, PAIRS:], 5, 0, most)
         times_gz(logs[:, 0:PAIRS], 4, 0, PAIRS)
+        logs = place("logs6", [P, PAIRS], F32, LOGS_AT + 2)
         logarithm(logs[:, 0:PUT_OFF], 5, most, PUT_OFF)
         scatter_weighted(6)
         daughters(6, 0, PAIRS)
-        logarithm(logs[:, PUT_OFF:PAIRS], 6, 0, most)
-        sigmoid(logs[:, 0:PAIRS])
+        logarithm(logs[:, PUT_OFF:], 6, 0, most)
+        sigmoid(logs[:])
         times_gz(logs[:, 0:PUT_OFF], 5, most, PUT_OFF)
-        times_gz(logs[:, PUT_OFF:PAIRS], 6, 0, most)
-        logarithm(logs[:, 0:PUT_OFF], 6, most, PUT_OFF)
+        times_gz(logs[:, PUT_OFF:], 6, 0, most)
+        first7 = place("logs7_first", [P, PUT_OFF + P], F32, LOGS_AT + 2)
+        next7 = place("logs7_next", [P, HALF - P], F32, LOGS_AT + 2.625)
+        last7 = place("logs7_last", [P, HALF], F32, LOGS_AT + 4.125)
+        logarithm(first7[:, 0:PUT_OFF], 6, most, PUT_OFF)
         scatter_weighted(7)
-        last = logs[:, PUT_OFF : PUT_OFF + PAIRS]
         for m0, w in LAST_PIECES:
             daughters(7, m0, w)
-            logarithm(last[:, m0 : m0 + w], 7, m0, w)
-        sigmoid(logs[:, 0 : PUT_OFF + P])
-        times_gz(logs[:, 0:PUT_OFF], 6, most, PUT_OFF)
-        times_gz(last[:, 0:P], 7, 0, P)
-        for m0, w in ((128, 384), (512, 512)):
-            sigmoid(last[:, m0 : m0 + w])
-            times_gz(last[:, m0 : m0 + w], 7, m0, w)
-        w3_c = place("w3_c", [P, 2, KP], U32, WEIGHTED_AT + 6)
-        w3_s = place("w3_s", [P, 2, KP], U8, SMALL_AT)
+            if m0 == 0:
+                logarithm(first7[:, PUT_OFF:], 7, 0, P)
+                logarithm(next7[:], 7, P, HALF - P)
+            else:
+                logarithm(last7[:, m0 - HALF : m0 - HALF + w], 7, m0, w)
+        sigmoid(first7[:])
+        times_gz(first7[:, 0:PUT_OFF], 6, most, PUT_OFF)
+        times_gz(first7[:, PUT_OFF:], 7, 0, P)
+        sigmoid(next7[:])
+        times_gz(next7[:], 7, P, HALF - P)
+        sigmoid(last7[:])
+        times_gz(last7[:], 7, HALF, HALF)
+
+        z_q = {}
+
+        def quantize_z(b, stage, m0, w, kib):
+            codes, scales = quantize(stage, w, "z%d_%d" % (b, m0), kib)
+            for i in range(0, w, P):
+                z_q[b, m0 + i] = (codes[:, i : i + P].bitcast(FP8X4), scales[:, i : i + P])
+
+        def quantize_woven(m0, kib):
+            quantize_z(0, woven0[:, m0 : m0 + HALF, :].rearrange("p m t -> p (m t)"), m0, HALF, kib)
+
+        quantize_woven(0, WEIGHTED_AT)
+        w3_c = place("w3_c", [P, 2, KP], U32, WEIGHTED_AT + 4)
+        w3_s = place("w3_s", [P, 2, KP], U8, SMALL_AT + 3)
         for a in range(2):
             nc.vector.quantize_mx(out=w3_c[:, a, :].bitcast(FP8X4), scales=w3_s[:, a, :], in_=w3_bf[:, a, :])
 
-        z_c = [place("z_c%d" % b, [P, PAIRS], U32, (WEIGHTED_AT + 12, Z_AT + 4)[b]) for b in range(2)]
-        z_s = [place("z_s%d" % b, [P, PAIRS], U8, Z_AT + 8 + b) for b in range(2)]
-
-        def make_z(summed, factor, w, stage):
+        def make_z(summed, factor, stage):
             nc.vector.tensor_tensor(
                 out=stage.rearrange("p (c i t) -> p c t i", i=PACK, t=PACK),
                 in0=summed.rearrange("p t (c i) -> p c t i", i=PACK),
@@ -410,31 +445,36 @@ def tile_list_airway_tree_step_kernel(
                 op=ALU.mult,
             )
 
-        def quantize_z(b, stage, m0, w):
-            nc.vector.quantize_mx(
-                out=z_c[b][:, m0 : m0 + w].bitcast(FP8X4), scales=z_s[b][:, m0 : m0 + w], in_=stage
+        def passes_turned(acc_a, acc_b, b, m0):
+            codes, scales = z_q[b, m0]
+            nc.tensor.matmul_mx(
+                out=acc_b[:], lhsT=codes, lhsT_scale=scales,
+                rhs=w3_c[:, b, :].bitcast(FP8X4), rhs_scale=w3_s[:, b, :],
+                start=(b == 0), stop=(b == 1),
+            )
+            nc.tensor.matmul_mx(
+                out=acc_a[:], lhsT=codes, lhsT_scale=scales,
+                rhs=w2_w[:, 2 * N * b : 2 * N * (b + 1)].bitcast(FP4X4), rhs_scale=w2_s[:, N * b : N * (b + 1)],
+                start=(b == 0), stop=(b == 1),
             )
 
-        def passes(acc_a, acc_b, b, m0):
-            cols = slice(m0, m0 + P)
-            nc.tensor.matmul_mx(
-                out=acc_b[:],
-                lhsT=z_c[b][:, cols].bitcast(FP8X4),
-                lhsT_scale=z_s[b][:, cols],
-                rhs=w3_c[:, b, :].bitcast(FP8X4),
-                rhs_scale=w3_s[:, b, :],
-                start=(b == 0),
-                stop=(b == 1),
-            )
-            nc.tensor.matmul_mx(
-                out=acc_a[:],
-                lhsT=z_c[b][:, cols].bitcast(FP8X4),
-                lhsT_scale=z_s[b][:, cols],
-                rhs=w2_w[:, 2 * N * b : 2 * N * (b + 1)].bitcast(FP4X4),
-                rhs_scale=w2_s[:, N * b : N * (b + 1)],
-                start=(b == 0),
-                stop=(b == 1),
-            )
+        def passes_upright(acc_a, acc_b, b, m0):
+            codes, scales = z_q[b, m0]
+            for t in range(PACK):
+                nc.tensor.matmul_mx(
+                    out=acc_b[:, P * t : P * (t + 1)],
+                    lhsT=w3_c[:, b, P * t : P * (t + 1)].bitcast(FP8X4), lhsT_scale=w3_s[:, b, P * t : P * (t + 1)],
+                    rhs=codes, rhs_scale=scales,
+                    start=(b == 0 and t == 0), stop=(b == 1 and t == PACK - 1),
+                )
+            for t in range(PACK):
+                c0 = N * b + P * t
+                nc.tensor.matmul_mx(
+                    out=acc_a[:, P * t : P * (t + 1)],
+                    lhsT=w2_dealt[:, 2 * c0 : 2 * (c0 + P)].bitcast(FP4X4), lhsT_scale=w2_s_dealt[:, c0 : c0 + P],
+                    rhs=codes, rhs_scale=scales,
+                    start=(b == 0 and t == 0), stop=(b == 1 and t == PACK - 1),
+                )
 
         y_c = place("y_c", [P, PAIRS], U32, Y_Q_AT)
         y_s = place("y_s", [P, PAIRS], U8, Y_Q_AT + 4)
@@ -442,102 +482,110 @@ def tile_list_airway_tree_step_kernel(
         out_words = out_1[0].rearrange("p m t -> p (m t)").bitcast(I32)
         out_scales = out_2[0].bitcast(I32)
 
-        opened = {}
+        opened, gates, turned, stages = {}, {}, {}, {}
 
-        def open_tile(m0):
-            acc_b = psum.tile([P, BANK], F32, name="acc", tag="bank", bufs=8)
-            acc_a = psum.tile([P, BANK], F32, name="acc", tag="bank", bufs=8)
-            passes(acc_a, acc_b, 0, m0)
-            opened[m0] = (acc_a, acc_b)
+        def passes(j, b):
+            form = passes_turned if j < TURNED else passes_upright
+            form(*opened[j], b, P * j)
 
-        def close_tile(m0):
-            passes(*opened[m0], 1, m0)
+        def open_tile(j):
+            acc_b = bank("acc")
+            acc_a = bank("acc")
+            opened[j] = (acc_a, acc_b)
+            passes(j, 0)
 
-        turned = {}
-
-        def turn_tile(m0):
-            acc_a, acc_b = opened[m0]
-            gate = place("gate", [P, PACK, P], F32, H_AT, bufs=2)
-            minus_a = place("minus_a", [P, PACK, P], F32, H_AT + 4, bufs=2)
+        def empty_sums(j):
+            acc_a, acc_b = opened[j]
+            gate = place("gate%d" % j, [P, PACK, P], F32, WGS_T_AT + 2 * (j % 3))
             nc.scalar.activation(out=gate[:].rearrange("p t m -> p (t m)"), in_=acc_b[:], func=ACT.Silu)
-            src = acc_a[:].rearrange("p (m u e) -> p u m e", u=2, e=2)
-            dst = minus_a[:].rearrange("p (u e) m -> p u m e", e=2)
-            if m0 == PAIRS - P:
-                nc.vector.tensor_scalar(out=dst, in0=src, scalar1=-1.0, scalar2=None, op0=ALU.mult)
-            else:
-                nc.scalar.activation(out=dst, in_=src, func=ACT.Copy, scale=-1.0)
-            per_bank = 2 if m0 == PAIRS - P else PACK
-            banks = [
-                psum.tile([P, per_bank * P], F32, name="minus_y", tag="bank", bufs=8)
-                for i in range(PACK // per_bank)
-            ]
-            for k, term in enumerate((gate, minus_a)):
-                for t in range(PACK):
-                    i, u = divmod(t, per_bank)
-                    nc.tensor.matmul(
-                        banks[i][:, P * u : P * (u + 1)],
-                        lhsT=term[:, t, :],
-                        rhs=ident[:],
-                        is_transpose=True,
-                        start=(k == 0 and u == 0),
-                        stop=(k == 1 and u == per_bank - 1),
-                    )
-            turned[m0] = banks
+            gates[j] = gate
+            if j < TURNED:
+                minus_a = place("minus_a%d" % j, [P, PACK, P], F32, WGS_T_AT + 6 + 2 * (j % 3))
+                nc.scalar.activation(
+                    out=minus_a[:].rearrange("p (u e) m -> p u m e", e=2),
+                    in_=acc_a[:].rearrange("p (m u e) -> p u m e", u=2, e=2),
+                    func=ACT.Copy,
+                    scale=-1.0,
+                )
+                minus_y = bank("minus_y")
+                for k, term in enumerate((gate, minus_a)):
+                    for t in range(PACK):
+                        nc.tensor.matmul(
+                            minus_y[:, P * t : P * (t + 1)],
+                            lhsT=term[:, t, :],
+                            rhs=ident[:],
+                            is_transpose=True,
+                            start=(k == 0 and t == 0),
+                            stop=(k == 1 and t == PACK - 1),
+                        )
+                turned[j] = minus_y
 
-        def finish_tile(m0):
-            banks = turned[m0]
-            stage = place("y_stage", [P, PACK * P], BF16, W1_Q_AT, bufs=4)
-            y = place("y", [P, PACK, P], F32, H_AT + 8, bufs=6)
-            if m0 == PAIRS - P:
+        def finish_tile(j):
+            m0 = P * j
+            first, count, kib = [run for run in Y_RUNS if run[0] <= j < run[0] + run[1]][0]
+            if j == first:
+                stages[first] = place("y_stage%d" % j, [P, count, PACK * P], BF16, kib)
+            stage = stages[first][:, j - first, :]
+            y = place("y%d" % j, [P, PACK, P], F32, WGS_T_AT + 12 + 2 * (j % 6))
+            woven = stage.rearrange("p (c i t) -> p c t i", i=PACK, t=PACK)
+            if j < TURNED:
                 nc.scalar.activation(
-                    out=y[:, 0:2, :].rearrange("p t m -> p (t m)"), in_=banks[0][:], func=ACT.Copy, scale=-1.0
+                    out=y[:].rearrange("p t m -> p (t m)"), in_=turned[j][:], func=ACT.Copy, scale=-1.0
                 )
-                nc.vector.tensor_scalar(
-                    out=y[:, 2:4, :].rearrange("p t m -> p (t m)"),
-                    in0=banks[1][:],
-                    scalar1=-1.0,
-                    scalar2=None,
-                    op0=ALU.mult,
+                nc.scalar.activation(
+                    out=woven,
+                    in_=turned[j][:].rearrange("p (t c i) -> p c t i", t=PACK, i=PACK),
+                    func=ACT.Copy,
+                    scale=-1.0,
                 )
             else:
-                nc.scalar.activation(
-                    out=y[:].rearrange("p t m -> p (t m)"), in_=banks[0][:], func=ACT.Copy, scale=-1.0
+                nc.vector.tensor_tensor(
+                    out=y[:].rearrange("p t m -> p (t m)"),
+                    in0=opened[j][0][:],
+                    in1=gates[j][:].rearrange("p t m -> p (t m)"),
+                    op=ALU.subtract,
                 )
-            nc.vector.tensor_copy(
-                out=stage[:].rearrange("p (c i t) -> p c t i", i=PACK, t=PACK),
-                in_=y[:].rearrange("p t (c i) -> p c t i", i=PACK),
-            )
-            nc.vector.quantize_mx(out=y_c[:, m0 : m0 + P].bitcast(FP8X4), scales=y_s[:, m0 : m0 + P], in_=stage[:])
-            nc.sync.dma_start(out=out_words[:, m0 : m0 + P], in_=y_c[:, m0 : m0 + P].bitcast(I32))
+                rows = y[:].rearrange("p t (c i) -> p c t i", i=PACK)
+                if j == tiles - 2:
+                    nc.vector.tensor_copy(out=woven, in_=rows)
+                else:
+                    nc.scalar.copy(out=woven, in_=rows)
             nc.sync.dma_start(out=out_rows[:, :, m0 : m0 + P], in_=y[:])
+            if j == first + count - 1:
+                cols = slice(P * first, P * (first + count))
+                nc.vector.quantize_mx(
+                    out=y_c[:, cols].bitcast(FP8X4),
+                    scales=y_s[:, cols],
+                    in_=stages[first][:].rearrange("p j c -> p (j c)"),
+                )
+                nc.sync.dma_start(out=out_words[:, cols], in_=y_c[:, cols].bitcast(I32))
 
-        def late_parents(m0):
-            if m0 == 0:
-                part = place("sums1_first", [P, PACK, P], F32, WEIGHTED_AT + 3)
-            else:
-                part = place("sums1", [P, PACK, P], F32, WEIGHTED_AT + 2, bufs=2)
+        def late_parents(j):
+            part = place("sums1_%d" % j, [P, PACK, P], F32, (WEIGHTED_AT + 10, LOGS_AT + 0.625)[j % 2])
             for t in range(PACK):
-                parents(part[:, t, :], PACK + t, m0, P)
+                parents(part[:, t, :], PACK + t, P * j, P)
             return part
 
-        for m0, w in HALVES:
-            quantize_z(0, woven0[:, m0 : m0 + w, :].rearrange("p m t -> p (m t)"), m0, w)
+        tiles = PAIRS // P
         part = late_parents(0)
-        for m0 in range(0, AHEAD * P, P):
-            open_tile(m0)
-        for m0 in range(0, PAIRS, P):
-            stage = place("z_stage", [P, PACK * P], BF16, WEIGHTED_AT, bufs=2)
-            make_z(part[:], damp1[:, :, m0 : m0 + P], P, stage[:])
-            quantize_z(1, stage[:], m0, P)
-            if m0 + P < PAIRS:
-                part = late_parents(m0 + P)
-            close_tile(m0)
-            turn_tile(m0)
-            if m0 > 0:
-                finish_tile(m0 - P)
-            if 0 < m0 <= PAIRS - AHEAD * P:
-                open_tile(m0 + (AHEAD - 1) * P)
-        finish_tile(PAIRS - P)
+        for j in range(AHEAD):
+            open_tile(j)
+        for j in range(tiles):
+            m0 = P * j
+            stage = place("z_stage%d" % j, [P, PACK * P], BF16, WEIGHTED_AT + 12 + j % 2)
+            make_z(part[:], damp1[:, :, m0 : m0 + P], stage[:])
+            if j + 1 < tiles:
+                part = late_parents(j + 1)
+            quantize_z(1, stage[:], m0, P, Z_AT + 0.625 * j)
+            if j == 0:
+                quantize_woven(HALF, LOGS_AT + 2.625)
+            passes(j, 1)
+            empty_sums(j)
+            if j > 0:
+                finish_tile(j - 1)
+            if 0 < j <= tiles - AHEAD:
+                open_tile(j + AHEAD - 1)
+        finish_tile(tiles - 1)
         for q in range(4):
             queue = nc.sync if q % 2 == 0 else nc.scalar
             queue.dma_start(out=out_scales[4 * q : 4 * q + 4, :], in_=y_s[32 * q : 32 * q + 4, :].bitcast(I32))

@@ -370,10 +370,10 @@ def tile_list_airway_tree_step_kernel(
                 op0=ALU.mult,
                 op1=ALU.add,
             )
-        w2_s_dealt = place("w2_s_dealt", [P, 2 * N], U8, Z0_AT)
+        w2_s_dealt = place("w2_s_dealt", [P, 2 * N], U8, Z_PLAIN_AT)
         nc.gpsimd.tensor_copy(
-            out=w2_s_dealt[:].rearrange("p (a t m) -> p a m t", a=2, t=PACK),
-            in_=w2_s[:].rearrange("p (a m t) -> p a m t", a=2, t=PACK),
+            out=w2_s_dealt[:].rearrange("p (a t m) -> p a t m", a=2, t=PACK),
+            in_=w2_s[:].rearrange("p (a m t) -> p a t m", a=2, t=PACK),
         )
 
         def scatter_weighted(s):
@@ -387,20 +387,37 @@ def tile_list_airway_tree_step_kernel(
         daughters(4, 0, PAIRS)
         daughters(5, 0, PAIRS)
         most = PAIRS - PUT_OFF
+        flat = damp1[:].rearrange("p t m -> p (t m)")
+
+        def sigmoid_back(logs, first, count):
+            nc.scalar.activation(out=flat[:, first : first + count], in_=logs, func=ACT.Sigmoid, scale=-2.0)
+
+        factor = place("factor", [P, PACK, PAIRS], F32, DAMP01_AT)
+
+        def gz_scalar(logs, s, m0, w):
+            nc.scalar.activation(
+                out=factor[:, s - PACK, m0 : m0 + w], in_=logs, func=ACT.Copy, scale=gz_sb[1][:, s - PACK : s - PACK + 1]
+            )
+
+        def gz_gpsimd(s, m0, w):
+            nc.gpsimd.tensor_scalar(
+                out=factor[:, s - PACK, m0 : m0 + w], in0=damp[s][:, m0 : m0 + w],
+                scalar1=gz_sb[1][:, s - PACK : s - PACK + 1], scalar2=0.0, op0=ALU.mult, op1=ALU.add,
+            )
+
         logs = place("logs45", [P, PAIRS + most], F32, LOGS_AT)
         logarithm(logs[:, 0:PAIRS], 4, 0, PAIRS)
         logarithm(logs[:, PAIRS:], 5, 0, most)
-        sigmoid(logs[:])
-        times_gz(logs[:, PAIRS:], 5, 0, most)
-        times_gz(logs[:, 0:PAIRS], 4, 0, PAIRS)
+        sigmoid_back(logs[:], 0, PAIRS + most)
+        gz_gpsimd(4, 0, PAIRS)
         logs = place("logs6", [P, PAIRS], F32, LOGS_AT + 2)
         logarithm(logs[:, 0:PUT_OFF], 5, most, PUT_OFF)
         scatter_weighted(6)
         daughters(6, 0, PAIRS)
         logarithm(logs[:, PUT_OFF:], 6, 0, most)
-        sigmoid(logs[:])
-        times_gz(logs[:, 0:PUT_OFF], 5, most, PUT_OFF)
-        times_gz(logs[:, PUT_OFF:], 6, 0, most)
+        sigmoid_back(logs[:], PAIRS + most, PAIRS)
+        gz_gpsimd(5, 0, PAIRS)
+        gz_gpsimd(6, 0, most)
         first7 = place("logs7_first", [P, PUT_OFF + P], F32, LOGS_AT + 2)
         next7 = place("logs7_next", [P, HALF - P], F32, LOGS_AT + 2.625)
         last7 = place("logs7_last", [P, HALF], F32, LOGS_AT + 4.125)
@@ -414,12 +431,12 @@ def tile_list_airway_tree_step_kernel(
             else:
                 logarithm(last7[:, m0 - HALF : m0 - HALF + w], 7, m0, w)
         sigmoid(first7[:])
-        times_gz(first7[:, 0:PUT_OFF], 6, most, PUT_OFF)
-        times_gz(first7[:, PUT_OFF:], 7, 0, P)
+        gz_scalar(first7[:, PUT_OFF:], 7, 0, P)
         sigmoid(next7[:])
-        times_gz(next7[:], 7, P, HALF - P)
+        gz_scalar(next7[:], 7, P, HALF - P)
         sigmoid(last7[:])
-        times_gz(last7[:], 7, HALF, HALF)
+        gz_scalar(last7[:], 7, HALF, HALF)
+        gz_scalar(first7[:, 0:PUT_OFF], 6, most, PUT_OFF)
 
         z_q = {}
 
@@ -526,7 +543,7 @@ def tile_list_airway_tree_step_kernel(
             if j == first:
                 stages[first] = place("y_stage%d" % j, [P, count, PACK * P], BF16, kib)
             stage = stages[first][:, j - first, :]
-            y = place("y%d" % j, [P, PACK, P], F32, WGS_T_AT + 12 + 2 * (j % 6))
+            y = place("y%d" % j, [P, PACK, P], F32, DAMP1_AT + 2 * (j % 6))
             woven = stage.rearrange("p (c i t) -> p c t i", i=PACK, t=PACK)
             if j < TURNED:
                 nc.scalar.activation(
@@ -561,7 +578,7 @@ def tile_list_airway_tree_step_kernel(
                 nc.sync.dma_start(out=out_words[:, cols], in_=y_c[:, cols].bitcast(I32))
 
         def late_parents(j):
-            part = place("sums1_%d" % j, [P, PACK, P], F32, (WEIGHTED_AT + 10, LOGS_AT + 0.625)[j % 2])
+            part = place("sums1_%d" % j, [P, PACK, P], F32, WEIGHTED_AT + 10 + 2 * (j % 2))
             for t in range(PACK):
                 parents(part[:, t, :], PACK + t, P * j, P)
             return part
@@ -572,8 +589,8 @@ def tile_list_airway_tree_step_kernel(
             open_tile(j)
         for j in range(tiles):
             m0 = P * j
-            stage = place("z_stage%d" % j, [P, PACK * P], BF16, WEIGHTED_AT + 12 + j % 2)
-            make_z(part[:], damp1[:, :, m0 : m0 + P], stage[:])
+            stage = place("z_stage%d" % j, [P, PACK * P], BF16, WEIGHTED_AT + 14 + j % 2)
+            make_z(part[:], factor[:, :, m0 : m0 + P], stage[:])
             if j + 1 < tiles:
                 part = late_parents(j + 1)
             quantize_z(1, stage[:], m0, P, Z_AT + 0.625 * j)

@@ -46,12 +46,13 @@ SUMS01_AT = 58
 H_AT = {3: 66, 2: 70, 4: 74, 5: 78, 6: 82, 7: 86, 1: 92}
 H0_AT = (90, 102 + EDGE)
 RAW_B_AT = 66 - EDGE
-DAMP1_AT = 66
+DAMP1_AT = 66 + EDGE
 WGS_T_AT = 98
 RAW_A_AT = 98 + EDGE
 DAMP01_AT = 114
 RAW_W3_AT = (122, 134)
-Z0_AT = 122
+Z0_AT = 122 - EDGE
+FACTOR_RUNS = ((0, 128, 128), (128, 384, 122), (512, 512, 114))
 SUMS23_AT = 130
 WOVEN0_AT = 130
 DAMP23_AT = 138
@@ -63,6 +64,8 @@ Z_PLAIN_AT = 178
 SMALL_AT = 202
 Z_AT = 207
 Y_Q_AT = 213
+W3_Q_AT = 177
+SUM_BANKS = ((0, 1), (2, 3), (4, 5), (6, 7), (1, 3), (0, 5), (2, 7), (4, 1))
 Y_RUNS = ((0, 4, 43), (4, 3, 40), (7, 1, 47))
 
 
@@ -79,8 +82,8 @@ def tile_list_airway_tree_step_kernel(
         def place(name, shape, dtype, kib):
             return pool.tile(shape, dtype, name=name, tag=name, bufs=1, align_bytes=64, offset=int(kib * KB))
 
-        def bank(name):
-            return psum.tile([P, BANK], F32, name=name, tag="bank", bufs=8)
+        def bank(name, i):
+            return psum.tile([P, BANK], F32, name=name, tag=name, bufs=1, offset=i * BANK * 4)
 
         lists = {}
         for name in ("offs", "offs2", "offs3", "offs4"):
@@ -186,9 +189,12 @@ def tile_list_airway_tree_step_kernel(
             nc.vector.tensor_copy(out=v_w[1][:, j0 : j0 + w], in_=tab_w[1][:].indirect(entries("offs", j0, w)))
         clear_page(2)
 
+        used = []
+
         def features(s, j0, w, out):
             cols = slice(j0, j0 + w)
-            acc = bank("acc")
+            acc = bank("acc%d_%d" % (s, j0), len(used) % 8)
+            used.append(acc)
             for a in range(2):
                 codes, scales = w1_q[a, s]
                 nc.tensor.matmul_mx(
@@ -360,17 +366,18 @@ def tile_list_airway_tree_step_kernel(
         weigh(3)
         plain_z(2)
         plain_z(3)
-        woven0 = place("woven0", [P, PAIRS, PACK], BF16, WOVEN0_AT)
+        woven0 = {}
         for m0, w in HALVES:
+            woven0[m0] = place("woven0_%d" % m0, [P, w, PACK], BF16, WOVEN0_AT + m0 * PACK * 2 / KB)
             nc.gpsimd.tensor_scalar(
-                out=woven0[:, m0 : m0 + w, :],
+                out=woven0[m0][:],
                 in0=z0[:, :, m0 : m0 + w].rearrange("p t m -> p m t"),
                 scalar1=1.0,
                 scalar2=0.0,
                 op0=ALU.mult,
                 op1=ALU.add,
             )
-        w2_s_dealt = place("w2_s_dealt", [P, 2 * N], U8, Z_PLAIN_AT)
+        w2_s_dealt = place("w2_s_dealt", [P, 2 * N], U8, Z_PLAIN_AT + 7)
         nc.gpsimd.tensor_copy(
             out=w2_s_dealt[:].rearrange("p (a t m) -> p a t m", a=2, t=PACK),
             in_=w2_s[:].rearrange("p (a m t) -> p a t m", a=2, t=PACK),
@@ -382,46 +389,58 @@ def tile_list_airway_tree_step_kernel(
         damp1 = place("damp1", [P, PACK, PAIRS], F32, DAMP1_AT)
         for t in range(PACK):
             damp[PACK + t] = damp1[:, t, :]
-        scatter_weighted(4)
-        scatter_weighted(5)
-        daughters(4, 0, PAIRS)
-        daughters(5, 0, PAIRS)
         most = PAIRS - PUT_OFF
         flat = damp1[:].rearrange("p t m -> p (t m)")
 
         def sigmoid_back(logs, first, count):
             nc.scalar.activation(out=flat[:, first : first + count], in_=logs, func=ACT.Sigmoid, scale=-2.0)
 
-        factor = place("factor", [P, PACK, PAIRS], F32, DAMP01_AT)
+        factors = [(m0, w, place("factor%d" % m0, [P, PACK, w], F32, kib)) for m0, w, kib in FACTOR_RUNS]
+
+        def factor(m0, w):
+            first, tile = [(f, tile) for f, count, tile in factors if f <= m0 < f + count][0]
+            return tile[:, :, m0 - first : m0 - first + w]
 
         def gz_scalar(logs, s, m0, w):
             nc.scalar.activation(
-                out=factor[:, s - PACK, m0 : m0 + w], in_=logs, func=ACT.Copy, scale=gz_sb[1][:, s - PACK : s - PACK + 1]
+                out=factor(m0, w)[:, s - PACK, :], in_=logs, func=ACT.Copy, scale=gz_sb[1][:, s - PACK : s - PACK + 1]
             )
 
         def gz_gpsimd(s, m0, w):
             nc.gpsimd.tensor_scalar(
-                out=factor[:, s - PACK, m0 : m0 + w], in0=damp[s][:, m0 : m0 + w],
+                out=factor(m0, w)[:, s - PACK, :], in0=damp[s][:, m0 : m0 + w],
                 scalar1=gz_sb[1][:, s - PACK : s - PACK + 1], scalar2=0.0, op0=ALU.mult, op1=ALU.add,
             )
 
-        logs = place("logs45", [P, PAIRS + most], F32, LOGS_AT)
-        logarithm(logs[:, 0:PAIRS], 4, 0, PAIRS)
-        logarithm(logs[:, PAIRS:], 5, 0, most)
-        sigmoid_back(logs[:], 0, PAIRS + most)
-        gz_gpsimd(4, 0, PAIRS)
-        logs = place("logs6", [P, PAIRS], F32, LOGS_AT + 2)
-        logarithm(logs[:, 0:PUT_OFF], 5, most, PUT_OFF)
+        def runs(end):
+            return [(m0, min(w, end - m0)) for m0, w, kib in FACTOR_RUNS]
+
+        scatter_weighted(4)
+        scatter_weighted(5)
+        daughters(4, 0, PAIRS)
+        logs = place("logs4", [P, most], F32, LOGS_AT)
+        logarithm(logs[:], 4, 0, most)
+        sigmoid_back(logs[:], 0, most)
+        for m0, w in runs(most):
+            gz_gpsimd(4, m0, w)
+        logs = place("logs56", [P, 2 * PAIRS], F32, LOGS_AT)
+        logarithm(logs[:, 0:PUT_OFF], 4, most, PUT_OFF)
         scatter_weighted(6)
+        daughters(5, 0, PAIRS)
         daughters(6, 0, PAIRS)
-        logarithm(logs[:, PUT_OFF:], 6, 0, most)
-        sigmoid_back(logs[:], PAIRS + most, PAIRS)
-        gz_gpsimd(5, 0, PAIRS)
-        gz_gpsimd(6, 0, most)
+        logarithm(logs[:, PUT_OFF : PUT_OFF + PAIRS], 5, 0, PAIRS)
+        logarithm(logs[:, PUT_OFF + PAIRS :], 6, 0, most)
+        sigmoid_back(logs[:, 0 : PUT_OFF + PAIRS], most, PUT_OFF + PAIRS)
+        sigmoid_back(logs[:, PUT_OFF + PAIRS :], 2 * PAIRS, most)
+        gz_gpsimd(4, most, PUT_OFF)
+        for m0, w in runs(PAIRS):
+            gz_gpsimd(5, m0, w)
         first7 = place("logs7_first", [P, PUT_OFF + P], F32, LOGS_AT + 2)
         next7 = place("logs7_next", [P, HALF - P], F32, LOGS_AT + 2.625)
-        last7 = place("logs7_last", [P, HALF], F32, LOGS_AT + 4.125)
+        last7 = place("logs7_last", [P, HALF], F32, LOGS_AT + 6)
         logarithm(first7[:, 0:PUT_OFF], 6, most, PUT_OFF)
+        for m0, w in runs(most):
+            gz_scalar(damp[6][:, m0 : m0 + w], 6, m0, w)
         scatter_weighted(7)
         for m0, w in LAST_PIECES:
             daughters(7, m0, w)
@@ -432,11 +451,13 @@ def tile_list_airway_tree_step_kernel(
                 logarithm(last7[:, m0 - HALF : m0 - HALF + w], 7, m0, w)
         sigmoid(first7[:])
         gz_scalar(first7[:, PUT_OFF:], 7, 0, P)
-        sigmoid(next7[:])
-        gz_scalar(next7[:], 7, P, HALF - P)
-        sigmoid(last7[:])
-        gz_scalar(last7[:], 7, HALF, HALF)
         gz_scalar(first7[:, 0:PUT_OFF], 6, most, PUT_OFF)
+        next_bare = place("bare7_next", [P, HALF - P], F32, LOGS_AT + 1.125)
+        nc.scalar.activation(out=next_bare[:], in_=next7[:], func=ACT.Sigmoid, scale=-2.0)
+        gz_scalar(next_bare[:], 7, P, HALF - P)
+        last_bare = place("bare7_last", [P, HALF], F32, LOGS_AT + 3.5)
+        nc.scalar.activation(out=last_bare[:], in_=last7[:], func=ACT.Sigmoid, scale=-2.0)
+        gz_scalar(last_bare[:], 7, HALF, HALF)
 
         z_q = {}
 
@@ -446,10 +467,10 @@ def tile_list_airway_tree_step_kernel(
                 z_q[b, m0 + i] = (codes[:, i : i + P].bitcast(FP8X4), scales[:, i : i + P])
 
         def quantize_woven(m0, kib):
-            quantize_z(0, woven0[:, m0 : m0 + HALF, :].rearrange("p m t -> p (m t)"), m0, HALF, kib)
+            quantize_z(0, woven0[m0][:].rearrange("p m t -> p (m t)"), m0, HALF, kib)
 
         quantize_woven(0, WEIGHTED_AT)
-        w3_c = place("w3_c", [P, 2, KP], U32, WEIGHTED_AT + 4)
+        w3_c = place("w3_c", [P, 2, KP], U32, W3_Q_AT)
         w3_s = place("w3_s", [P, 2, KP], U8, SMALL_AT + 3)
         for a in range(2):
             nc.vector.quantize_mx(out=w3_c[:, a, :].bitcast(FP8X4), scales=w3_s[:, a, :], in_=w3_bf[:, a, :])
@@ -493,7 +514,7 @@ def tile_list_airway_tree_step_kernel(
                     start=(b == 0 and t == 0), stop=(b == 1 and t == PACK - 1),
                 )
 
-        y_c = place("y_c", [P, PAIRS], U32, Y_Q_AT)
+        y_c = place("y_c", [P, PAIRS], U32, 114)
         y_s = place("y_s", [P, PAIRS], U8, Y_Q_AT + 4)
         out_rows = out_0.rearrange("(p t) m -> p t m", t=PACK)
         out_words = out_1[0].rearrange("p m t -> p (m t)").bitcast(I32)
@@ -506,8 +527,8 @@ def tile_list_airway_tree_step_kernel(
             form(*opened[j], b, P * j)
 
         def open_tile(j):
-            acc_b = bank("acc")
-            acc_a = bank("acc")
+            acc_b = bank("acc_b%d" % j, SUM_BANKS[j][0])
+            acc_a = bank("acc_a%d" % j, SUM_BANKS[j][1])
             opened[j] = (acc_a, acc_b)
             passes(j, 0)
 
@@ -524,7 +545,7 @@ def tile_list_airway_tree_step_kernel(
                     func=ACT.Copy,
                     scale=-1.0,
                 )
-                minus_y = bank("minus_y")
+                minus_y = bank("minus_y%d" % j, SUM_BANKS[j][0])
                 for k, term in enumerate((gate, minus_a)):
                     for t in range(PACK):
                         nc.tensor.matmul(
@@ -543,7 +564,7 @@ def tile_list_airway_tree_step_kernel(
             if j == first:
                 stages[first] = place("y_stage%d" % j, [P, count, PACK * P], BF16, kib)
             stage = stages[first][:, j - first, :]
-            y = place("y%d" % j, [P, PACK, P], F32, DAMP1_AT + 2 * (j % 6))
+            y = place("y%d" % j, [P, PACK, P], F32, {4: 118, 5: 120}.get(j, 66 + 2 * j))
             woven = stage.rearrange("p (c i t) -> p c t i", i=PACK, t=PACK)
             if j < TURNED:
                 nc.scalar.activation(
@@ -577,25 +598,29 @@ def tile_list_airway_tree_step_kernel(
                 )
                 nc.sync.dma_start(out=out_words[:, cols], in_=y_c[:, cols].bitcast(I32))
 
-        def late_parents(j):
-            part = place("sums1_%d" % j, [P, PACK, P], F32, WEIGHTED_AT + 10 + 2 * (j % 2))
-            for t in range(PACK):
-                parents(part[:, t, :], PACK + t, P * j, P)
-            return part
+        summed = {}
+
+        def late_parents(j, count, kib, slices):
+            if (j, count) not in summed:
+                summed[j, count] = place("sums1_%d" % j, [P, PACK, count * P], F32, kib)
+                for i in range(count):
+                    summed[j + i] = summed[j, count][:, :, P * i : P * (i + 1)]
+            for t in slices:
+                parents(summed[j, count][:, t, :], PACK + t, P * j, count * P)
 
         tiles = PAIRS // P
-        part = late_parents(0)
+        late_parents(0, 2, 173, range(PACK))
         for j in range(AHEAD):
             open_tile(j)
         for j in range(tiles):
             m0 = P * j
-            stage = place("z_stage%d" % j, [P, PACK * P], BF16, WEIGHTED_AT + 14 + j % 2)
-            make_z(part[:], factor[:, :, m0 : m0 + P], stage[:])
-            if j + 1 < tiles:
-                part = late_parents(j + 1)
+            stage = place("z_stage%d" % j, [P, PACK * P], BF16, 181 + j % 2 if j else 164.5)
+            make_z(summed[j], factor(m0, P), stage[:])
+            if j < tiles - 2:
+                late_parents(2 * (j // 2 + 1), 2, (128, 173, 128)[j // 2], (2 * (j % 2), 2 * (j % 2) + 1))
             quantize_z(1, stage[:], m0, P, Z_AT + 0.625 * j)
             if j == 0:
-                quantize_woven(HALF, LOGS_AT + 2.625)
+                quantize_woven(HALF, 164.5)
             passes(j, 1)
             empty_sums(j)
             if j > 0:

@@ -520,7 +520,7 @@ def tile_list_airway_tree_step_kernel(
         out_words = out_1[0].rearrange("p m t -> p (m t)").bitcast(I32)
         out_scales = out_2[0].bitcast(I32)
 
-        opened, gates, turned, stages = {}, {}, {}, {}
+        opened, gates, turned, stages, y_pair = {}, {}, {}, {}, {}
 
         def passes(j, b):
             form = passes_turned if j < TURNED else passes_upright
@@ -564,11 +564,16 @@ def tile_list_airway_tree_step_kernel(
             if j == first:
                 stages[first] = place("y_stage%d" % j, [P, count, PACK * P], BF16, kib)
             stage = stages[first][:, j - first, :]
-            y = place("y%d" % j, [P, PACK, P], F32, {4: 118, 5: 120}.get(j, 66 + 2 * j))
+            if j < TURNED:
+                y = place("y%d" % j, [P, PACK, P], F32, 66 + 2 * j)[:]
+            else:
+                if j % 2 == 0:
+                    y_pair[j] = place("y%d" % j, [P, PACK, 2 * P], F32, {4: 118, 6: 74}[j])
+                y = y_pair[j - j % 2][:, :, P * (j % 2) : P * (j % 2 + 1)]
             woven = stage.rearrange("p (c i t) -> p c t i", i=PACK, t=PACK)
             if j < TURNED:
                 nc.scalar.activation(
-                    out=y[:].rearrange("p t m -> p (t m)"), in_=turned[j][:], func=ACT.Copy, scale=-1.0
+                    out=y.rearrange("p t m -> p (t m)"), in_=turned[j][:], func=ACT.Copy, scale=-1.0
                 )
                 nc.scalar.activation(
                     out=woven,
@@ -578,17 +583,20 @@ def tile_list_airway_tree_step_kernel(
                 )
             else:
                 nc.vector.tensor_tensor(
-                    out=y[:].rearrange("p t m -> p (t m)"),
-                    in0=opened[j][0][:],
-                    in1=gates[j][:].rearrange("p t m -> p (t m)"),
+                    out=y,
+                    in0=opened[j][0][:].rearrange("p (t m) -> p t m", t=PACK),
+                    in1=gates[j][:],
                     op=ALU.subtract,
                 )
-                rows = y[:].rearrange("p t (c i) -> p c t i", i=PACK)
+                rows = y.rearrange("p t (c i) -> p c t i", i=PACK)
                 if j == tiles - 2:
                     nc.vector.tensor_copy(out=woven, in_=rows)
                 else:
                     nc.scalar.copy(out=woven, in_=rows)
-            nc.sync.dma_start(out=out_rows[:, :, m0 : m0 + P], in_=y[:])
+            if j < TURNED:
+                nc.sync.dma_start(out=out_rows[:, :, m0 : m0 + P], in_=y)
+            elif j % 2 == 1:
+                nc.sync.dma_start(out=out_rows[:, :, m0 - P : m0 + P], in_=y_pair[j - 1][:])
             if j == first + count - 1:
                 cols = slice(P * first, P * (first + count))
                 nc.vector.quantize_mx(
@@ -596,7 +604,8 @@ def tile_list_airway_tree_step_kernel(
                     scales=y_s[:, cols],
                     in_=stages[first][:].rearrange("p j c -> p (j c)"),
                 )
-                nc.sync.dma_start(out=out_words[:, cols], in_=y_c[:, cols].bitcast(I32))
+                queue = nc.scalar if j >= TURNED else nc.sync
+                queue.dma_start(out=out_words[:, cols], in_=y_c[:, cols].bitcast(I32))
 
         summed = {}
 

@@ -42,8 +42,8 @@ W2_DEALT_AT = 40
 W1_Q_AT = 42
 TAB_S_AT = 52
 WGS_AT = 54
-SUMS01_AT = 58
-H_AT = {3: 66, 2: 70, 4: 74, 5: 78, 6: 82, 7: 86, 1: 92}
+PARENTS01_AT = 58
+H_AT = {3: 66, 2: 70, 4: 222, 5: 78, 6: 82, 7: 86, 1: 92}
 H0_AT = (90, 102 + EDGE)
 RAW_B_AT = 66 - EDGE
 DAMP1_AT = 66 + EDGE
@@ -53,12 +53,15 @@ DAMP01_AT = 114
 RAW_W3_AT = (122, 134)
 Z0_AT = 122 - EDGE
 FACTOR_RUNS = ((0, 128, 128), (128, 384, 122), (512, 512, 114))
-SUMS23_AT = 130
+PARENTS23_AT = 130
 WOVEN0_AT = 130
 DAMP23_AT = 138
 W3_BF_AT = 146
 STAGE_B_AT = 154
-WEIGHTED_AT = 162
+WEIGHTED_EARLY_AT = {2: 154, 3: 158, 4: 218}
+SUM0_AT = 154
+SUMS123_AT = 226 - EDGE
+WEIGHTED_AT = 166
 REST_AT = (162 + EDGE, 166 + EDGE, 170 + EDGE, 174 + EDGE, 186, 190, 194, 198)
 Z_PLAIN_AT = 178
 SMALL_AT = 202
@@ -302,16 +305,35 @@ def tile_list_airway_tree_step_kernel(
             for t in range(PACK):
                 cols = slice(KP * a + P * t, KP * a + P * (t + 1))
                 w1_q[a, PACK + t] = (codes[:, cols], scales[:, cols])
-        two_slices(sums, "sums01", 0, SUMS01_AT)
+        fetched, weighted = {}, {}
+
+        def early_parents(s):
+            nc.vector.tensor_copy(out=fetched[s], in_=page_of(s)[:].indirect(lists["offs3"][:]))
+
+        def weigh(s):
+            factors = wgs_plain if s < PACK else wgs_t[s - PACK]
+            nc.gpsimd.tensor_tensor(out=weighted[s], in0=h_sb[s][:], in1=factors[:], op=ALU.mult)
+
+        def add_rest(s):
+            nc.gpsimd.tensor_tensor(out=sums[s], in0=fetched[s], in1=rest_sb[s][:], op=ALU.add)
+
+        def scatter_weighted(s):
+            nc.vector.tensor_copy(out=page_of(s)[:].indirect(lists["offs2"][:]), in_=weighted[s])
+
+        two_slices(fetched, "parents01", 0, PARENTS01_AT)
         for s in (0, 1):
-            parents(sums[s], s, 0, PAIRS)
+            early_parents(s)
         for s in (2, 3):
             whole_features(s)
+            weighted[s] = place("weighted%d" % s, [P, S], F32, WEIGHTED_EARLY_AT[s])[:]
+            weigh(s)
         w3_bf = place("stage_w3", [P, 2, PACK * KP], BF16, W3_BF_AT)
         for a in range(2):
             round_dealt(w3_raw[a], w3_bf[:, a, :])
         for s in range(PACK, 2 * PACK):
             whole_features(s)
+        weighted[4] = place("weighted4", [P, S], F32, WEIGHTED_EARLY_AT[4])[:]
+        weigh(4)
 
         def logarithm(logs, s, m0, w):
             nc.scalar.activation(out=logs, in_=damp[s][:, m0 : m0 + w], func=ACT.Ln, bias=LN_FLOOR)
@@ -333,10 +355,17 @@ def tile_list_airway_tree_step_kernel(
 
         damp_two(0)
         for s in (2, 3):
-            scatter(s)
-        two_slices(sums, "sums23", 2, SUMS23_AT)
+            scatter_weighted(s)
+        sums[0] = place("sum0", [P, PAIRS], F32, SUM0_AT)[:]
+        sums123 = place("sums123", [P, 3, PAIRS], F32, SUMS123_AT)
+        for s in (1, 2, 3):
+            sums[s] = sums123[:, s - 1, :]
+        for s in (0, 1):
+            add_rest(s)
+        two_slices(fetched, "parents23", 2, PARENTS23_AT)
         for s in (2, 3):
-            parents(sums[s], s, 0, PAIRS)
+            early_parents(s)
+            add_rest(s)
         two_slices(damp, "damp23", 2, DAMP23_AT)
         for s in (2, 3):
             daughters(s, 0, PAIRS)
@@ -347,23 +376,22 @@ def tile_list_airway_tree_step_kernel(
             in_=w2_w[:].bitcast(U16).rearrange("p (a m t) -> p a m t", a=2, t=PACK),
         )
 
-        weighted = place("weighted", [P, PACK, S], F32, WEIGHTED_AT)
+        weighted_late = place("weighted", [P, 3, S], F32, WEIGHTED_AT)
+        for s in (5, 6, 7):
+            weighted[s] = weighted_late[:, s - 5, :]
         z_plain = place("z_plain", [P, PACK, PAIRS], BF16, Z_PLAIN_AT)
         z0 = place("z0", [P, PACK, PAIRS], BF16, Z0_AT)
-
-        def weigh(t):
-            nc.gpsimd.tensor_tensor(out=weighted[:, t, :], in0=h_sb[PACK + t][:], in1=wgs_t[t][:], op=ALU.mult)
 
         def plain_z(s):
             nc.gpsimd.tensor_tensor(out=z_plain[:, s, :], in0=sums[s], in1=damp[s], op=ALU.mult)
             for t in range(PACK):
                 nc.sync.dma_start(out=z0[32 * s : 32 * (s + 1), t, :], in_=z_plain[t:P:PACK, s, :])
 
-        for t in range(3):
-            weigh(t)
+        weigh(5)
+        weigh(6)
         plain_z(0)
         plain_z(1)
-        weigh(3)
+        weigh(7)
         plain_z(2)
         plain_z(3)
         woven0 = {}
@@ -382,9 +410,6 @@ def tile_list_airway_tree_step_kernel(
             out=w2_s_dealt[:].rearrange("p (a t m) -> p a t m", a=2, t=PACK),
             in_=w2_s[:].rearrange("p (a m t) -> p a t m", a=2, t=PACK),
         )
-
-        def scatter_weighted(s):
-            nc.vector.tensor_copy(out=page_of(s)[:].indirect(lists["offs2"][:]), in_=weighted[:, s - PACK, :])
 
         damp1 = place("damp1", [P, PACK, PAIRS], F32, DAMP1_AT)
         for t in range(PACK):
@@ -623,13 +648,13 @@ def tile_list_airway_tree_step_kernel(
             open_tile(j)
         for j in range(tiles):
             m0 = P * j
-            stage = place("z_stage%d" % j, [P, PACK * P], BF16, 181 + j % 2 if j else 164.5)
+            stage = place("z_stage%d" % j, [P, PACK * P], BF16, 181 + j % 2 if j else WEIGHTED_AT + 2.5)
             make_z(summed[j], factor(m0, P), stage[:])
             if j < tiles - 2:
                 late_parents(2 * (j // 2 + 1), 2, (128, 173, 128)[j // 2], (2 * (j % 2), 2 * (j % 2) + 1))
             quantize_z(1, stage[:], m0, P, Z_AT + 0.625 * j)
             if j == 0:
-                quantize_woven(HALF, 164.5)
+                quantize_woven(HALF, WEIGHTED_AT + 2.5)
             passes(j, 1)
             empty_sums(j)
             if j > 0:

@@ -68,8 +68,9 @@ SMALL_AT = 202
 Z_AT = 207
 Y_Q_AT = 213
 W3_Q_AT = 177
+GATE_AT = (98, 100, 102, 98, 110, 102, 98, 100)
 SUM_BANKS = ((0, 1), (2, 3), (4, 5), (6, 7), (1, 3), (0, 5), (2, 7), (4, 1))
-Y_RUNS = ((0, 4, 43), (4, 3, 40), (7, 1, 47))
+Y_RUNS = ((0, 4, 43, 114), (4, 2, 48, 100), (6, 2, 50, 116))
 
 
 def tile_list_airway_tree_step_kernel(
@@ -539,7 +540,6 @@ def tile_list_airway_tree_step_kernel(
                     start=(b == 0 and t == 0), stop=(b == 1 and t == PACK - 1),
                 )
 
-        y_c = place("y_c", [P, PAIRS], U32, 114)
         y_s = place("y_s", [P, PAIRS], U8, Y_Q_AT + 4)
         out_rows = out_0.rearrange("(p t) m -> p t m", t=PACK)
         out_words = out_1[0].rearrange("p m t -> p (m t)").bitcast(I32)
@@ -559,7 +559,7 @@ def tile_list_airway_tree_step_kernel(
 
         def empty_sums(j):
             acc_a, acc_b = opened[j]
-            gate = place("gate%d" % j, [P, PACK, P], F32, WGS_T_AT + 2 * (j % 3))
+            gate = place("gate%d" % j, [P, PACK, P], F32, GATE_AT[j])
             nc.scalar.activation(out=gate[:].rearrange("p t m -> p (t m)"), in_=acc_b[:], func=ACT.Silu)
             gates[j] = gate
             if j < TURNED:
@@ -583,54 +583,60 @@ def tile_list_airway_tree_step_kernel(
                         )
                 turned[j] = minus_y
 
-        def finish_tile(j):
+        tiles = PAIRS // P
+        y_of = {}
+
+        def float_rows(j):
             m0 = P * j
-            first, count, kib = [run for run in Y_RUNS if run[0] <= j < run[0] + run[1]][0]
+            if j < TURNED:
+                y_of[j] = place("y%d" % j, [P, PACK, P], F32, 66 + 2 * j)[:]
+                nc.scalar.activation(
+                    out=y_of[j].rearrange("p t m -> p (t m)"), in_=turned[j][:], func=ACT.Copy, scale=-1.0
+                )
+                nc.sync.dma_start(out=out_rows[:, :, m0 : m0 + P], in_=y_of[j])
+                return
+            if j % 2 == 0:
+                y_pair[j] = place("y%d" % j, [P, PACK, 2 * P], F32, {4: 181, 6: 74}[j])
+            y_of[j] = y_pair[j - j % 2][:, :, P * (j % 2) : P * (j % 2 + 1)]
+            nc.vector.tensor_tensor(
+                out=y_of[j],
+                in0=opened[j][0][:].rearrange("p (t m) -> p t m", t=PACK),
+                in1=gates[j][:],
+                op=ALU.subtract,
+            )
+            if j % 2 == 1:
+                nc.sync.dma_start(out=out_rows[:, :, m0 - P : m0 + P], in_=y_pair[j - 1][:])
+
+        def packed_rows(j):
+            first, count, kib, codes_kib = [run for run in Y_RUNS if run[0] <= j < run[0] + run[1]][0]
             if j == first:
                 stages[first] = place("y_stage%d" % j, [P, count, PACK * P], BF16, kib)
-            stage = stages[first][:, j - first, :]
+            woven = stages[first][:, j - first, :].rearrange("p (c i t) -> p c t i", i=PACK, t=PACK)
             if j < TURNED:
-                y = place("y%d" % j, [P, PACK, P], F32, 66 + 2 * j)[:]
-            else:
-                if j % 2 == 0:
-                    y_pair[j] = place("y%d" % j, [P, PACK, 2 * P], F32, {4: 118, 6: 74}[j])
-                y = y_pair[j - j % 2][:, :, P * (j % 2) : P * (j % 2 + 1)]
-            woven = stage.rearrange("p (c i t) -> p c t i", i=PACK, t=PACK)
-            if j < TURNED:
-                nc.scalar.activation(
-                    out=y.rearrange("p t m -> p (t m)"), in_=turned[j][:], func=ACT.Copy, scale=-1.0
-                )
                 nc.scalar.activation(
                     out=woven,
                     in_=turned[j][:].rearrange("p (t c i) -> p c t i", t=PACK, i=PACK),
                     func=ACT.Copy,
                     scale=-1.0,
                 )
-            else:
-                nc.vector.tensor_tensor(
-                    out=y,
-                    in0=opened[j][0][:].rearrange("p (t m) -> p t m", t=PACK),
-                    in1=gates[j][:],
-                    op=ALU.subtract,
+            elif j < tiles - 2:
+                nc.gpsimd.tensor_scalar(
+                    out=stages[first][:, j - first, :].rearrange("p (m t) -> p m t", t=PACK),
+                    in0=y_of[j].rearrange("p t m -> p m t"),
+                    scalar1=1.0, scalar2=0.0, op0=ALU.mult, op1=ALU.add,
                 )
-                rows = y.rearrange("p t (c i) -> p c t i", i=PACK)
-                if j == tiles - 2:
-                    nc.vector.tensor_copy(out=woven, in_=rows)
-                else:
-                    nc.scalar.copy(out=woven, in_=rows)
-            if j < TURNED:
-                nc.sync.dma_start(out=out_rows[:, :, m0 : m0 + P], in_=y)
-            elif j % 2 == 1:
-                nc.sync.dma_start(out=out_rows[:, :, m0 - P : m0 + P], in_=y_pair[j - 1][:])
+            else:
+                nc.scalar.copy(out=woven, in_=y_of[j].rearrange("p t (c i) -> p c t i", i=PACK))
             if j == first + count - 1:
                 cols = slice(P * first, P * (first + count))
+                y_c = place("y_c%d" % first, [P, P * count], U32, codes_kib)
                 nc.vector.quantize_mx(
-                    out=y_c[:, cols].bitcast(FP8X4),
+                    out=y_c[:].bitcast(FP8X4),
                     scales=y_s[:, cols],
                     in_=stages[first][:].rearrange("p j c -> p (j c)"),
                 )
                 queue = nc.scalar if j >= TURNED else nc.sync
-                queue.dma_start(out=out_words[:, cols], in_=y_c[:, cols].bitcast(I32))
+                queue.dma_start(out=out_words[:, cols], in_=y_c[:].bitcast(I32))
 
         summed = {}
 
@@ -642,7 +648,6 @@ def tile_list_airway_tree_step_kernel(
             for t in slices:
                 parents(summed[j, count][:, t, :], PACK + t, P * j, count * P)
 
-        tiles = PAIRS // P
         late_parents(0, 2, 173, range(PACK))
         for j in range(AHEAD):
             open_tile(j)
@@ -657,11 +662,15 @@ def tile_list_airway_tree_step_kernel(
                 quantize_woven(HALF, WEIGHTED_AT + 2.5)
             passes(j, 1)
             empty_sums(j)
-            if j > 0:
-                finish_tile(j - 1)
+            if 0 < j <= TURNED:
+                float_rows(j - 1)
+                packed_rows(j - 1)
             if 0 < j <= tiles - AHEAD:
                 open_tile(j + AHEAD - 1)
-        finish_tile(tiles - 1)
+        for j in range(TURNED, tiles):
+            float_rows(j)
+        for j in range(TURNED, tiles):
+            packed_rows(j)
         for q in range(4):
             queue = nc.sync if q % 2 == 0 else nc.scalar
             queue.dma_start(out=out_scales[4 * q : 4 * q + 4, :], in_=y_s[32 * q : 32 * q + 4, :].bitcast(I32))

@@ -545,7 +545,7 @@ def tile_list_airway_tree_step_kernel(
         out_words = out_1[0].rearrange("p m t -> p (m t)").bitcast(I32)
         out_scales = out_2[0].bitcast(I32)
 
-        opened, gates, turned, stages, y_pair = {}, {}, {}, {}, {}
+        opened, gates, turned, stages, y_pair, sum_a = {}, {}, {}, {}, {}, {}
 
         def passes(j, b):
             form = passes_turned if j < TURNED else passes_upright
@@ -562,6 +562,9 @@ def tile_list_airway_tree_step_kernel(
             gate = place("gate%d" % j, [P, PACK, P], F32, GATE_AT[j])
             nc.scalar.activation(out=gate[:].rearrange("p t m -> p (t m)"), in_=acc_b[:], func=ACT.Silu)
             gates[j] = gate
+            if j == TURNED:
+                sum_a[j] = place("sum_a%d" % j, [P, PACK, P], F32, WGS_T_AT + 6 + 2 * (j % 3))
+                nc.scalar.copy(out=sum_a[j][:].rearrange("p t m -> p (t m)"), in_=acc_a[:])
             if j < TURNED:
                 minus_a = place("minus_a%d" % j, [P, PACK, P], F32, WGS_T_AT + 6 + 2 * (j % 3))
                 nc.scalar.activation(
@@ -598,12 +601,15 @@ def tile_list_airway_tree_step_kernel(
             if j % 2 == 0:
                 y_pair[j] = place("y%d" % j, [P, PACK, 2 * P], F32, {4: 181, 6: 74}[j])
             y_of[j] = y_pair[j - j % 2][:, :, P * (j % 2) : P * (j % 2 + 1)]
-            nc.vector.tensor_tensor(
-                out=y_of[j],
-                in0=opened[j][0][:].rearrange("p (t m) -> p t m", t=PACK),
-                in1=gates[j][:],
-                op=ALU.subtract,
-            )
+            if j == TURNED:
+                nc.gpsimd.tensor_tensor(out=y_of[j], in0=sum_a[j][:], in1=gates[j][:], op=ALU.subtract)
+            else:
+                nc.vector.tensor_tensor(
+                    out=y_of[j],
+                    in0=opened[j][0][:].rearrange("p (t m) -> p t m", t=PACK),
+                    in1=gates[j][:],
+                    op=ALU.subtract,
+                )
             if j % 2 == 1:
                 nc.sync.dma_start(out=out_rows[:, :, m0 - P : m0 + P], in_=y_pair[j - 1][:])
 

@@ -70,7 +70,7 @@ Y_Q_AT = 213
 W3_Q_AT = 177
 GATE_AT = (98, 100, 102, 98, 110, 102, 98, 100)
 SUM_BANKS = ((0, 1), (2, 3), (4, 5), (6, 7), (1, 3), (0, 5), (2, 7), (4, 1))
-Y_RUNS = ((0, 4, 43, 114), (4, 2, 48, 100), (6, 2, 50, 116))
+Y_RUNS = ((0, 4, 43, 114), (4, 3, 48, 100), (7, 1, 51, 48))
 
 
 def tile_list_airway_tree_step_kernel(
@@ -485,6 +485,7 @@ def tile_list_airway_tree_step_kernel(
         nc.scalar.activation(out=last_bare[:], in_=last7[:], func=ACT.Sigmoid, scale=-2.0)
         gz_scalar(last_bare[:], 7, HALF, HALF)
 
+        tiles = PAIRS // P
         z_q = {}
 
         def quantize_z(b, stage, m0, w, kib):
@@ -522,7 +523,7 @@ def tile_list_airway_tree_step_kernel(
                 start=(b == 0), stop=(b == 1),
             )
 
-        def passes_upright(acc_a, acc_b, b, m0):
+        def passes_w3(acc_b, b, m0):
             codes, scales = z_q[b, m0]
             for t in range(PACK):
                 nc.tensor.matmul_mx(
@@ -531,6 +532,9 @@ def tile_list_airway_tree_step_kernel(
                     rhs=codes, rhs_scale=scales,
                     start=(b == 0 and t == 0), stop=(b == 1 and t == PACK - 1),
                 )
+
+        def passes_w2(acc_a, b, m0):
+            codes, scales = z_q[b, m0]
             for t in range(PACK):
                 c0 = N * b + P * t
                 nc.tensor.matmul_mx(
@@ -548,8 +552,15 @@ def tile_list_airway_tree_step_kernel(
         opened, gates, turned, stages, y_pair, sum_a = {}, {}, {}, {}, {}, {}
 
         def passes(j, b):
-            form = passes_turned if j < TURNED else passes_upright
-            form(*opened[j], b, P * j)
+            acc_a, acc_b = opened[j]
+            if j < TURNED:
+                passes_turned(acc_a, acc_b, b, P * j)
+                return
+            passes_w3(acc_b, b, P * j)
+            if (j, b) == (tiles - 1, 1):
+                passes_w2(opened[j - 1][0], b, P * (j - 1))
+            if (j, b) != (tiles - 2, 1):
+                passes_w2(acc_a, b, P * j)
 
         def open_tile(j):
             acc_b = bank("acc_b%d" % j, SUM_BANKS[j][0])
@@ -557,10 +568,16 @@ def tile_list_airway_tree_step_kernel(
             opened[j] = (acc_a, acc_b)
             passes(j, 0)
 
+        def column_runs(j):
+            return (slice(0, P // 2), slice(P // 2, P)) if j == tiles - 1 else (slice(0, P),)
+
         def empty_sums(j):
             acc_a, acc_b = opened[j]
             gate = place("gate%d" % j, [P, PACK, P], F32, GATE_AT[j])
-            nc.scalar.activation(out=gate[:].rearrange("p t m -> p (t m)"), in_=acc_b[:], func=ACT.Silu)
+            for cols in column_runs(j):
+                nc.scalar.activation(
+                    out=gate[:, :, cols], in_=acc_b[:].rearrange("p (t m) -> p t m", t=PACK)[:, :, cols], func=ACT.Silu
+                )
             gates[j] = gate
             if j == TURNED:
                 sum_a[j] = place("sum_a%d" % j, [P, PACK, P], F32, WGS_T_AT + 6 + 2 * (j % 3))
@@ -586,7 +603,6 @@ def tile_list_airway_tree_step_kernel(
                         )
                 turned[j] = minus_y
 
-        tiles = PAIRS // P
         y_of = {}
 
         def float_rows(j):
@@ -604,17 +620,25 @@ def tile_list_airway_tree_step_kernel(
             if j == TURNED:
                 nc.gpsimd.tensor_tensor(out=y_of[j], in0=sum_a[j][:], in1=gates[j][:], op=ALU.subtract)
             else:
-                nc.vector.tensor_tensor(
-                    out=y_of[j],
-                    in0=opened[j][0][:].rearrange("p (t m) -> p t m", t=PACK),
-                    in1=gates[j][:],
-                    op=ALU.subtract,
-                )
+                for cols in column_runs(j):
+                    nc.vector.tensor_tensor(
+                        out=y_of[j][:, :, cols],
+                        in0=opened[j][0][:].rearrange("p (t m) -> p t m", t=PACK)[:, :, cols],
+                        in1=gates[j][:, :, cols],
+                        op=ALU.subtract,
+                    )
             if j % 2 == 1:
                 nc.sync.dma_start(out=out_rows[:, :, m0 - P : m0 + P], in_=y_pair[j - 1][:])
 
+        def run_of(j):
+            return [run for run in Y_RUNS if run[0] <= j < run[0] + run[1]][0]
+
         def packed_rows(j):
-            first, count, kib, codes_kib = [run for run in Y_RUNS if run[0] <= j < run[0] + run[1]][0]
+            round_rows(j)
+            pack_run(j)
+
+        def round_rows(j):
+            first, count, kib, codes_kib = run_of(j)
             if j == first:
                 stages[first] = place("y_stage%d" % j, [P, count, PACK * P], BF16, kib)
             woven = stages[first][:, j - first, :].rearrange("p (c i t) -> p c t i", i=PACK, t=PACK)
@@ -625,7 +649,9 @@ def tile_list_airway_tree_step_kernel(
                     func=ACT.Copy,
                     scale=-1.0,
                 )
-            elif j < tiles - 2:
+            elif j == tiles - 1:
+                nc.vector.tensor_copy(out=woven, in_=y_of[j].rearrange("p t (c i) -> p c t i", i=PACK))
+            elif j == TURNED:
                 nc.gpsimd.tensor_scalar(
                     out=stages[first][:, j - first, :].rearrange("p (m t) -> p m t", t=PACK),
                     in0=y_of[j].rearrange("p t m -> p m t"),
@@ -633,6 +659,9 @@ def tile_list_airway_tree_step_kernel(
                 )
             else:
                 nc.scalar.copy(out=woven, in_=y_of[j].rearrange("p t (c i) -> p c t i", i=PACK))
+
+        def pack_run(j):
+            first, count, kib, codes_kib = run_of(j)
             if j == first + count - 1:
                 cols = slice(P * first, P * (first + count))
                 y_c = place("y_c%d" % first, [P, P * count], U32, codes_kib)
@@ -675,8 +704,10 @@ def tile_list_airway_tree_step_kernel(
                 open_tile(j + AHEAD - 1)
         for j in range(TURNED, tiles):
             float_rows(j)
-        for j in range(TURNED, tiles):
+        round_rows(tiles - 1)
+        for j in range(TURNED, tiles - 1):
             packed_rows(j)
+        pack_run(tiles - 1)
         for q in range(4):
             queue = nc.sync if q % 2 == 0 else nc.scalar
             queue.dma_start(out=out_scales[4 * q : 4 * q + 4, :], in_=y_s[32 * q : 32 * q + 4, :].bitcast(I32))

@@ -69,6 +69,8 @@ Z_AT = 207
 Y_Q_AT = 213
 W3_Q_AT = 177
 GATE_AT = (98, 100, 102, 98, 110, 102, 98, 100)
+STORE_RUNS = ((4, 1, 52.5), (5, 2, 54.5), (7, 1, 74))
+LAST_STAGE_AT = 54
 SUM_BANKS = ((0, 1), (2, 3), (4, 5), (6, 7), (1, 3), (0, 5), (2, 7), (4, 1))
 Y_RUNS = ((0, 4, 43, 114), (4, 3, 48, 100), (7, 1, 51, 48))
 
@@ -614,9 +616,10 @@ def tile_list_airway_tree_step_kernel(
                 )
                 nc.sync.dma_start(out=out_rows[:, :, m0 : m0 + P], in_=y_of[j])
                 return
-            if j % 2 == 0:
-                y_pair[j] = place("y%d" % j, [P, PACK, 2 * P], F32, {4: 181, 6: 74}[j])
-            y_of[j] = y_pair[j - j % 2][:, :, P * (j % 2) : P * (j % 2 + 1)]
+            first, count, kib = [run for run in STORE_RUNS if run[0] <= j < run[0] + run[1]][0]
+            if j == first:
+                y_pair[j] = place("y%d" % j, [P, PACK, count * P], F32, kib)
+            y_of[j] = y_pair[first][:, :, P * (j - first) : P * (j - first + 1)]
             if j == TURNED:
                 nc.gpsimd.tensor_tensor(out=y_of[j], in0=sum_a[j][:], in1=gates[j][:], op=ALU.subtract)
             else:
@@ -627,8 +630,8 @@ def tile_list_airway_tree_step_kernel(
                         in1=gates[j][:, :, cols],
                         op=ALU.subtract,
                     )
-            if j % 2 == 1:
-                nc.sync.dma_start(out=out_rows[:, :, m0 - P : m0 + P], in_=y_pair[j - 1][:])
+            if j == first + count - 1:
+                nc.sync.dma_start(out=out_rows[:, :, P * first : P * (first + count)], in_=y_pair[first][:])
 
         def run_of(j):
             return [run for run in Y_RUNS if run[0] <= j < run[0] + run[1]][0]
@@ -688,7 +691,7 @@ def tile_list_airway_tree_step_kernel(
             open_tile(j)
         for j in range(tiles):
             m0 = P * j
-            stage = place("z_stage%d" % j, [P, PACK * P], BF16, 181 + j % 2 if j else WEIGHTED_AT + 2.5)
+            stage = place("z_stage%d" % j, [P, PACK * P], BF16, {0: WEIGHTED_AT + 2.5, tiles - 1: LAST_STAGE_AT}.get(j, 181 + j % 2))
             make_z(summed[j], factor(m0, P), stage[:])
             if j < tiles - 2:
                 late_parents(2 * (j // 2 + 1), 2, (128, 173, 128)[j // 2], (2 * (j % 2), 2 * (j % 2) + 1))

@@ -27,7 +27,7 @@ QUARTER = 256
 HALF = 512
 HALVES = ((0, HALF), (HALF, HALF))
 AHEAD = 4
-TURNED = 4
+TURNED = 3
 PUT_OFF = 32
 LAST_PIECES = ((0, 512), (512, 256), (768, 256))
 EDGE = 1 / 16
@@ -68,11 +68,11 @@ SMALL_AT = 202
 Z_AT = 207
 Y_Q_AT = 213
 W3_Q_AT = 177
-GATE_AT = (98, 100, 102, 98, 110, 102, 98, 100)
-STORE_RUNS = ((4, 1, 52.5), (5, 2, 54.5), (7, 1, 74))
+GATE_AT = (98, 100, 102, 98, 110, 102, 112, 100)
+STORE_RUNS = ((3, 3, 52.5), (6, 2, 74))
 LAST_STAGE_AT = 54
-SUM_BANKS = ((0, 1), (2, 3), (4, 5), (6, 7), (1, 3), (0, 5), (2, 7), (4, 1))
-Y_RUNS = ((0, 4, 43, 114), (4, 3, 48, 100), (7, 1, 51, 48))
+SUM_BANKS = ((0, 1), (2, 3), (4, 5), (6, 7), (1, 3), (0, 5), (2, 6), (7, 4))
+Y_RUNS = ((0, 3, 43, 114), (3, 4, 177, 100), (7, 1, 51, 177))
 
 
 def tile_list_airway_tree_step_kernel(
@@ -652,8 +652,6 @@ def tile_list_airway_tree_step_kernel(
                     func=ACT.Copy,
                     scale=-1.0,
                 )
-            elif j == tiles - 1:
-                nc.vector.tensor_copy(out=woven, in_=y_of[j].rearrange("p t (c i) -> p c t i", i=PACK))
             elif j == TURNED:
                 nc.gpsimd.tensor_scalar(
                     out=stages[first][:, j - first, :].rearrange("p (m t) -> p m t", t=PACK),
@@ -707,10 +705,8 @@ def tile_list_airway_tree_step_kernel(
                 open_tile(j + AHEAD - 1)
         for j in range(TURNED, tiles):
             float_rows(j)
-        round_rows(tiles - 1)
-        for j in range(TURNED, tiles - 1):
+        for j in range(TURNED, tiles):
             packed_rows(j)
-        pack_run(tiles - 1)
         for q in range(4):
             queue = nc.sync if q % 2 == 0 else nc.scalar
             queue.dma_start(out=out_scales[4 * q : 4 * q + 4, :], in_=y_s[32 * q : 32 * q + 4, :].bitcast(I32))

from contextlib import ExitStack

import concourse.mybir as mybir
from concourse.masks import make_identity

K, T, S, H, T2, PAIRS, N = 1024, 2048, 1024, 1024, 2048, 1024, 512
FLOPS = 2 * K * H * S + 2 * 2 * H * N * PAIRS

F32 = mybir.dt.float32
BF16 = mybir.dt.bfloat16
I32 = mybir.dt.int32
U32 = mybir.dt.uint32
U16 = mybir.dt.uint16
U8 = mybir.dt.uint8
FP8X4 = mybir.dt.float8_e4m3fn_x4
FP4X4 = mybir.dt.float4_e2m1fn_x4
ACT = mybir.ActivationFunctionType
ALU = mybir.AluOpType

P = 128
PACK = 4
KP = P * PACK
BANK = 512
KB = 1024
LN_FLOOR = 2.0 ** -60
QUARTER = 256
HALF = 512
HALVES = ((0, HALF), (HALF, HALF))
AHEAD = 4
TURNED = 3
PUT_OFF = 32
LAST_PIECES = ((0, 512), (512, 256), (768, 256))
EDGE = 1 / 16

PAGE_AT = (0, 8, 16, 24)
TAB_AT = (186, 16)
STAGE_AT = (24, 26, 28)
V_AT = 32
V_S_AT = 40
LOGS_AT = 32
W2_DEALT_AT = 40
W1_Q_AT = 42
TAB_S_AT = 52
WGS_AT = 54
PARENTS01_AT = 58
H_AT = {3: 66, 2: 70, 4: 222, 5: 78, 6: 82, 7: 86, 1: 92}
H0_AT = (90, 102 + EDGE)
RAW_B_AT = 66 - EDGE
DAMP1_AT = 66 + EDGE
WGS_T_AT = 98
RAW_A_AT = 98 + EDGE
DAMP01_AT = 114
RAW_W3_AT = (122, 134)
Z0_AT = 122 - EDGE
FACTOR_RUNS = ((0, 128, 128), (128, 384, 122), (512, 512, 114))
PARENTS23_AT = 130
WOVEN0_AT = 130
DAMP23_AT = 138
W3_BF_AT = 146
STAGE_B_AT = 154
WEIGHTED_EARLY_AT = {2: 154, 3: 158, 4: 218}
SUM0_AT = 154
SUMS123_AT = 226 - EDGE
WEIGHTED_AT = 166
REST_AT = (162 + EDGE, 166 + EDGE, 170 + EDGE, 174 + EDGE, 186, 190, 194, 198)
Z_PLAIN_AT = 178
SMALL_AT = 202
Z_AT = 207
Y_Q_AT = 213
W3_Q_AT = 177
GATE_AT = (98, 100, 102, 98, 110, 102, 112, 100)
STORE_RUNS = ((3, 3, 52.5), (6, 2, 74))
LAST_STAGE_AT = 54
SUM_BANKS = ((0, 1), (2, 3), (4, 5), (6, 7), (1, 3), (0, 5), (2, 6), (7, 4))
Y_RUNS = ((0, 3, 43, 114), (3, 4, 177, 100), (7, 1, 51, 177))


def tile_list_airway_tree_step_kernel(
    tc, tab_words, tab_scales, offs, w1, wgs, offs2, offs3, offs4, rest, gz,
    w2_words, w2_scales, w3, out_0, out_1, out_2,
):
    nc = tc.nc
    with ExitStack() as ctx:
        held = ctx.enter_context(tc.tile_pool(name="held", bufs=1))
        pool = ctx.enter_context(tc.tile_pool(name="pool", bufs=1))
        psum = ctx.enter_context(tc.psum_pool(name="psum", bufs=1))

        def place(name, shape, dtype, kib):
            return pool.tile(shape, dtype, name=name, tag=name, bufs=1, align_bytes=64, offset=int(kib * KB))

        def bank(name, i):
            return psum.tile([P, BANK], F32, name=name, tag=name, bufs=1, offset=i * BANK * 4)

        lists = {}
        for name in ("offs", "offs2", "offs3", "offs4"):
            lists[name] = held.tile([P, S // 16], U16, name=name)

        def entries(name, j0, w):
            return lists[name][:, j0 // 16 : (j0 + w) // 16]

        pages = [None] * PACK

        def clear_page(i):
            pages[i] = place("page%d" % i, [P, T2], F32, PAGE_AT[i])
            nc.gpsimd.memset(pages[i][:].bitcast(I32), 0)

        tab_s = place("tab_s", [P, T], U8, TAB_S_AT)
        w2_s = place("w2_s", [P, 2 * N], U8, SMALL_AT + 2)
        ident = place("ident", [P, P], F32, SMALL_AT + 4)
        nc.gpsimd.memset(tab_s[:].bitcast(I32), 0)
        clear_page(0)
        nc.gpsimd.memset(w2_s[:].bitcast(I32), 0)
        make_identity(nc, ident[:])
        clear_page(1)

        def load_weight(w, a, c0, width, name, kib):
            raw = place(name, [P, PACK, width], F32, kib)
            nc.sync.dma_start(
                out=raw[:],
                in_=w[KP * a : KP * (a + 1), c0 : c0 + width].rearrange("(p j) c -> p j c", j=PACK),
            )
            return raw

        def round_plain(raw, stage):
            nc.scalar.copy(
                out=stage.rearrange("p (c i j) -> p c j i", i=PACK, j=PACK),
                in_=raw[:].rearrange("p j (c i) -> p c j i", i=PACK),
            )

        def round_dealt(raw, stage):
            nc.scalar.copy(
                out=stage.rearrange("p (t m j) -> p m j t", t=PACK, j=PACK),
                in_=raw[:].rearrange("p j (m t) -> p m j t", t=PACK),
            )

        def quantize(stage, words, name, kib):
            codes = place(name + "_c", [P, words], U32, kib)
            scales = place(name + "_s", [P, words], U8, kib + words * 4 / KB)
            nc.vector.quantize_mx(out=codes[:].bitcast(FP8X4), scales=scales[:], in_=stage)
            return codes, scales

        def load_table(a):
            tw = place("tab_w%d" % a, [P, T], U32, TAB_AT[a])
            nc.sync.dma_start(out=tw[:].bitcast(I32), in_=tab_words[a].rearrange("p t i -> p (t i)").bitcast(I32))
            return tw

        nc.sync.dma_start(lists["offs"][:], offs)
        tab_s_dram = tab_scales.bitcast(I32)
        for q in range(4):
            nc.sync.dma_start(
                out=tab_s[32 * q : 32 * q + 8, :].bitcast(I32),
                in_=tab_s_dram[:, 4 * q : 4 * q + 4, :],
            )
        raw_s0, tab_w = [], []
        for a in range(2):
            raw_s0.append(load_weight(w1, a, 0, P, "raw_s0_%d" % a, RAW_A_AT + 2 * a))
            tab_w.append(load_table(a))
        nc.sync.dma_start(lists["offs2"][:], offs2)
        wgs_plain = place("wgs_plain", [P, S], F32, WGS_AT)
        nc.sync.dma_start(out=wgs_plain[:], in_=wgs)
        raw_s1 = [load_weight(w1, a, P, P, "raw_s1_%d" % a, RAW_A_AT + 4 + 2 * a) for a in range(2)]
        raw_s23 = [load_weight(w1, a, 2 * P, 2 * P, "raw_s23_%d" % a, RAW_A_AT + 8 + 4 * a) for a in range(2)]
        raw_b = [load_weight(w1, a, KP, KP, "raw_b_%d" % a, RAW_B_AT + 8 - 8 * a) for a in range(2)]
        nc.sync.dma_start(lists["offs4"][:], offs4)
        nc.sync.dma_start(lists["offs3"][:], offs3)

        rest_dealt = rest[KP : 2 * KP, :].rearrange("(p t) m -> t p m", t=PACK)
        rest_sb = {}

        def load_rest(s):
            rest_sb[s] = place("rest%d" % s, [P, PAIRS], F32, REST_AT[s])
            rows = rest[P * s : P * (s + 1), :] if s < PACK else rest_dealt[s - PACK]
            nc.sync.dma_start(out=rest_sb[s][:], in_=rows)

        v_s = place("v_s", [P, S], U8, V_S_AT)
        nc.vector.tensor_copy(out=v_s[:], in_=tab_s[:].indirect(lists["offs"][:]))
        v_w = [place("v_w%d" % a, [P, S], U32, V_AT + 4 * a) for a in range(2)]
        nc.vector.tensor_copy(out=v_w[0][:], in_=tab_w[0][:].indirect(lists["offs"][:]))

        w1_q = {}

        def plain_weights(raws, first, count, name, stage_kib, kib):
            width = P * count
            stage = place("stage_" + name, [P, 2 * PACK * width], BF16, stage_kib)
            for a in range(2):
                round_plain(raws[a], stage[:, PACK * width * a : PACK * width * (a + 1)])
            codes, scales = quantize(stage[:], 2 * width, "w1_" + name, kib)
            for a in range(2):
                for i in range(count):
                    cols = slice(width * a + P * i, width * a + P * (i + 1))
                    w1_q[a, first + i] = (codes[:, cols], scales[:, cols])

        plain_weights(raw_s0, 0, 1, "s0", STAGE_AT[0], W1_Q_AT)
        for j0, w in ((0, QUARTER), (QUARTER, QUARTER), (HALF, HALF)):
            nc.vector.tensor_copy(out=v_w[1][:, j0 : j0 + w], in_=tab_w[1][:].indirect(entries("offs", j0, w)))
        clear_page(2)

        used = []

        def features(s, j0, w, out):
            cols = slice(j0, j0 + w)
            acc = bank("acc%d_%d" % (s, j0), len(used) % 8)
            used.append(acc)
            for a in range(2):
                codes, scales = w1_q[a, s]
                nc.tensor.matmul_mx(
                    out=acc[:, 0:w],
                    lhsT=codes.bitcast(FP8X4),
                    lhsT_scale=scales,
                    rhs=v_w[a][:, cols].bitcast(FP8X4),
                    rhs_scale=v_s[4 * a : P, cols],
                    start=(a == 0),
                    stop=(a == 1),
                )
            nc.scalar.activation(out=out, in_=acc[:, 0:w], func=ACT.Exp)

        h_sb = {}

        def whole_features(s):
            h_sb[s] = place("h%d" % s, [P, S], F32, H_AT[s])
            for j0, w in HALVES:
                features(s, j0, w, h_sb[s][:, j0 : j0 + w])

        def page_of(s):
            return pages[(0, 1, 0, 1, 0, 1, 2, 3)[s]]

        def scatter_first(half, j0):
            nc.vector.tensor_tensor(
                out=pages[0][:].indirect(entries("offs2", j0, HALF)),
                in0=half[:], in1=wgs_plain[:, j0 : j0 + HALF], op=ALU.mult,
            )

        def scatter(s):
            nc.vector.tensor_tensor(
                out=page_of(s)[:].indirect(lists["offs2"][:]), in0=h_sb[s][:], in1=wgs_plain[:], op=ALU.mult
            )

        first_half = place("h0_first", [P, HALF], F32, H0_AT[0])
        for j0 in (0, QUARTER):
            features(0, j0, QUARTER, first_half[:, j0 : j0 + QUARTER])
        scatter_first(first_half, 0)
        plain_weights(raw_s1, 1, 1, "s1", STAGE_AT[1], W1_Q_AT + 1.25)
        second_half = place("h0_second", [P, HALF], F32, H0_AT[1])
        features(0, HALF, HALF, second_half[:])
        scatter_first(second_half, HALF)
        whole_features(1)
        scatter(1)
        plain_weights(raw_s23, 2, 2, "s23", STAGE_AT[2], W1_Q_AT + 2.5)
        clear_page(3)

        for s in range(PACK):
            load_rest(s)
        wgs_rows = wgs.rearrange("(i t) j -> t i j", t=PACK)
        wgs_t = {}

        def load_wgs(t):
            wgs_t[t] = place("wgs%d" % t, [P, S], F32, WGS_T_AT + 4 * t)
            for q in (0, 2, 1, 3):
                nc.sync.dma_start(out=wgs_t[t][32 * q : 32 * (q + 1), :], in_=wgs_rows[t])

        w3_raw = [load_weight(w3, a, 0, N, "raw_w3_%d" % a, RAW_W3_AT[a]) for a in range(2)]
        gz_sb = [place("gz_sb%d" % b, [P, PACK], F32, SMALL_AT + 4.5 + b * EDGE) for b in range(2)]
        with nc.allow_non_contiguous_dma(reason="one factor a partition"):
            nc.sync.dma_start(out=gz_sb[0][:], in_=gz[0:KP].rearrange("(s p) -> p s", p=P))
        nc.sync.dma_start(out=gz_sb[1][:], in_=gz[KP : 2 * KP].rearrange("(p t) -> p t", t=PACK))
        for t in range(PACK):
            load_wgs(t)
        w2_w = place("w2_w", [P, 2 * 2 * N], U8, SMALL_AT)
        nc.sync.dma_start(
            out=w2_w[:].bitcast(I32).rearrange("p (a c) -> p a c", a=2),
            in_=w2_words.bitcast(I32).rearrange("a p c -> p a c"),
        )
        w2_s_dram = w2_scales.bitcast(I32)
        for q in range(4):
            nc.sync.dma_start(
                out=w2_s[32 * q : 32 * q + 4, :].bitcast(I32).rearrange("r (a c) -> r a c", a=2),
                in_=w2_s_dram[:, 4 * q : 4 * q + 4, :].rearrange("a r c -> r a c"),
            )
        for s in range(PACK, 2 * PACK):
            load_rest(s)

        damp, sums = {}, {}

        def two_slices(store, name, first, kib):
            both = place(name, [P, 2, PAIRS], F32, kib)
            for i in range(2):
                store[first + i] = both[:, i, :]

        def daughters(s, m0, w):
            nc.vector.tensor_copy(out=damp[s][:, m0 : m0 + w], in_=page_of(s)[:].indirect(entries("offs4", m0, w)))

        def parents(out, s, m0, w):
            nc.vector.tensor_tensor(
                out=out,
                in0=page_of(s)[:].indirect(entries("offs3", m0, w)),
                in1=rest_sb[s][:, m0 : m0 + w],
                op=ALU.add,
            )

        two_slices(damp, "damp01", 0, DAMP01_AT)
        for s in (0, 1):
            daughters(s, 0, PAIRS)
        stage = place("stage_b", [P, 2 * PACK * KP], BF16, STAGE_B_AT)
        for a in range(2):
            round_dealt(raw_b[a], stage[:, PACK * KP * a : PACK * KP * (a + 1)])
        codes, scales = quantize(stage[:], 2 * KP, "w1_b", W1_Q_AT + 5)
        for a in range(2):
            for t in range(PACK):
                cols = slice(KP * a + P * t, KP * a + P * (t + 1))
                w1_q[a, PACK + t] = (codes[:, cols], scales[:, cols])
        fetched, weighted = {}, {}

        def early_parents(s):
            nc.vector.tensor_copy(out=fetched[s], in_=page_of(s)[:].indirect(lists["offs3"][:]))

        def weigh(s):
            factors = wgs_plain if s < PACK else wgs_t[s - PACK]
            nc.gpsimd.tensor_tensor(out=weighted[s], in0=h_sb[s][:], in1=factors[:], op=ALU.mult)

        def add_rest(s):
            nc.gpsimd.tensor_tensor(out=sums[s], in0=fetched[s], in1=rest_sb[s][:], op=ALU.add)

        def scatter_weighted(s):
            nc.vector.tensor_copy(out=page_of(s)[:].indirect(lists["offs2"][:]), in_=weighted[s])

        two_slices(fetched, "parents01", 0, PARENTS01_AT)
        for s in (0, 1):
            early_parents(s)
        for s in (2, 3):
            whole_features(s)
            weighted[s] = place("weighted%d" % s, [P, S], F32, WEIGHTED_EARLY_AT[s])[:]
            weigh(s)
        w3_bf = place("stage_w3", [P, 2, PACK * KP], BF16, W3_BF_AT)
        for a in range(2):
            round_dealt(w3_raw[a], w3_bf[:, a, :])
        for s in range(PACK, 2 * PACK):
            whole_features(s)
        weighted[4] = place("weighted4", [P, S], F32, WEIGHTED_EARLY_AT[4])[:]
        weigh(4)

        def logarithm(logs, s, m0, w):
            nc.scalar.activation(out=logs, in_=damp[s][:, m0 : m0 + w], func=ACT.Ln, bias=LN_FLOOR)

        def sigmoid(logs):
            nc.scalar.activation(out=logs, in_=logs, func=ACT.Sigmoid, scale=-2.0)

        def times_gz(logs, s, m0, w):
            b, t = divmod(s, PACK)
            nc.scalar.activation(out=damp[s][:, m0 : m0 + w], in_=logs, func=ACT.Copy, scale=gz_sb[b][:, t : t + 1])

        def damp_two(s):
            logs = place("logs", [P, 2 * PAIRS], F32, LOGS_AT)
            for i in range(2):
                logarithm(logs[:, PAIRS * i : PAIRS * (i + 1)], s + i, 0, PAIRS)
            sigmoid(logs[:])
            for i in range(2):
                times_gz(logs[:, PAIRS * i : PAIRS * (i + 1)], s + i, 0, PAIRS)

        damp_two(0)
        for s in (2, 3):
            scatter_weighted(s)
        sums[0] = place("sum0", [P, PAIRS], F32, SUM0_AT)[:]
        sums123 = place("sums123", [P, 3, PAIRS], F32, SUMS123_AT)
        for s in (1, 2, 3):
            sums[s] = sums123[:, s - 1, :]
        for s in (0, 1):
            add_rest(s)
        two_slices(fetched, "parents23", 2, PARENTS23_AT)
        for s in (2, 3):
            early_parents(s)
            add_rest(s)
        two_slices(damp, "damp23", 2, DAMP23_AT)
        for s in (2, 3):
            daughters(s, 0, PAIRS)
        damp_two(2)
        w2_dealt = place("w2_dealt", [P, 2 * 2 * N], U8, W2_DEALT_AT)
        nc.scalar.copy(
            out=w2_dealt[:].bitcast(U16).rearrange("p (a t m) -> p a m t", a=2, t=PACK),
            in_=w2_w[:].bitcast(U16).rearrange("p (a m t) -> p a m t", a=2, t=PACK),
        )

        weighted_late = place("weighted", [P, 3, S], F32, WEIGHTED_AT)
        for s in (5, 6, 7):
            weighted[s] = weighted_late[:, s - 5, :]
        z_plain = place("z_plain", [P, PACK, PAIRS], BF16, Z_PLAIN_AT)
        z0 = place("z0", [P, PACK, PAIRS], BF16, Z0_AT)

        def plain_z(s):
            nc.gpsimd.tensor_tensor(out=z_plain[:, s, :], in0=sums[s], in1=damp[s], op=ALU.mult)
            for t in range(PACK):
                nc.sync.dma_start(out=z0[32 * s : 32 * (s + 1), t, :], in_=z_plain[t:P:PACK, s, :])

        weigh(5)
        weigh(6)
        plain_z(0)
        plain_z(1)
        weigh(7)
        plain_z(2)
        plain_z(3)
        woven0 = {}
        for m0, w in HALVES:
            woven0[m0] = place("woven0_%d" % m0, [P, w, PACK], BF16, WOVEN0_AT + m0 * PACK * 2 / KB)
            nc.gpsimd.tensor_scalar(
                out=woven0[m0][:],
                in0=z0[:, :, m0 : m0 + w].rearrange("p t m -> p m t"),
                scalar1=1.0,
                scalar2=0.0,
                op0=ALU.mult,
                op1=ALU.add,
            )
        w2_s_dealt = place("w2_s_dealt", [P, 2 * N], U8, Z_PLAIN_AT + 7)
        nc.gpsimd.tensor_copy(
            out=w2_s_dealt[:].rearrange("p (a t m) -> p a t m", a=2, t=PACK),
            in_=w2_s[:].rearrange("p (a m t) -> p a t m", a=2, t=PACK),
        )

        damp1 = place("damp1", [P, PACK, PAIRS], F32, DAMP1_AT)
        for t in range(PACK):
            damp[PACK + t] = damp1[:, t, :]
        most = PAIRS - PUT_OFF
        flat = damp1[:].rearrange("p t m -> p (t m)")

        def sigmoid_back(logs, first, count):
            nc.scalar.activation(out=flat[:, first : first + count], in_=logs, func=ACT.Sigmoid, scale=-2.0)

        factors = [(m0, w, place("factor%d" % m0, [P, PACK, w], F32, kib)) for m0, w, kib in FACTOR_RUNS]

        def factor(m0, w):
            first, tile = [(f, tile) for f, count, tile in factors if f <= m0 < f + count][0]
            return tile[:, :, m0 - first : m0 - first + w]

        def gz_scalar(logs, s, m0, w):
            nc.scalar.activation(
                out=factor(m0, w)[:, s - PACK, :], in_=logs, func=ACT.Copy, scale=gz_sb[1][:, s - PACK : s - PACK + 1]
            )

        def gz_gpsimd(s, m0, w):
            nc.gpsimd.tensor_scalar(
                out=factor(m0, w)[:, s - PACK, :], in0=damp[s][:, m0 : m0 + w],
                scalar1=gz_sb[1][:, s - PACK : s - PACK + 1], scalar2=0.0, op0=ALU.mult, op1=ALU.add,
            )

        def runs(end):
            return [(m0, min(w, end - m0)) for m0, w, kib in FACTOR_RUNS]

        scatter_weighted(4)
        scatter_weighted(5)
        daughters(4, 0, PAIRS)
        logs = place("logs4", [P, most], F32, LOGS_AT)
        logarithm(logs[:], 4, 0, most)
        sigmoid_back(logs[:], 0, most)
        for m0, w in runs(most):
            gz_gpsimd(4, m0, w)
        logs = place("logs56", [P, 2 * PAIRS], F32, LOGS_AT)
        logarithm(logs[:, 0:PUT_OFF], 4, most, PUT_OFF)
        scatter_weighted(6)
        daughters(5, 0, PAIRS)
        daughters(6, 0, PAIRS)
        logarithm(logs[:, PUT_OFF : PUT_OFF + PAIRS], 5, 0, PAIRS)
        logarithm(logs[:, PUT_OFF + PAIRS :], 6, 0, most)
        sigmoid_back(logs[:, 0 : PUT_OFF + PAIRS], most, PUT_OFF + PAIRS)
        sigmoid_back(logs[:, PUT_OFF + PAIRS :], 2 * PAIRS, most)
        gz_gpsimd(4, most, PUT_OFF)
        for m0, w in runs(PAIRS):
            gz_gpsimd(5, m0, w)
        first7 = place("logs7_first", [P, PUT_OFF + P], F32, LOGS_AT + 2)
        next7 = place("logs7_next", [P, HALF - P], F32, LOGS_AT + 2.625)
        last7 = place("logs7_last", [P, HALF], F32, LOGS_AT + 6)
        logarithm(first7[:, 0:PUT_OFF], 6, most, PUT_OFF)
        for m0, w in runs(most):
            gz_scalar(damp[6][:, m0 : m0 + w], 6, m0, w)
        scatter_weighted(7)
        for m0, w in LAST_PIECES:
            daughters(7, m0, w)
            if m0 == 0:
                logarithm(first7[:, PUT_OFF:], 7, 0, P)
                logarithm(next7[:], 7, P, HALF - P)
            else:
                logarithm(last7[:, m0 - HALF : m0 - HALF + w], 7, m0, w)
        sigmoid(first7[:])
        gz_scalar(first7[:, PUT_OFF:], 7, 0, P)
        gz_scalar(first7[:, 0:PUT_OFF], 6, most, PUT_OFF)
        next_bare = place("bare7_next", [P, HALF - P], F32, LOGS_AT + 1.125)
        nc.scalar.activation(out=next_bare[:], in_=next7[:], func=ACT.Sigmoid, scale=-2.0)
        gz_scalar(next_bare[:], 7, P, HALF - P)
        last_bare = place("bare7_last", [P, HALF], F32, LOGS_AT + 3.5)
        nc.scalar.activation(out=last_bare[:], in_=last7[:], func=ACT.Sigmoid, scale=-2.0)
        gz_scalar(last_bare[:], 7, HALF, HALF)

        tiles = PAIRS // P
        z_q = {}

        def quantize_z(b, stage, m0, w, kib):
            codes, scales = quantize(stage, w, "z%d_%d" % (b, m0), kib)
            for i in range(0, w, P):
                z_q[b, m0 + i] = (codes[:, i : i + P].bitcast(FP8X4), scales[:, i : i + P])

        def quantize_woven(m0, kib):
            quantize_z(0, woven0[m0][:].rearrange("p m t -> p (m t)"), m0, HALF, kib)

        quantize_woven(0, WEIGHTED_AT)
        w3_c = place("w3_c", [P, 2, KP], U32, W3_Q_AT)
        w3_s = place("w3_s", [P, 2, KP], U8, SMALL_AT + 3)
        for a in range(2):
            nc.vector.quantize_mx(out=w3_c[:, a, :].bitcast(FP8X4), scales=w3_s[:, a, :], in_=w3_bf[:, a, :])

        def make_z(summed, factor, stage):
            nc.vector.tensor_tensor(
                out=stage.rearrange("p (c i t) -> p c t i", i=PACK, t=PACK),
                in0=summed.rearrange("p t (c i) -> p c t i", i=PACK),
                in1=factor.rearrange("p t (c i) -> p c t i", i=PACK),
                op=ALU.mult,
            )

        def passes_turned(acc_a, acc_b, b, m0):
            codes, scales = z_q[b, m0]
            nc.tensor.matmul_mx(
                out=acc_b[:], lhsT=codes, lhsT_scale=scales,
                rhs=w3_c[:, b, :].bitcast(FP8X4), rhs_scale=w3_s[:, b, :],
                start=(b == 0), stop=(b == 1),
            )
            nc.tensor.matmul_mx(
                out=acc_a[:], lhsT=codes, lhsT_scale=scales,
                rhs=w2_w[:, 2 * N * b : 2 * N * (b + 1)].bitcast(FP4X4), rhs_scale=w2_s[:, N * b : N * (b + 1)],
                start=(b == 0), stop=(b == 1),
            )

        def passes_w3(acc_b, b, m0):
            codes, scales = z_q[b, m0]
            for t in range(PACK):
                nc.tensor.matmul_mx(
                    out=acc_b[:, P * t : P * (t + 1)],
                    lhsT=w3_c[:, b, P * t : P * (t + 1)].bitcast(FP8X4), lhsT_scale=w3_s[:, b, P * t : P * (t + 1)],
                    rhs=codes, rhs_scale=scales,
                    start=(b == 0 and t == 0), stop=(b == 1 and t == PACK - 1),
                )

        def passes_w2(acc_a, b, m0):
            codes, scales = z_q[b, m0]
            for t in range(PACK):
                c0 = N * b + P * t
                nc.tensor.matmul_mx(
                    out=acc_a[:, P * t : P * (t + 1)],
                    lhsT=w2_dealt[:, 2 * c0 : 2 * (c0 + P)].bitcast(FP4X4), lhsT_scale=w2_s_dealt[:, c0 : c0 + P],
                    rhs=codes, rhs_scale=scales,
                    start=(b == 0 and t == 0), stop=(b == 1 and t == PACK - 1),
                )

        y_s = place("y_s", [P, PAIRS], U8, Y_Q_AT + 4)
        out_rows = out_0.rearrange("(p t) m -> p t m", t=PACK)
        out_words = out_1[0].rearrange("p m t -> p (m t)").bitcast(I32)
        out_scales = out_2[0].bitcast(I32)

        opened, gates, turned, stages, y_pair, sum_a = {}, {}, {}, {}, {}, {}

        def passes(j, b):
            acc_a, acc_b = opened[j]
            if j < TURNED:
                passes_turned(acc_a, acc_b, b, P * j)
                return
            passes_w3(acc_b, b, P * j)
            if (j, b) == (tiles - 1, 1):
                passes_w2(opened[j - 1][0], b, P * (j - 1))
            if (j, b) != (tiles - 2, 1):
                passes_w2(acc_a, b, P * j)

        def open_tile(j):
            acc_b = bank("acc_b%d" % j, SUM_BANKS[j][0])
            acc_a = bank("acc_a%d" % j, SUM_BANKS[j][1])
            opened[j] = (acc_a, acc_b)
            passes(j, 0)

        def column_runs(j):
            return (slice(0, P // 2), slice(P // 2, P)) if j == tiles - 1 else (slice(0, P),)

        def empty_sums(j):
            acc_a, acc_b = opened[j]
            gate = place("gate%d" % j, [P, PACK, P], F32, GATE_AT[j])
            for cols in column_runs(j):
                nc.scalar.activation(
                    out=gate[:, :, cols], in_=acc_b[:].rearrange("p (t m) -> p t m", t=PACK)[:, :, cols], func=ACT.Silu
                )
            gates[j] = gate
            if j == TURNED:
                sum_a[j] = place("sum_a%d" % j, [P, PACK, P], F32, WGS_T_AT + 6 + 2 * (j % 3))
                nc.scalar.copy(out=sum_a[j][:].rearrange("p t m -> p (t m)"), in_=acc_a[:])
            if j < TURNED:
                minus_a = place("minus_a%d" % j, [P, PACK, P], F32, WGS_T_AT + 6 + 2 * (j % 3))
                nc.scalar.activation(
                    out=minus_a[:].rearrange("p (u e) m -> p u m e", e=2),
                    in_=acc_a[:].rearrange("p (m u e) -> p u m e", u=2, e=2),
                    func=ACT.Copy,
                    scale=-1.0,
                )
                minus_y = bank("minus_y%d" % j, SUM_BANKS[j][0])
                for k, term in enumerate((gate, minus_a)):
                    for t in range(PACK):
                        nc.tensor.matmul(
                            minus_y[:, P * t : P * (t + 1)],
                            lhsT=term[:, t, :],
                            rhs=ident[:],
                            is_transpose=True,
                            start=(k == 0 and t == 0),
                            stop=(k == 1 and t == PACK - 1),
                        )
                turned[j] = minus_y

        y_of = {}

        def float_rows(j):
            m0 = P * j
            if j < TURNED:
                y_of[j] = place("y%d" % j, [P, PACK, P], F32, 66 + 2 * j)[:]
                nc.scalar.activation(
                    out=y_of[j].rearrange("p t m -> p (t m)"), in_=turned[j][:], func=ACT.Copy, scale=-1.0
                )
                nc.sync.dma_start(out=out_rows[:, :, m0 : m0 + P], in_=y_of[j])
                return
            first, count, kib = [run for run in STORE_RUNS if run[0] <= j < run[0] + run[1]][0]
            if j == first:
                y_pair[j] = place("y%d" % j, [P, PACK, count * P], F32, kib)
            y_of[j] = y_pair[first][:, :, P * (j - first) : P * (j - first + 1)]
            if j == TURNED:
                nc.gpsimd.tensor_tensor(out=y_of[j], in0=sum_a[j][:], in1=gates[j][:], op=ALU.subtract)
            else:
                for cols in column_runs(j):
                    nc.vector.tensor_tensor(
                        out=y_of[j][:, :, cols],
                        in0=opened[j][0][:].rearrange("p (t m) -> p t m", t=PACK)[:, :, cols],
                        in1=gates[j][:, :, cols],
                        op=ALU.subtract,
                    )
            if j == first + count - 1:
                nc.sync.dma_start(out=out_rows[:, :, P * first : P * (first + count)], in_=y_pair[first][:])

        def run_of(j):
            return [run for run in Y_RUNS if run[0] <= j < run[0] + run[1]][0]

        def packed_rows(j):
            round_rows(j)
            pack_run(j)

        def round_rows(j):
            first, count, kib, codes_kib = run_of(j)
            if j == first:
                stages[first] = place("y_stage%d" % j, [P, count, PACK * P], BF16, kib)
            woven = stages[first][:, j - first, :].rearrange("p (c i t) -> p c t i", i=PACK, t=PACK)
            if j < TURNED:
                nc.scalar.activation(
                    out=woven,
                    in_=turned[j][:].rearrange("p (t c i) -> p c t i", t=PACK, i=PACK),
                    func=ACT.Copy,
                    scale=-1.0,
                )
            elif j == TURNED:
                nc.gpsimd.tensor_scalar(
                    out=stages[first][:, j - first, :].rearrange("p (m t) -> p m t", t=PACK),
                    in0=y_of[j].rearrange("p t m -> p m t"),
                    scalar1=1.0, scalar2=0.0, op0=ALU.mult, op1=ALU.add,
                )
            else:
                nc.scalar.copy(out=woven, in_=y_of[j].rearrange("p t (c i) -> p c t i", i=PACK))

        def pack_run(j):
            first, count, kib, codes_kib = run_of(j)
            if j == first + count - 1:
                cols = slice(P * first, P * (first + count))
                y_c = place("y_c%d" % first, [P, P * count], U32, codes_kib)
                nc.vector.quantize_mx(
                    out=y_c[:].bitcast(FP8X4),
                    scales=y_s[:, cols],
                    in_=stages[first][:].rearrange("p j c -> p (j c)"),
                )
                queue = nc.scalar if j >= TURNED else nc.sync
                queue.dma_start(out=out_words[:, cols], in_=y_c[:].bitcast(I32))

        summed = {}

        def late_parents(j, count, kib, slices):
            if (j, count) not in summed:
                summed[j, count] = place("sums1_%d" % j, [P, PACK, count * P], F32, kib)
                for i in range(count):
                    summed[j + i] = summed[j, count][:, :, P * i : P * (i + 1)]
            for t in slices:
                parents(summed[j, count][:, t, :], PACK + t, P * j, count * P)

        late_parents(0, 2, 173, range(PACK))
        for j in range(AHEAD):
            open_tile(j)
        for j in range(tiles):
            m0 = P * j
            stage = place("z_stage%d" % j, [P, PACK * P], BF16, {0: WEIGHTED_AT + 2.5, tiles - 1: LAST_STAGE_AT}.get(j, 181 + j % 2))
            make_z(summed[j], factor(m0, P), stage[:])
            if j < tiles - 2:
                late_parents(2 * (j // 2 + 1), 2, (128, 173, 128)[j // 2], (2 * (j % 2), 2 * (j % 2) + 1))
            quantize_z(1, stage[:], m0, P, Z_AT + 0.625 * j)
            if j == 0:
                quantize_woven(HALF, WEIGHTED_AT + 2.5)
            passes(j, 1)
            empty_sums(j)
            if 0 < j <= TURNED:
                float_rows(j - 1)
                packed_rows(j - 1)
            if 0 < j <= tiles - AHEAD:
                open_tile(j + AHEAD - 1)
        for j in range(TURNED, tiles):
            float_rows(j)
        for j in range(TURNED, tiles):
            packed_rows(j)
        for q in range(4):
            queue = nc.sync if q % 2 == 0 else nc.scalar
            queue.dma_start(out=out_scales[4 * q : 4 * q + 4, :], in_=y_s[32 * q : 32 * q + 4, :].bitcast(I32))
